import numpy as np, ml_dtypes
CORES = [2,3,42,43,82,83,122,123]
N = 8
BF = ml_dtypes.bfloat16
def gentries(a):
    return np.ascontiguousarray(a.reshape(8, 16, -1).transpose(0, 2, 1)).reshape(8, -1)
def gtable(e):
    e = np.asarray(e); return np.ascontiguousarray(e.reshape(8, -1, 16).transpose(0, 2, 1)).reshape(128, -1).astype(np.int32)
M, K, D, CAP, A, RO = 448, 1536, 8, 64, 1, 4
W, S, L = N * M, K // D, K // N
PS, ST = 0.015625, 0.015625
LIM = np.float32(4.0)
HOT = np.array([4.0, 2.0, 1.3359375, 1.0, 0.80078125, 0.66796875, 0.57421875])
COLD = np.array([3.984375, 1.9921875, 1.328125, 0.99609375, 0.796875, 0.6640625, 0.5703125])
def pay(rng, a):
    v = 1.0 + 0.2 * rng.standard_normal((N, 128, W), dtype=np.float32) + 0.1 * rng.integers(-1, 2, (N, 128, 1)) + a * (2.0 * rng.random((N, 1, W)) - 1.0)
    return np.clip(v, 0.5, 1.5).astype(BF)
def parts(rng):
    e = pay(rng, 0.0); w = np.exp2(4.0 * rng.random((N, 8, W)) - 2.0)
    share = rng.choice(np.array([0.05, 0.2, 0.5, 0.9]), (N, 8, N, 1))
    l = np.where(rng.random((N, 8, N, M)) < share, rng.integers(1, 8, (N, 8, N, M)), 0).reshape(N, 8, W)
    b = np.ascontiguousarray(np.argsort(rng.random((N, 8, RO, W)), axis=-1)[..., :2 * K]).reshape(N, 8, RO, 2, K)
    t = np.clip(0.625 * rng.standard_normal((N, 16, RO * S)), -1.0, 1.0).astype(BF)
    return e, w, l, b, t
def pack(e, w, l, b, t):
    return {"e0": e, "wt": np.asarray(w).astype(BF), "lag": np.asarray(l).astype(np.int32), "bt": np.stack([gtable(a.reshape(8, -1)) for a in b]), "tg": t}
def close(rng, n):
    v = (np.exp2(np.arange(-9.0, -5.0))[:, None] * np.arange(128, 256)).reshape(-1)
    x = (v[:, None] * (A * (RO - 1) + np.arange(8))).reshape(-1); o = np.argsort(x, kind="stable"); k = x[o]
    i = rng.choice(np.flatnonzero((k[1:] > k[:-1]) & (k[1:].astype(np.float16) == k[:-1].astype(np.float16))), n)
    lo = o[i]; hi = o[i + 1]
    return v[lo // 8], lo % 8, v[hi // 8], hi % 8
def herd(rng, w, l, b, g, q, lo):
    x = np.stack([np.concatenate([np.array([M - 1, 0]), 1 + rng.permutation(M - 2)]) + h * M for h in range(N)])
    m = x[:, :L]; a = x[:, L:2 * L]; o = x[:, 2 * L:]
    w[:, g] = 0.25; w[:, g][:, m] = 4.0
    l[:, g] = 0; l[:, g][:, m] = 7
    near = np.zeros(L // 2, bool); kind = np.arange(16) % 6
    if q >= 0:
        X = min(CAP, L - CAP); l[q, g][m[:, 2:X]] = rng.choice(np.array([lo, 7]), (N, X - 2))
        if lo > 0:
            w[q, g][m[:, 2:10]] = 0.75; l[q, g][m[:, 2:10]] = 7
            w[q, g][o[:, :8]] = (6.5 + (N - 1 + A) * (RO - 1)) * 0.75 * 0.142857142857; l[q, g][o[:, :8]] = 7
    else:
        y = CAP // 2 + rng.permutation(L // 2 - CAP // 2)[:(L - CAP) // 4]; near[y] = True
        wl, al, wh, ah = close(rng, len(y))
        w[:, g][:, m[:, 2 * y]] = wl; l[:, g][:, m[:, 2 * y]] = al; w[:, g][:, m[:, 2 * y + 1]] = wh; l[:, g][:, m[:, 2 * y + 1]] = ah
        w[:, g][:, o[:, :16]] = np.array([4.0, 4.0, 2.0, 2.0, 4.0, 4.0])[kind]
        l[:, g][:, o[:, :16]] = np.array([A, A, 2 * A - 1, 2 * A + 1, A + 1, A - 1])[kind]
    k = int(rng.integers(0, N)); k2 = (k + 1) % N
    j = np.arange(K); h = j % N; i = j // N
    for r in range(N):
        b[r, g, :, 0] = m[h, L - 1 - i if r == q else i]; b[r, g, :, 1] = a[h, i]
        if q == -2:
            f = m.copy(); s = a.copy(); f[k] = a[k2]; s[k2] = m[k]
            b[r, g, RO - 2, 0] = f[h, i]; b[r, g, RO - 2, 1] = s[h, i]
        sp = np.arange(0); first = np.zeros(0, bool)
        if q < 0:
            z = 1 + rng.permutation(CAP // 2 - 1)[:8]; sp = rng.permutation(np.concatenate([2 * z, 2 * z + 1])); first = kind % 2 == 1
        elif r == q and lo > 0:
            sp = np.arange(2, 10); first = rng.random(8) < 0.5
        n = len(sp); c = n // 2; p = m[:, sp]; v = o[:, :n]
        z = np.concatenate([rng.permutation(np.setdiff1d(np.arange(1, L // 2), sp // 2)), np.array([0])])
        f = np.concatenate([np.where(first, v, p), a[:, c:L // 2], m[:, 2 * z]], axis=1)
        s = np.concatenate([np.where(first, p, v), a[:, L // 2 + c:], m[:, 2 * z + 1]], axis=1)
        t = rng.random((N, L)) < 0.5; t[:, :n] = True; t[:, L // 2 + c:] |= near[z]
        if q == -1:
            f[k2] = m[k2]; s[k2] = m[k]; f[k] = a[k2]; s[k] = a[k]; t[k2] = True
        b[r, g, RO - 1, 0] = np.where(t, f, s)[h, i]; b[r, g, RO - 1, 1] = np.where(t, s, f)[h, i]
def leave(rng, w, l, b, g, q, v):
    x = np.stack([np.concatenate([np.array([M - 1, 0]), 1 + rng.permutation(M - 2)]) + h * M for h in range(N)])
    m = x[:, :L]; a = x[:, L:2 * L]; j = np.arange(K); h = j % N; i = j // N
    w[:, g] = 0.25; w[:, g][:, m] = 4.0
    l[:, g] = 0; l[:, g][:, m] = 7
    w[q, g][m[:, CAP:CAP + 16]] = v
    b[:, g, :RO - 1, 0] = m[h, i]; b[:, g, :RO - 1, 1] = a[h, i]
    b[q, g, RO - 2, 0] = m[h, L - 1 - i]
    z = rng.permutation(np.setdiff1d(np.arange(M), np.concatenate([np.arange(16), CAP + np.arange(16)])))[:2 * L - 32]
    f = np.concatenate([m[:, :16], x[:, z[:L - 16]]], axis=1); s = np.concatenate([m[:, CAP:CAP + 16], x[:, z[L - 16:]]], axis=1)
    t = rng.random((N, L)) < 0.5
    b[q, g, RO - 1, 0] = np.where(t, f, s)[h, i]; b[q, g, RO - 1, 1] = np.where(t, s, f)[h, i]
def full(rng, w, l, b, r, g, h):
    Q = K // 8; T = K - M - Q; k = (h + 1) % N; x = np.arange(W).reshape(N, M)
    y = rng.permutation(x[k]); z = rng.permutation(x[[v for v in range(N) if v != h and v != k]].reshape(-1))
    n = np.concatenate([rng.permutation(np.concatenate([x[h], z[:T]])), y[:Q]]); o = rng.permutation(np.concatenate([z[T:], y[Q:]]))[:K]
    v = rng.integers(1, 8, K); w[r, g][n] = HOT[v - 1]; l[r, g][n] = v
    v = rng.integers(0, 8, K); w[r, g][o] = np.where(v == 0, 4.0, COLD[v - 1]); l[r, g][o] = v
    t = rng.random(K) < 0.5
    b[r, g, 0, 0] = np.where(t, n, o); b[r, g, 0, 1] = np.where(t, o, n)
def setup_inputs(rng):
    return pack(*parts(rng))
def setup_inputs_spread(rng):
    e, w, l, b, t = parts(rng)
    e = np.where(rng.random((N, 1, W)) > 0.0625, pay(rng, 0.5).astype(np.float32), np.float32(0.5)).astype(BF)
    return pack(e, w, l, b, t)
def setup_inputs_ends(rng):
    e, w, l, b, t = parts(rng)
    w = rng.choice(np.array([0.25, 4.0]), (N, 8, W)); l = rng.choice(np.array([0, 7]), (N, 8, W))
    o = 1 + np.argsort(rng.random((N, 8, RO, W - 2)), axis=-1)[..., :2 * K - 2]
    b[..., 0, :K - 1] = o[..., :K - 1]; b[..., 1, :K - 1] = o[..., K - 1:]
    b[..., 0, K - 1] = W - 1; b[..., 1, K - 1] = 0
    l[..., 0] = 7; l[..., W - 1] = 7; w[..., 0] = 4.0; w[..., W - 1] = 4.0
    for g in (1, 3, 5, 7): herd(rng, w, l, b, g, N - 1 if g == 7 else int(rng.integers(0, N)), 0)
    t = rng.choice(np.array([-1.0, 1.0]), t.shape).astype(BF)
    q = int(rng.integers(0, N)); v = rng.choice(np.array([0.5, 1.5]), (N, 8, W)); v[q] = 1.5
    k = (q + int(rng.integers(1, N))) % N; y = rng.choice(np.array([0.5, 1.5]), (N, 8, W)); y[k] = 0.5
    t[k, 14, S - 1] = 1.0; t[k, 14, 0] = 1.0
    z = w * l; na = b[:, :, 0, 0]; nb = b[:, :, 0, 1]
    n = np.where(np.take_along_axis(z, nb, 2) > np.take_along_axis(z, na, 2), nb, na)
    for g in range(8):
        v[n[q, g] // M, g, n[q, g]] = 1.5
        y[n[k, g] // M, g, n[k, g]] = 0.5
    e = e.reshape(N, 8, 16, W).copy(); e[:, :, 15] = v.astype(BF); e[:, :, 14] = y.astype(BF); e = e.reshape(N, 128, W)
    return pack(e, w, l, b, t)
def setup_inputs_corners(rng):
    e, w, l, b, t = parts(rng)
    for r in range(N):
        for g in range(8):
            if r > 0 and (r + g) % 3 == 0:
                full(rng, w, l, b, r, g, (r + g) % N); continue
            sl = rng.permutation(K).reshape(N, L)
            for h in range(N):
                n = int(rng.choice(np.array([0, 1, CAP - 1, CAP, CAP + 1, L])))
                if r == 0 and h == 1: n = (CAP, 0, 1, CAP - 1, CAP + 1, L, CAP, CAP + 1)[g]
                nm = (h * M + rng.permutation(M))[:2 * L].reshape(2, L)
                z = rng.integers(1, 8, (2, L)); hot = np.zeros((2, L), bool); k = rng.permutation(L)[:n]; y = rng.integers(0, 3, n)
                z[1] = np.where(rng.random(L) < 0.3, z[0], z[1])
                hot[0, k] = y != 1; hot[1, k] = y != 0
                none = (rng.random((2, L)) < 0.4) & ~hot
                w[r, g][nm] = np.where(none, rng.choice(np.array([0.25, 4.0]), (2, L)), np.where(hot, HOT[z - 1], COLD[z - 1]))
                l[r, g][nm] = np.where(none, 0, z)
                b[r, g, 0][:, sl[h]] = nm
    return pack(e, w, l, b, t)
def setup_inputs_crowd(rng):
    e, w, l, b, t = parts(rng)
    for g, q in ((0, -1), (2, int(rng.integers(0, N))), (4, -2), (6, int(rng.integers(0, N))), (7, N - 1)): herd(rng, w, l, b, g, q, 6)
    leave(rng, w, l, b, 1, int(rng.integers(0, N)), 4.0 * (N - 1 + 2 * A + np.where(np.arange(16) % 4 == 3, 0.5, -0.5)) / (7 + A * (RO - 1)))
    return pack(e, w, l, b, t)
def setup_inputs_calm(rng):
    e, w, l, b, t = parts(rng)
    w = rng.choice(np.concatenate([HOT, COLD, np.array([0.5, 0.498046875])]), (N, 8, W))
    act = (rng.permutation(N)[:, None] < (np.arange(8) % 4)[None, :])[:, :, None]
    w = np.where(act | (rng.random((N, 8, W)) < 0.25), w, 0.25)
    l = rng.integers(0, 4, (N, 8, W)) * (np.arange(8) % 2)[None, :, None]
    return pack(e, w, l, b, t)
def cand(bt):
    return np.stack([gentries(np.asarray(a)) for a in bt]).astype(np.int64).reshape(N, 8, RO, 2, K)
def check_ranges(d):
    bad = []
    for k, lo, hi in (("e0", 0.5, 1.5), ("wt", 0.25, 4), ("lag", 0, 7), ("bt", 0, W - 1), ("tg", -1, 1)):
        v = np.asarray(d[k]).astype(np.float64)
        if not (np.min(v) >= lo and np.max(v) <= hi): bad.append("range of " + k)
    b = np.sort(cand(d["bt"]).reshape(N, 8, RO, 2 * K), axis=-1)
    if np.any(b[..., 1:] == b[..., :-1]): bad.append("candidates of a round differ")
    return bad
def reference(e0, wt, lag, bt, tg):
    R = e0.astype(np.float64).reshape(N, 8, 16, W).copy(); P = np.zeros((N, 8, 16, W)); u = np.zeros((N, 8, W), np.int64)
    H = np.concatenate([R[h, :, :, h * M:(h + 1) * M] for h in range(N)], axis=2)
    c = np.zeros((8, W), np.int64); seen = -lag.astype(np.int64); b = cand(bt); w32 = wt.astype(np.float32); tgt = tg.astype(np.float64)
    for t in range(RO):
        sc = w32 * (c[None] - seen + A * u).astype(np.float32)
        took = []; asked = []
        for r in range(N):
            na = b[r, :, t, 0]; nb = b[r, :, t, 1]; sa = np.take_along_axis(sc[r], na, 1); sb = np.take_along_axis(sc[r], nb, 1)
            n = np.where(sb > sa, nb, na); due = np.where(sb > sa, sb, sa) >= LIM; home = n // M; ok = np.zeros((8, K), bool)
            for h in range(N):
                m = due & (home == h); ok = ok | (m & (np.add.accumulate(m.astype(np.int64), axis=1) <= CAP))
            took.append(n); asked.append([n[g][ok[g]] for g in range(8)])
        for r in range(N):
            for g in range(8):
                ix = asked[r][g]; H[g][:, ix] += P[r, g][:, ix]; c[g][ix] += 1
        for r in range(N):
            for g in range(8):
                ix = asked[r][g]; R[r, g][:, ix] = H[g][:, ix]; P[r, g][:, ix] = 0.0; u[r, g][ix] = 0; seen[r, g][ix] = c[g][ix]
        for r in range(N):
            n = took[r]; ix = np.broadcast_to(n[:, None, :], (8, 16, K)); x = np.take_along_axis(R[r], ix, 2); y = x.reshape(8, 16, D, S)
            p = np.add.reduce(y[:, :, :D // 2] * y[:, :, D // 2:], axis=(0, 2))
            e = np.tanh(tgt[r][:, t * S:(t + 1) * S] - PS * p)
            step = (ST * e[None, :, None, :] * np.concatenate([y[:, :, D // 2:], y[:, :, :D // 2]], axis=2)).reshape(8, 16, K)
            np.put_along_axis(R[r], ix, x + step, 2)
            if t < RO - 1:
                np.put_along_axis(P[r], ix, np.take_along_axis(P[r], ix, 2) + step, 2)
                np.put_along_axis(u[r], n, np.take_along_axis(u[r], n, 1) + 1, 1)
    return {"yr": R.reshape(N, 128, W).astype(np.float32), "yh": np.stack([H[:, :, h * M:(h + 1) * M].reshape(128, M) for h in range(N)]).astype(np.float32)}

def check_inputs(d):
    bad = list(check_ranges(d))
    if not bad:
        for name, y in reference(**d).items():
            for q in range(N):
                v = np.abs(np.asarray(y[q], np.float64)); s = np.sqrt(np.mean(v * v))
                if v.max() > 2 * s or s < 2.0 ** -2: bad.append('%s of rank %d is uneven or too small' % (name, q))
    return bad

@@ -1,0 +1,689 @@
+from concourse.bass import DstId, RemoteDMATransfer
+from concourse.mybir import AluOpType as ALU, ActivationFunctionType as AF, AxisListType as AX
+
+N, W, K, M, RO, CAP = 8, 3584, 1536, 448, 4, 64
+MAG = 12582912.0
+SC = 2.0 ** -17
+F, B16, I32, U16 = "float32", "bfloat16", "int32", "uint16"
+
+
+def sb(n, d):
+    return ("sbuf", [128, n], d)
+
+
+SCRATCH = {
+    "big": sb(W + RO * K, F), "base": sb(W + RO * K, F), "wn": sb(2 * W, F), "cw": sb(1024 + K, F), "tb": sb(W, B16),
+    "cs": sb(8 * 224, B16), "vv": sb(K, F), "hh": sb(512, F), "bti": sb(768, I32), "b16": sb(768, U16), "hq": sb(192, F),
+    "hi": sb(768, I32), "dn": sb(384, F), "dh": sb(384, F), "lagc": sb(224, I32), "wc": sb(224, B16), "am": sb(224, F),
+    "tt": sb(224, F), "cab": sb(672, F), "yy": sb(448, F), "yz": sb(448, F), "fill": sb(672, F), "zr": sb(64, F), "pk": sb(224, F),
+    "d8": sb(224, F), "gf": sb(224, F), "dc": sb(224, I32), "s1": sb(112, F), "s2": sb(56, F), "s3": sb(28, I32), "fs": sb(84, F),
+    "fl": sb(672, F), "pi": sb(8, I32), "pc": sb(24, F), "xr": sb(224, F), "e1": sb(144, F), "gs": sb(576, B16), "gq": sb(144, F),
+    "gh": sb(144, B16), "ge": sb(384, F), "lt": sb(128, B16), "ut": sb(128, B16), "idn": sb(128, B16), "x16": sb(128, F),
+    "ee": sb(128, F), "dj": sb(96, F), "kk": sb(32, F), "vq": sb(224, F), "mm": sb(784, B16), "sc": sb(784, B16), "d97": sb(784, B16),
+    "zz": sb(784, B16), "ii": sb(784, B16), "tau": sb(8, F), "wk": sb(23 * 96, F), "nd": sb(96, B16), "kh": sb(96, B16),
+    "o16": sb(384, U16), "c16": sb(384, U16), "xl": sb(384, U16), "qw": sb(160, F), "q16": sb(128, U16), "lg": sb(512, B16),
+    "rb16": sb(256, U16), "ll": sb(RO * 256, U16), "bs": sb(512, F), "psn": sb(1536, F), "pl": sb(1536, F), "tm": sb(128, F),
+    "asn": sb(1536, F), "h0s": sb(M, B16), "h0d": ("dram", [N, 128, M], B16), "pr": sb(768, F), "tgb": sb(768, B16), "tgs": sb(768, F), "es": sb(192, F), "y16": sb(224, U16),
+    "cg0": sb(16 + 2 * K, B16), "cg1": sb(16 + 2 * K, B16),
+}
+PSUM = ("p_s", "p_c0", "p_c1", "p_l", "p_p", "p_x", "p_t0", "p_t1")
+for _n in PSUM:
+    SCRATCH[_n] = ("psum", [128, 512], F)
+ND = 72
+SEMAPHORES = (["dve", "act", "pe", "pool", "sent", "ha"] + ["d%d" % i for i in range(ND)] + ["fa%d" % t for t in range(3)]
+              + ["la%d" % t for t in range(1, RO)] + ["aa%d" % t for t in range(1, RO)] + ["pa%d" % s for s in range(N)])
+
+PLAN = {"cy": 0.00104, "ga": 1.56, "sa": 3.8, "pe": 0.00055, "dma": 1.9, "net": 1.0}
+OPT = {"cg": (("act", 0, 64), ("dve", 64, 128), ("act", 128, 160), ("dve", 160, 192)), "ns": ("a", "a", "a", "aaa"),
+       "cs": ("aaa", "aaa", "aaa", "a"), "home": "dddd", "lin": "ddad", "ii": "a", "ans": ("dddddddd",) * 3 + ("dadadada",), "fin": "dadadada", "look": 0.6,
+       "bias": {'cg0': 0.4, 'cg1': 21.3, 'xl2': 1.2, 'ns1': -1.3, 'ns3': -6.3, 'ns0': -6.9, 'age0': 22.7, 'st3': -30.8, 'hm3': -5.5,
+                'st0': -1.1, 'ptr3': -0.3, 'prep2': 2.0, 'st1': 0.4, 'ptr0': -13.6, 'cnt2': -0.8, 'prep3': 4.6, 'prep1': -4.6,
+                'ns2': 6.5, 'ptr2': 0.7, 'hm2': -1.5, 'ls1': -1.1, 'age3': 18.5, 'st2': -0.1, 'ls3': 0.2, 'cnt1': 1.5, 'age2': 0.7,
+                'age1': -0.2, 'cnt0': -0.2, 'xl3': -1.8, 'cnt3': 0.2, 'xl1': -2.2, 'init': 0.1, 'cg2': -0.4, 'cg3': 1.2, 'ls2': 0.8,
+                'prep0': 0.3}}
+
+
+def R(name, a, b, step=1, p=None, ind=None):
+    return ("R", name, a, b, step, p, ind)
+
+
+def isr(x):
+    return isinstance(x, tuple) and x[0] == "R"
+
+
+def cnt(r):
+    return 16 * (r[6][3] - r[6][2]) if r[6] else len(range(r[2], r[3], r[4]))
+
+
+def peers(r, cores, topo):
+    me = cores[r]
+    order = [(r + k) % N for k in range(1, N)]
+    near = [d for d in order if topo.chip(cores[d]) == topo.chip(me)]
+    far = [d for d in order if d not in near]
+    ef = topo.engines(me, cores[far[0]])
+    en = [e for e in topo.engines(me, cores[near[0]]) if e not in ef]
+    return near, far, en, ef
+
+
+def msk(es):
+    return sum(1 << e for e in es)
+
+
+def pieces(r, cores, topo):
+    near, far, en, ef = peers(r, cores, topo)
+    n1 = len(ef) // 4
+    n2 = len(ef) // (len(far) - 4)
+    c1 = [(d, ef[i * n1:(i + 1) * n1]) for i, d in enumerate(far[:4])] + [(near[0], en)]
+    c2 = [(d, ef[i * n2:(i + 1) * n2]) for i, d in enumerate(far[4:])]
+    return c1, c2
+
+
+def plan(r, T, topo, sc, opt):
+    CY, PEC = sc["cy"], sc["pe"]
+    cores = list(T.cores)
+    ops = []
+    nd = [0]
+    tag = ["init"]
+
+    def add(eng, call, reads, writes, cost, lat=0.0, sem=None, after=()):
+        ops.append({"eng": eng, "call": call, "rd": [x for x in reads if isr(x)], "wr": [x for x in writes if isr(x)],
+                    "tag": tag[0], "cost": cost, "lat": lat, "sem": sem, "after": list(after)})
+        return len(ops) - 1
+
+    def ap(x):
+        if not isr(x):
+            return x
+        t = T[x[1]]
+        if x[1] == "h0d":
+            return t[x[2]]
+        p = x[5]
+        ps = slice(None) if p is None else (slice(p[1], 128, 16) if p[0] == "rows" else slice(0, p[1]))
+        a = t[ps, x[2]:x[3]] if x[4] == 1 else t[ps, x[2]:x[3]:x[4]]
+        return a.indirect(ap(x[6])) if x[6] else a
+
+    def offs(*xs):
+        return [x[6] for x in xs if isr(x) and x[6]]
+
+    def two(*xs):
+        return all(SCRATCH[x[1]][2] in (B16, U16) for x in xs)
+
+    def vcost(o, i, base):
+        if o[6]:
+            return 0.05 + cnt(o) * sc["sa"] * CY
+        if i[6]:
+            return 0.05 + cnt(i) * sc["ga"] * CY
+        return 0.05 + max(64, cnt(i) * base) * CY
+
+    def tt(o, a, b, op):
+        f = 1 if (a[1] in PSUM or b[1] in PSUM) else 2
+        return add("dve", lambda g: g.vector.tensor_tensor(ap(o), ap(a), ap(b), op), [a, b] + offs(o, a), [o], vcost(o, a, f))
+
+    def ts(o, a, s1, op0, s2=None, op1=None):
+        if op1 is None:
+            call = lambda g: g.vector.tensor_scalar(ap(o), ap(a), ap(s1), None, op0)
+        else:
+            call = lambda g: g.vector.tensor_scalar(ap(o), ap(a), ap(s1), ap(s2), op0, op1)
+        return add("dve", call, [a, s1, s2], [o], vcost(o, a, 0.5 if two(o, a) else 1))
+
+    def cp(o, a):
+        return add("dve", lambda g: g.vector.tensor_copy(ap(o), ap(a)), [a] + offs(o, a), [o], vcost(o, a, 0.5 if two(o, a) else 1))
+
+    def ms(o, v):
+        return add("dve", lambda g: g.vector.memset(ap(o), v), [], [o], vcost(o, o, 0.5 if two(o) else 1))
+
+    def scan(o, d0, d1):
+        return add("dve", lambda g: g.vector.tensor_tensor_scan(ap(o), ap(d0), ap(d1), 0.0, ALU.mult, ALU.add), [d0, d1], [o],
+                   vcost(o, d1, 0.5 if two(o, d0, d1) else 1))
+
+    def total(o, a):
+        return add("dve", lambda g: g.vector.tensor_reduce(ap(o), ap(a), AX.X, ALU.add), [a], [o], vcost(o, a, 1))
+
+    def act(o, a, func=AF.Identity, scale=None, bias=None):
+        if scale is None:
+            call = lambda g: g.scalar.activation(ap(o), ap(a), func)
+        else:
+            call = lambda g: g.scalar.activation(ap(o), ap(a), func, bias=ap(bias) if isr(bias) else float(bias or 0.0),
+                                                 scale=ap(scale) if isr(scale) else float(scale))
+        return add("act", call, [a, scale, bias] + offs(o, a), [o], 0.015 + vcost(o, a, 1))
+
+    def lin(key, o, a, scale, bias):
+        if opt["lin"][key] == "a":
+            return act(o, a, scale=scale, bias=bias)
+        return ts(o, a, scale if isr(scale) else float(scale), ALU.mult, bias if isr(bias) else float(bias), ALU.add)
+
+    def const(o, v):
+        return lin(2, o, R("xr", 0, cnt(o)), 0.0, v)
+
+    def move(eng, o, a):
+        return cp(o, a) if eng == "dve" else act(o, a)
+
+    def mms(lst):
+        def call(g):
+            ins = None
+            for o, l, x, s0, s1 in lst:
+                ins = g.tensor.matmul(ap(o), ap(l), ap(x), s0, s1)
+            return ins
+        c = sum(max(64, cnt(x)) * (4 if SCRATCH[x[1]][2] == F else 1) for o, l, x, s0, s1 in lst)
+        return add("pe", call, [q[1] for q in lst] + [q[2] for q in lst], [q[0] for q in lst], 0.1 + c * PEC)
+
+    def wrap(o, sel, s0, src, a, n):
+        return mms([(o, R(sel, s0 + 15 - i, s0 + 143 - i), R(src, a + i, a + 16 * n, 16), i == 0, i == 15) for i in range(16)])
+
+    def iota(o, pat, base, cm):
+        if SCRATCH[o[1]][2] != I32:
+            call = lambda g: g.iota(ap(o), pat, base, cm, allow_small_or_imprecise_dtypes=True)
+        else:
+            call = lambda g: g.iota(ap(o), pat, base, cm)
+        return add("pool", call, [], [o], 0.13 + 2 * cnt(o) * CY)
+
+    def dma(q, o, a, kb, behind=()):
+        s = "d%d" % nd[0]
+        nd[0] += 1
+        if q == "sp":
+            call = lambda g: g.sync.dma_start(ap(o), ap(a))
+        elif q == "act":
+            call = lambda g: g.scalar.dma_start(ap(o), ap(a))
+        else:
+            call = lambda g: g.dma_start(ap(o), ap(a))
+        return add(q, call, [a] + list(behind), [o], 0.1 if q != "pool" else 0.5, sc["dma"] + kb / 200.0, (s, 16))
+
+    def dst(d):
+        a = topo.addr(cores[d])
+        return DstId(rid=a[0], pnc=a[1])
+
+    sent = [0]
+
+    def send(trs, lat):
+        def call(g):
+            g.remote_dma_fused([RemoteDMATransfer(dst_ids=[dst(d) for d, x in ds], dma_engine_mask=msk(es), remote_sem=T.sem[sm],
+                                                  srcs=[ap(s)], dsts=[ap(x) for d, x in ds]) for s, ds, es, sm in trs],
+                               local_sem=T.sem.sent)
+            return None
+        sent[0] += sum(len(q[2]) for q in trs)
+        return add("pool", call, [q[0] for q in trs], [], 0.8, lat * sc["net"], ("none", 0))
+
+    def arrive(writes, sm, val, after):
+        return add("net", None, [], writes, 0.0, 0.0, (sm, val), after)
+
+    near, far, en, ef = peers(r, cores, topo)
+    c1, c2 = pieces(r, cores, topo)
+    into = {}
+    allin = 0
+    for s in range(N):
+        if s != r:
+            for i, c in enumerate(pieces(s, cores, topo)):
+                for d, es in c:
+                    if d == r:
+                        into[s] = (i, len(es))
+            q = peers(s, cores, topo)
+            allin += len(q[2]) if r in q[0] else len(q[3])
+
+    def bcast(src, land, sm, lat=3.6):
+        return send([(src, [(d, land) for d in far], ef, sm), (src, [(d, land) for d in near], en, sm)], lat)
+
+    def row(name, a, b, i):
+        return R(name, a, b, p=("rows", i))
+
+    dma("sp", R("lagc", 0, 224), T.lag[:], 114)
+    dma("act", R("wc", 0, 224), T.wt[:], 57)
+    dma("sp", R("bti", 0, 768), T.bt[:], 393)
+    ms(R("tb", 0, W), 0.0)
+    dma("sp", row("tb", 0, W, 0), T.wt[:], 57)
+    ts(R("am", 0, 224), R("lagc", 0, 224), -1.0, ALU.add)
+
+    def score(a, b):
+        tt(R("cs", 0, 224), a, b, ALU.mult)
+        tt(R("p_s", 288, 512), a, b, ALU.mult)
+        dma("sp", row("tb", 0, W, 1), R("cs", 0, 224), 57)
+        tt(R("cs", 224, 448), R("p_s", 288, 512), R("cs", 0, 224), ALU.subtract)
+        dma("sp", row("tb", 0, W, 2), R("cs", 224, 448), 57)
+
+    score(R("am", 0, 224), R("wc", 0, 224))
+    iota(R("pi", 0, 1), [[0, 1]], 0, 1)
+    iota(R("xr", 0, 224), [[1, 224]], 0, 0)
+    iota(R("x16", 0, 128), [[0, 8], [1, 16]], 0, 0)
+    ts(R("pi", 1, 2), R("pi", 0, 1), 15, ALU.bitwise_and)
+    ts(R("pi", 2, 3), R("pi", 0, 1), 1, ALU.bitwise_and)
+    cp(R("pc", 0, 3), R("pi", 0, 3))
+    pc = [R("pc", i, i + 1) for i in range(24)]
+    P_, P16, P2 = pc[:3]
+    tt(pc[3], P_, P16, ALU.subtract)
+    ts(pc[4], pc[3], 15.0, ALU.add)
+    ts(pc[5], P16, 224.0, ALU.mult)
+    ts(pc[6], P2, 224.0, ALU.mult, 64.0, ALU.add)
+    ts(R("e1", 0, 144), R("xr", 0, 144), pc[4], ALU.is_equal)
+    for i, (lo, hi) in enumerate(((0, 2), (3, 4), (5, 6), (7, 8))):
+        ts(pc[8 + i], P16, float(hi), ALU.is_le)
+        ts(pc[12 + i], P16, float(lo), ALU.is_ge, pc[8 + i], ALU.mult)
+        lin(2, R("gs", 144 * i, 144 * i + 144), R("e1", 0, 144), pc[12 + i], 0.0)
+    ts(pc[7], P16, 0.0, ALU.is_equal, 1.0 / SC, ALU.mult)
+    lin(2, R("gq", 0, 144), R("e1", 0, 144), pc[7], 0.0)
+    ms(R("gh", 0, 144), 0.0)
+    tt(R("gh", 0, 143), R("e1", 0, 143), R("e1", 1, 144), ALU.add)
+    ts(R("ge", 0, 128), R("xr", 0, 128), pc[3], ALU.is_ge)
+    ts(R("ge", 128, 256), R("xr", 0, 128), P_, ALU.is_ge)
+    ts(R("ge", 256, 384), R("xr", 0, 128), pc[4], ALU.is_gt)
+    tt(R("ut", 0, 128), R("ge", 0, 128), R("ge", 128, 256), ALU.subtract)
+    tt(R("lt", 0, 128), R("ge", 128, 256), R("ge", 256, 384), ALU.subtract)
+    ts(R("idn", 0, 128), R("xr", 0, 128), P_, ALU.is_equal)
+    ts(R("ee", 0, 128), R("x16", 0, 128), P16, ALU.is_equal)
+    lin(2, R("p_x", 0, 224), R("xr", 0, 224), 1.0, pc[5])
+    lin(2, R("p_x", 224, 448), R("xr", 0, 224), 1.0, pc[5])
+    lin(2, R("vq", 0, 224), R("xr", 0, 224), 1.0, pc[6])
+    act(R("cs", 1344, 1568), R("vq", 0, 224))
+    tt(R("cs", 1568, 1792), R("vq", 0, 224), R("cs", 1344, 1568), ALU.subtract)
+    dma("sp", row("tb", 0, W, 7), R("cs", 1344, 1568), 57)
+    dma("sp", row("tb", 0, W, 8), R("cs", 1568, 1792), 57)
+
+    def pointers(n):
+        act(R("cs", 448, 448 + n), R("p_x", 0, n))
+        tt(R("cs", 896, 896 + n), R("p_x", 0, n), R("cs", 448, 448 + n), ALU.subtract)
+        dma("sp", row("tb", 0, W, 3), R("cs", 448, 672), 57)
+        dma("sp", row("tb", 0, W, 4), R("cs", 896, 1120), 57)
+        if n > 224:
+            dma("sp", row("tb", 0, W, 5), R("cs", 672, 896), 57)
+            dma("sp", row("tb", 0, W, 6), R("cs", 1120, 1344), 57)
+
+    def refill():
+        dma("sp", row("wn", 0, 2 * W, 0), R("fill", 0, 448), 229)
+        dma("sp", row("wn", W, 2 * W, 1), R("fill", 448, 672), 114)
+
+    lin(2, R("dj", 0, 96), R("xr", 0, 96), 16.0, P16)
+    for h in range(8):
+        act(R("kk", 4 * h, 4 * h + 4), R("dj", 0, 4))
+    lin(2, R("dj", 0, 96), R("dj", 0, 96), 1.0, 1024.0)
+    iota(R("base", W + 3 * K, W + 4 * K), [[1, K]], 1, 0)
+    act(R("vv", 0, K), R("base", W + 3 * K, W + 4 * K), scale=SC)
+    ms(R("mm", 0, 784, 97), 0.0)
+    ms(R("mm", 776, 784), 0.0)
+    ms(R("d97", 0, 784), 1.0)
+    ms(R("d97", 0, 784, 97), 0.0)
+    const(R("d8", 0, 224), 8.0)
+    ms(R("d8", 0, 224, 8), 0.0)
+    const(R("fill", 0, 224), -8192.0 * SC)
+    const(R("fill", 224, 448), -8192.0 * SC)
+    const(R("fill", 448, 672), 8192.0 * SC)
+    const(R("zr", 0, 64), 0.0)
+    act(R("cw", 0, 1024), R("vv", 0, 1024), scale=0.0)
+    const(R("hh", 0, 64), 0.0)
+    for t in range(2):
+        const(R("cg%d" % t, 0, 16), 0.0)
+    for t in range(3):
+        const(R("fl", 224 * t + 28 * r, 224 * t + 28 * r + 28), 0.0)
+    refill()
+    dma("sp", R("h0s", 0, M), T.e0[:, r * M:(r + 1) * M], 114)
+    s = bcast(R("h0s", 0, M), R("h0d", r, r + 1), "ha", 11.0)
+    arrive([R("h0d", q, q + 1) for q in range(N) if q != r], "ha", allin, [s])
+    dma("pool", R("big", 0, W), T.e0[:], 1835, [R("tb", 0, W)])
+    for k in range(N):
+        q = (r + k) % N
+        dma("pool", R("big", W + M * q, W + M * q + M), R("h0d", q, q + 1) if k else T.e0[:, r * M:(r + 1) * M], 229, [R("tb", 0, W)])
+    dma("pool", R("hh", 64, 512), T.e0[:, r * M:(r + 1) * M], 229, [R("big", W, 2 * W)])
+    dma("pool", R("base", 0, W), T.e0[:], 1835, [R("big", W, 2 * W)])
+    top16 = ("top", 16)
+    dma("sp", R("tgb", 0, 768, p=top16), T.tg[:], 25)
+    act(R("tgs", 0, 768, p=top16), R("tgb", 0, 768, p=top16), scale=-64.0)
+
+    def wk(i):
+        return R("wk", 96 * i, 96 * i + 96)
+
+    def qw(i):
+        return R("qw", 32 * i, 32 * i + 32)
+
+    def prepare(t):
+        tag[0] = "prep%d" % t
+        a, m, b = 192 * t, 192 * t + 96, 192 * t + 192
+        cp(R("b16", a, b), R("bti", a, b))
+        ts(R("hq", 0, 192), R("bti", a, b), 1.0 / M, ALU.mult, 0.5 + 0.5 / M, ALU.add)
+        cp(R("hi", a, b), R("hq", 0, 192))
+        tt(R("dn", 96 * t, 96 * t + 96), R("bti", m, b), R("bti", a, m), ALU.subtract)
+        tt(R("dh", 96 * t, 96 * t + 96), R("hi", m, b), R("hi", a, m), ALU.subtract)
+
+    def control(t):
+        cg = "cg%d" % (t % 2)
+        a0 = 192 * t
+        c0 = W + K * t
+        tag[0] = "cg%d" % t
+        for eng, a, b in opt["cg"]:
+            move(eng, R(cg, 16 + 16 * a, 16 + 16 * b), R("tb", 0, W, ind=R("b16", a0 + a, a0 + b)))
+        for a in (0, 64, 128):
+            wrap(R("p_s", a, a + 64), "gs", 0, cg, 16 + 16 * a, 64)
+        sa, sel, mx, th, h1, tn, nm, gr, of1, p1, pos = [wk(i) for i in range(11)]
+        w1, w2, w3, of2, ra, d1, d2, rt, g4, z, xl, du = [wk(i) for i in range(11, 23)]
+        cp(sa, R("p_s", 0, 96))
+        tt(sel, R("p_s", 96, 192), sa, ALU.is_gt)
+        tt(mx, R("p_s", 96, 192), sa, ALU.max)
+        tt(tn, sel, R("dn", 96 * t, 96 * t + 96), ALU.mult)
+        ts(du, mx, 4.0, ALU.is_ge, float(W), ALU.mult)
+        tt(nm, tn, R("bti", a0, a0 + 96), ALU.add)
+        tt(of1, du, nm, ALU.add)
+        cp(R("o16", 96 * t, 96 * t + 96), of1)
+        tag[0] = "cnt%d" % t
+        tt(th, sel, R("dh", 96 * t, 96 * t + 96), ALU.mult)
+        ts(R("nd", 0, 96), mx, 4.0, ALU.is_lt, 128.0, ALU.mult)
+        tt(h1, th, R("hi", a0, a0 + 96), ALU.add)
+        tt(R("kh", 0, 96), h1, R("nd", 0, 96), ALU.add)
+        for h in range(8):
+            ts(R("mm", 97 * h + 1, 97 * h + 97), R("kh", 0, 96), float(h + 1), ALU.is_equal)
+        scan(R("sc", 0, 784), R("d97", 0, 784), R("mm", 0, 784))
+        for i, pb in enumerate(("p_c0", "p_c1")):
+            x = 388 * i
+            mms([(R(pb, 0, 388), R("lt", 0, 128), R("sc", x + 1, x + 389), True, False),
+                 (R(pb, 0, 388), R("ut", 0, 128), R("sc", x, x + 388), False, True)])
+        cn = R("p_s", 192, 288)
+        for i, pb in enumerate(("p_c0", "p_c1")):
+            x = 388 * i
+            tt(R("zz", x, x + 388), R(pb, 0, 388), R("mm", x + 1, x + 389), ALU.mult)
+            if t < RO - 1:
+                if opt["ii"] == "a":
+                    act(R("ii", x, x + 388), R(pb, 0, 388), AF.Sign, scale=-1.0, bias=CAP + 0.5)
+                else:
+                    ts(R("ii", x, x + 388), R(pb, 0, 388), float(CAP), ALU.is_le)
+            lst = [(cn, R("idn", 0, 128), R("zz", x + 97 * h, x + 97 * h + 96), False, i == 1 and h == 3) for h in range(4)]
+            if i == 0:
+                lst = [(cn, R("idn", 0, 128), R("nd", 0, 96), True, False)] + lst
+            mms(lst)
+        ts(gr, cn, float(CAP), ALU.is_le, float(W), ALU.mult)
+        if t > 0:
+            lin(0, p1, h1, 64.0, -65.0)
+            lin(0, w2, sel, 512.0, W)
+            tt(pos, cn, p1, ALU.add)
+        if t < RO - 1:
+            mms([(R("p_s", 288, 384), R("gh", 14 - 2 * h, 142 - 2 * h), R("ii", 97 * h, 97 * h + 96), h == 0, h == 7) for h in range(8)])
+            total(R("tau", 0, 1), R("p_s", 288, 384))
+            if opt["ii"] == "a":
+                ts(R("tau", 1, 2), R("tau", 0, 1), K + 1.0, ALU.add, SC / 2, ALU.mult)
+            else:
+                ts(R("tau", 1, 2), R("tau", 0, 1), 0.5, ALU.add, SC, ALU.mult)
+        if t == 0:
+            tt(xl, nm, gr, ALU.add)
+            cp(R("xl", 0, 96), xl)
+            return
+        tt(w1, pos, gr, ALU.subtract)
+        tt(w3, w1, w2, ALU.add)
+        tt(of2, w3, R("dj", 0, 96), ALU.min)
+        cp(R("c16", 96 * t, 96 * t + 96), of2)
+        tag[0] = "xl%d" % t
+        for a in (0, 96):
+            wrap(R("p_l", a, a + 96), "gs", 144, cg, 16 + 16 * a, 96)
+        lin(1, ra, R("p_l", 0, 96), 1.0, 0.0)
+        tt(d1, R("p_l", 96, 192), ra, ALU.subtract)
+        tt(d2, d1, sel, ALU.mult)
+        tt(rt, ra, d2, ALU.add)
+        lin(1, g4, gr, 4.0, c0 - 4 * W)
+        tt(z, pos, g4, ALU.add)
+        tt(xl, rt, z, ALU.max)
+        cp(R("xl", 96 * t, 96 * t + 96), xl)
+
+    def spread(engs, win, lst, t):
+        n = 96 // len(engs)
+        for i, eng in enumerate(engs):
+            o = R(win[1], win[2], win[3], ind=R(lst, 96 * t + n * i, 96 * t + n * i + n))
+            if eng == "a":
+                act(o, R("vv", 16 * n * i, 16 * n * (i + 1)), AF.Tanh)
+            else:
+                cp(o, R("vv", 16 * n * i, 16 * n * (i + 1)))
+
+    def names(t):
+        last = t == RO - 1
+        tag[0] = "ns%d" % t
+        f0 = 224 * t
+        nfl, ta = R("p_c0", 0, 224), R("p_c0", 224, 448)
+        spread(opt["ns"][t], R("wn", 0, 2 * W), "o16", t)
+        if not last:
+            dma("sp", R("cab", 448, 672), row("wn", W, 2 * W, 1), 114)
+        dma("sp", R("cab", 224, 448), row("wn", W, 2 * W, 0), 114)
+        dma("sp", R("cab", 0, 224), row("wn", 0, W, 0), 114)
+        if not last:
+            refill()
+            ts(nfl, R("cab", 448, 672), R("tau", 1, 2), ALU.is_gt)
+            scan(R("pk", 0, 224), R("d8", 0, 224), nfl)
+            cp(R("fs", 28 * t, 28 * t + 28), R("pk", 7, 224, 8))
+            s = bcast(R("fs", 28 * t, 28 * t + 28), R("fl", f0 + 28 * r, f0 + 28 * r + 28), "fa%d" % t)
+            arrive([R("fl", f0 + 28 * q, f0 + 28 * q + 28) for q in range(N) if q != r], "fa%d" % t, allin, [s])
+        tag[0] = "ptr%d" % t
+        tt(R("cab", 0, 224), R("cab", 0, 224), R("cab", 224, 448), ALU.max)
+        n = 224 if last else 448
+        if not last:
+            ts(ta, R("cab", 0, 224), 0.0, ALU.is_gt, float(N - 1), ALU.add)
+            tt(R("p_c1", 0, 224), R("am", 0, 224), ta, ALU.add)
+            tt(R("p_c1", 224, 448), R("wc", 0, 224), nfl, ALU.mult)
+        act(R("yy", 0, 224), R("cab", 0, 224), scale=1.0 / SC, bias=MAG + W - 1 + K * t)
+        act(R("yz", 0, 224), R("yy", 0, 224), scale=1.0, bias=-MAG)
+        tt(R("p_x", 0, 224), R("yz", 0, 224), R("p_x", 0, 224), ALU.max)
+        if not last:
+            ts(R("gf", 0, 224), R("cab", 448, 672), R("tau", 1, 2), ALU.is_le)
+            tt(R("yz", 224, 448), R("gf", 0, 224), R("p_x", 0, 224), ALU.mult)
+            tt(R("p_x", 224, 448), R("yz", 224, 448), R("p_x", 224, 448), ALU.max)
+        pointers(n)
+        tag[0] = "age%d" % t
+        if not last:
+            tt(R("s1", 0, 112), R("fl", f0, f0 + 112), R("fl", f0 + 112, f0 + 224), ALU.add)
+            tt(R("s2", 0, 56), R("s1", 0, 56), R("s1", 56, 112), ALU.add)
+            tt(R("s3", 0, 28), R("s2", 0, 28), R("s2", 28, 56), ALU.add)
+            for b in range(8):
+                ts(R("dc", b, 224, 8), R("s3", 0, 28), 3 * (7 - b), ALU.logical_shift_right, 7, ALU.bitwise_and)
+            tt(R("tt", 0, 224), R("p_c1", 0, 224), R("dc", 0, 224), ALU.subtract)
+            score(R("p_c1", 224, 448), R("tt", 0, 224))
+            tt(R("am", 0, 224), R("tt", 0, 224), nfl, ALU.mult)
+        else:
+            wrap(R("p_c1", 0, 224), "gs", 144, "tb", 0, 224)
+            cp(R("y16", 0, 224), R("p_c1", 0, 224))
+
+    def lists(t):
+        cg = "cg%d" % (t % 2)
+        tag[0] = "ls%d" % t
+        spread(opt["cs"][t], R("cw", 0, 1024 + K), "c16", t)
+        wrap(R("p_l", 192, 256), "gq", 0, "cw", 0, 64)
+        if t < RO - 1:
+            dma("sp", row("cw", 0, 1024, 0), R("zr", 0, 64), 32)
+        ts(qw(0), R("p_l", 224, 256), 0.5, ALU.is_gt, float(K), ALU.mult)
+        tt(qw(1), R("p_l", 192, 224), qw(0), ALU.add)
+        tt(qw(2), R("p_l", 224, 256), qw(1), ALU.add)
+        ts(qw(3), qw(2), MAG + 15.0, ALU.add)
+        ts(R("q16", 32 * t, 32 * t + 32), qw(3), -MAG, ALU.add)
+        act(R("lg", 0, 512), R(cg, 0, 16 + 2 * K, ind=R("q16", 32 * t, 32 * t + 32)))
+        wrap(R("p_l", 256, 288), "gs", 144, "lg", 0, 32)
+        wrap(R("p_l", 288, 320), "gs", 288, "lg", 0, 32)
+        wrap(R("p_l", 320, 352), "gs", 432, "lg", 0, 32)
+        l0 = 256 * t
+        mine = R("ll", l0 + 32 * r, l0 + 32 * r + 32)
+        cp(R("rb16", 64 * t, 64 * t + 64), R("p_l", 256, 320))
+        tt(qw(4), R("p_l", 320, 352), R("kk", 0, 32), ALU.max)
+        cp(mine, qw(4))
+        s = bcast(mine, mine, "la%d" % t)
+        arrive([R("ll", l0 + 32 * q, l0 + 32 * q + 32) for q in range(N) if q != r], "la%d" % t, allin, [s])
+
+    def data(t):
+        c0 = W + K * t
+
+        def home(s):
+            return R("hh", 0, 512, ind=R("ll", 256 * t + 32 * s + 4 * r, 256 * t + 32 * s + 4 * r + 4))
+        tag[0] = "hm%d" % t
+        if t > 0:
+            p0 = 512 * (t - 1)
+            act(R("bs", 0, 512), R("base", 0, c0, ind=R("rb16", 64 * t + 32, 64 * t + 64)))
+            tt(R("psn", p0, p0 + 512), R("big", 0, c0, ind=R("rb16", 64 * t, 64 * t + 32)), R("bs", 0, 512), ALU.subtract)
+            ss = [send([(R("psn", p0 + 64 * d, p0 + 64 * d + 64), [(d, R("pl", p0 + 64 * r, p0 + 64 * r + 64))], es, "pa%d" % r)
+                        for d, es in c], lat) for c, lat in ((c1, 3.6), (c2, 3.8))]
+            order = [r] + sorted(into, key=lambda s: (s not in near, into[s][0], (s - r) % N))
+            for i, s in enumerate(order):
+                if s == r:
+                    src = R("psn", p0 + 64 * r, p0 + 64 * r + 64)
+                else:
+                    src = R("pl", p0 + 64 * s, p0 + 64 * s + 64)
+                    arrive([src], "pa%d" % s, t * into[s][1], [ss[0 if i <= 5 else 1]])
+                tm = R("tm", 64 * (i % 2), 64 * (i % 2) + 64)
+                if opt["home"][t] == "a":
+                    act(tm, home(s))
+                    tt(home(s), tm, src, ALU.add)
+                else:
+                    tt(tm, home(s), src, ALU.add)
+                    cp(home(s), tm)
+        a0 = 512 * (t - 1)
+        for i, d in enumerate([d for d, es in c1 + c2] + [r] if t else []):
+            o = R("big", c0 + 64 * r, c0 + 64 * r + 64) if d == r else R("asn", a0 + 64 * d, a0 + 64 * d + 64)
+            move("act" if opt["ans"][t][i] == "a" else "dve", o, home(d))
+        if t > 0:
+            ss = [send([(R("asn", a0 + 64 * d, a0 + 64 * d + 64), [(d, R("big", c0 + 64 * r, c0 + 64 * r + 64))], es, "aa%d" % t)
+                        for d, es in c], lat) for c, lat in ((c1, 3.6), (c2, 3.8))]
+            arrive([R("big", c0 + 64 * q, c0 + 64 * q + 64) for q in range(N) if q != r], "aa%d" % t, sum(v[1] for v in into.values()), ss)
+        if t == RO - 1:
+            dma("sp", T.yh[:], R("hh", 64, 512), 229)
+        tag[0] = "st%d" % t
+        pp = R("p_p", 0, 192)
+        mms([(pp, R("ee", 0, 128, p=top16), R("tgs", 192 * t, 192 * t + 192, p=top16), True, False)])
+
+        def xg(a, b):
+            return R("big", 0, c0 + 512 if t else 2 * W, ind=R("xl", 96 * t + a, 96 * t + b))
+        for k in range(4):
+            xa = R("base", c0 + 192 * k, c0 + 192 * k + 192)
+            act(xa, xg(12 * k, 12 * k + 12))
+            tt(R("pr", 192 * k, 192 * k + 192), xg(48 + 12 * k, 60 + 12 * k), xa, ALU.mult)
+            mms([(pp, R("ee", 0, 128), R("pr", 192 * k, 192 * k + 192), False, k == 3)])
+        act(R("base", c0 + 768, c0 + 1152), xg(48, 72))
+        act(R("base", c0 + 1152, c0 + 1536), xg(72, 96))
+        act(R("es", 0, 192), pp, AF.Tanh, scale=-1.0 / 64, bias=0.0)
+        act(R("p_p", 0, 192), R("es", 0, 192), scale=1.0 / 64)
+        act(R("p_p", 192, 384), R("es", 0, 192), scale=1.0 / 64)
+        for i, (own, par) in enumerate(((768, 0), (1152, 384), (0, 768), (384, 1152))):
+            tb = R("p_t%d" % (i % 2), 0, 384)
+            tt(tb, R("base", c0 + par, c0 + par + 384), R("p_p", 0, 384), ALU.mult)
+            tt(R("big", c0 + own, c0 + own + 384), R("base", c0 + own, c0 + own + 384), tb, ALU.add)
+
+    for t in range(RO):
+        prepare(t)
+    for t in range(RO):
+        control(t)
+        if t < RO - 1:
+            names(t)
+            if t > 0:
+                lists(t)
+        else:
+            lists(t)
+            names(t)
+        data(t)
+    for i in range(8):
+        a = M * i
+        move("dve" if opt["fin"][i] == "d" else "act", R("base", a, a + M), R("big", 0, W + RO * K, ind=R("y16", 28 * i, 28 * i + 28)))
+        dma("sp" if i % 2 == 0 else "pool", T.yr[:, a:a + M], R("base", a, a + M), 229)
+    return ops, sent[0]
+
+
+def clash(x, y):
+    if x[1] != y[1] or x[3] <= y[2] or y[3] <= x[2]:
+        return False
+    if x[4] > 1 and x[4] == y[4] and (x[2] - y[2]) % x[4]:
+        return False
+    return not (x[5] and y[5] and x[5][0] == "rows" and y[5][0] == "rows" and x[5][1] != y[5][1])
+
+
+def depends(ops):
+    seen = {}
+    deps = []
+    for i, o in enumerate(ops):
+        d = set()
+        mine = [(x, False) for x in o["rd"]] + [(x, True) for x in o["wr"]]
+        for x, w in mine:
+            for j, y, v in seen.get(x[1], ()):
+                if (x[1] in PSUM and ops[j]["eng"] != o["eng"]) or ((w or v) and clash(x, y)):
+                    d.add(j)
+        for x, w in mine:
+            seen.setdefault(x[1], []).append((i, x, w))
+        deps.append(d)
+    return deps
+
+
+def schedule(ops, deps, opt):
+    n = len(ops)
+    pre = [set(deps[i]) | set(ops[i]["after"]) for i in range(n)]
+    succ = [[] for i in range(n)]
+    for i in range(n):
+        for j in pre[i]:
+            succ[j].append(i)
+    tail = [0.0] * n
+    for i in range(n - 1, -1, -1):
+        tail[i] = ops[i]["cost"] + ops[i]["lat"] + 0.08 + max([tail[j] for j in succ[i]] + [0.0])
+    tail = [tail[i] + opt["bias"].get(ops[i]["tag"], 0.0) for i in range(n)]
+    left = [len(p) for p in pre]
+    ready = [0.0] * n
+    free = {}
+    pool = [i for i in range(n) if left[i] == 0]
+    order = []
+    times = {}
+    while pool:
+        best = None
+        for e in sorted(set(ops[i]["eng"] for i in pool)):
+            c = [i for i in pool if ops[i]["eng"] == e]
+            t0 = max(free.get(e, 0.0), min(ready[i] for i in c))
+            i = max([i for i in c if ready[i] <= t0 + opt["look"]], key=lambda i: (tail[i] - max(0.0, ready[i] - t0), -i))
+            if best is None or t0 < best[0]:
+                best = (t0, max(free.get(e, 0.0), ready[i]), i)
+        t0, s, i = best
+        pool.remove(i)
+        e = ops[i]["eng"]
+        if e != "net":
+            free[e] = s + ops[i]["cost"]
+        end = s + ops[i]["cost"] + ops[i]["lat"]
+        times[i] = (s, end)
+        order.append(i)
+        for j in succ[i]:
+            ready[j] = max(ready[j], end + 0.08)
+            left[j] -= 1
+            if left[j] == 0:
+                pool.append(j)
+    return order, times
+
+
+def rank_program(g, core, T, topo):
+    r = T.rank_of(core)
+    if r is None:
+        return
+    ops, sent = plan(r, T, topo, PLAN, OPT)
+    deps = depends(ops)
+    ref = plan(0, T, topo, PLAN, OPT)[0]
+    order, times = schedule(ref, depends(ref), OPT)
+    queue = {"dve": g.vector, "act": g.scalar, "pe": g.tensor, "pool": g, "sp": g.sync}
+    count = {}
+    mark = {}
+    clock = {}
+    known = {e: {} for e in queue}
+    top = {}
+    for i in order:
+        o = ops[i]
+        e = o["eng"]
+        if e == "net":
+            mark[i] = o["sem"]
+            clock[i] = {o["sem"][0]: o["sem"][1]}
+            top[o["sem"][0]] = max(top.get(o["sem"][0], 0), o["sem"][1])
+            continue
+        kn = known[e]
+        need = {}
+        for j in deps[i]:
+            if e == "pe" and ops[j]["eng"] == "pe":
+                continue
+            s, v = mark[j]
+            if kn.get(s, 0) < v and need.get(s, (0, 0))[0] < v:
+                need[s] = (v, j)
+        for s, (v, j) in sorted(need.items(), key=lambda x: -times[x[1][1]][1]):
+            if kn.get(s, 0) < v:
+                queue[e].wait_ge(T.sem[s], v)
+                for s2, v2 in clock[j].items():
+                    kn[s2] = max(kn.get(s2, 0), v2)
+        ins = o["call"](g)
+        if ins is None:
+            continue
+        if o["sem"] is None:
+            count[e] = count.get(e, 0) + 1
+            mark[i] = (e, count[e])
+            ins.then_inc(T.sem[e], 1)
+        else:
+            mark[i] = o["sem"]
+            ins.then_inc(T.sem[o["sem"][0]], 16)
+        c = dict(kn)
+        c[mark[i][0]] = mark[i][1]
+        clock[i] = c
+        top[mark[i][0]] = max(top.get(mark[i][0], 0), mark[i][1])
+    top["sent"] = sent
+    for s in sorted(top):
+        g.wait_ge(T.sem[s], top[s])

@@ -1,10 +1,14 @@
 from concourse.bass import DstId, RemoteDMATransfer
-from concourse.mybir import AluOpType as ALU, ActivationFunctionType as AF, AxisListType as AX
+from concourse.mybir import AluOpType as ALU, ActivationFunctionType as AF
 
 N, W, K, M, RO, CAP = 8, 3584, 1536, 448, 4, 64
-MAG = 12582912.0
-SC = 2.0 ** -17
-F, B16, I32, U16 = "float32", "bfloat16", "int32", "uint16"
+SC = 2.0 ** -18
+V0 = K + 65
+KP = K + 64
+O = RO * KP
+KH = 152
+BIG = 12288.0
+F, B16, H16, I32, U16 = "float32", "bfloat16", "float16", "int32", "uint16"
 
 
 def sb(n, d):
@@ -12,35 +16,31 @@ def sb(n, d):
 
 
 SCRATCH = {
-    "big": sb(W + RO * K, F), "base": sb(W + RO * K, F), "wn": sb(2 * W, F), "cw": sb(1024 + K, F), "tb": sb(W, B16),
-    "cs": sb(8 * 224, B16), "vv": sb(K, F), "hh": sb(512, F), "bti": sb(768, I32), "b16": sb(768, U16), "hq": sb(192, F),
-    "hi": sb(768, I32), "dn": sb(384, F), "dh": sb(384, F), "lagc": sb(224, I32), "wc": sb(224, B16), "am": sb(224, F),
-    "tt": sb(224, F), "cab": sb(672, F), "yy": sb(448, F), "yz": sb(448, F), "fill": sb(672, F), "zr": sb(64, F), "pk": sb(224, F),
-    "d8": sb(224, F), "gf": sb(224, F), "dc": sb(224, I32), "s1": sb(112, F), "s2": sb(56, F), "s3": sb(28, I32), "fs": sb(84, F),
-    "fl": sb(672, F), "pi": sb(8, I32), "pc": sb(24, F), "xr": sb(224, F), "e1": sb(144, F), "gs": sb(576, B16), "gq": sb(144, F),
-    "gh": sb(144, B16), "ge": sb(384, F), "lt": sb(128, B16), "ut": sb(128, B16), "idn": sb(128, B16), "x16": sb(128, F),
-    "ee": sb(128, F), "dj": sb(96, F), "kk": sb(32, F), "vq": sb(224, F), "mm": sb(784, B16), "sc": sb(784, B16), "d97": sb(784, B16),
-    "zz": sb(784, B16), "ii": sb(784, B16), "tau": sb(8, F), "wk": sb(23 * 96, F), "nd": sb(96, B16), "kh": sb(96, B16),
-    "o16": sb(384, U16), "c16": sb(384, U16), "xl": sb(384, U16), "qw": sb(160, F), "q16": sb(128, U16), "lg": sb(512, B16),
-    "rb16": sb(256, U16), "ll": sb(RO * 256, U16), "bs": sb(512, F), "psn": sb(1536, F), "pl": sb(1536, F), "tm": sb(128, F),
-    "asn": sb(1536, F), "h0s": sb(M, B16), "h0d": ("dram", [N, 128, M], B16), "pr": sb(768, F), "tgb": sb(768, B16), "tgs": sb(768, F), "es": sb(192, F), "y16": sb(224, U16),
-    "cg0": sb(16 + 2 * K, B16), "cg1": sb(16 + 2 * K, B16),
+    "bg": sb(O + W + RO * K, F), "eb": sb(2 * W, B16), "wn": sb(W, F), "cw": sb(K + 3072, B16), "tb": sb(W, B16), "vv": sb(K, F),
+    "vb": sb(K, B16), "vt": sb(288, B16), "hb": sb(512, F), "ho": sb(M, F), "tn": sb(512, F),
+    "cg0": sb(64 + 2 * K, B16), "cg1": sb(64 + 2 * K, B16), "hh": sb(512, F), "bti": sb(768, I32), "b16": sb(768, U16),
+    "lagc": sb(224, I32), "wc": sb(224, B16), "cs": sb(8 * 224, B16), "ag": sb(224, B16), "sg": sb(448, B16), "ng": sb(224, B16),
+    "cab": sb(448, F), "pt": sb(448, F), "ct": sb(7 * 224, B16), "fill": sb(448, F), "zr": sb(1024, B16), "pk": sb(224, H16), "d4": sb(224, B16),
+    "dc": sb(224, I32), "s3": sb(56, I32), "fs": sb(3 * 56, H16), "fl": sb(3 * 448, H16), "pi": sb(8, I32), "pc": sb(16, F),
+    "xr": sb(576, F), "x16": sb(128, F), "gs": sb(576, B16), "gh": sb(144, B16), "ge": sb(384, F), "lt": sb(128, B16),
+    "ut": sb(128, B16), "im": sb(7 * 128, B16), "i32": sb(256, F), "i16": sb(128, H16), "ee": sb(128, F), "dj": sb(96, F), "kk": sb(32, F),
+    "t15": sb(224, B16), "t24": sb(96, B16), "mm": sb(784, B16), "sc": sb(784, B16), "d97": sb(784, B16), "zz": sb(784, B16),
+    "ii": sb(784, B16), "tau": sb(104, F), "sl": sb(768, B16), "dd": sb(768, F), "nm": sb(192, F), "wk": sb(10 * 96, F), "nd": sb(96, B16),
+    "kh": sb(96, B16), "o16": sb(384, U16), "c16": sb(384, U16), "xl": sb(384, U16), "qw": sb(64, F), "q16": sb(128, U16),
+    "lg": sb(512, B16), "ml": sb(RO * 128, U16), "ll": sb(RO * 256, U16), "bs": sb(1024, F), "psn": sb(1536, F), "pl": sb(1536, F),
+    "tm": sb(128, F), "asn": sb(1536, F), "pr": sb(768, F), "tgb": sb(768, B16), "tgs": sb(768, F), "es": sb(192, F), "y16": sb(224, U16),
 }
-PSUM = ("p_s", "p_c0", "p_c1", "p_l", "p_p", "p_x", "p_t0", "p_t1")
+PSUM = ("p_s", "p_c0", "p_c1", "p_n", "p_l", "p_p", "p_t0", "p_t1")
 for _n in PSUM:
     SCRATCH[_n] = ("psum", [128, 512], F)
-ND = 72
+ND = 80
 SEMAPHORES = (["dve", "act", "pe", "pool", "sent", "ha"] + ["d%d" % i for i in range(ND)] + ["fa%d" % t for t in range(3)]
               + ["la%d" % t for t in range(1, RO)] + ["aa%d" % t for t in range(1, RO)] + ["pa%d" % s for s in range(N)])
 
-PLAN = {"cy": 0.00104, "ga": 1.56, "sa": 3.8, "pe": 0.00055, "dma": 1.9, "net": 1.0}
-OPT = {"cg": (("act", 0, 64), ("dve", 64, 128), ("act", 128, 160), ("dve", 160, 192)), "ns": ("a", "a", "a", "aaa"),
-       "cs": ("aaa", "aaa", "aaa", "a"), "home": "dddd", "lin": "ddad", "ii": "a", "ans": ("dddddddd",) * 3 + ("dadadada",), "fin": "dadadada", "look": 0.6,
-       "bias": {'cg0': 0.4, 'cg1': 21.3, 'xl2': 1.2, 'ns1': -1.3, 'ns3': -6.3, 'ns0': -6.9, 'age0': 22.7, 'st3': -30.8, 'hm3': -5.5,
-                'st0': -1.1, 'ptr3': -0.3, 'prep2': 2.0, 'st1': 0.4, 'ptr0': -13.6, 'cnt2': -0.8, 'prep3': 4.6, 'prep1': -4.6,
-                'ns2': 6.5, 'ptr2': 0.7, 'hm2': -1.5, 'ls1': -1.1, 'age3': 18.5, 'st2': -0.1, 'ls3': 0.2, 'cnt1': 1.5, 'age2': 0.7,
-                'age1': -0.2, 'cnt0': -0.2, 'xl3': -1.8, 'cnt3': 0.2, 'xl1': -2.2, 'init': 0.1, 'cg2': -0.4, 'cg3': 1.2, 'ls2': 0.8,
-                'prep0': 0.3}}
+PLAN = {"cy": 0.0009, "ga": 1.5, "sa": 3.3, "pe": 0.00048, "dma": 1.9, "net": 1.0, "gap": 0.08}
+OPT = {"cg": (("a", 0, 48), ("d", 48, 96), ("a", 96, 144), ("d", 144, 192)), "ns": ("a", "a", "a", "aaa"), "cs": (0, 4, 4, 4),
+       "home": "ab", "x2": "aa", "step": "mqqd", "ans": ("", "dadadada", "dadadada", "dadadada"), "fin": "dadadada", "tries": 1000}
+OTHER = ({"cy": 0.00083, "ga": 1.2, "sa": 2.0, "net": 1.25}, {"cy": 0.0011, "ga": 1.8, "sa": 5.0, "pe": 0.0006, "gap": 0.1})
 
 
 def R(name, a, b, step=1, p=None, ind=None):
@@ -85,8 +85,8 @@ def plan(r, T, topo, sc, opt):
     nd = [0]
     tag = ["init"]
 
-    def add(eng, call, reads, writes, cost, lat=0.0, sem=None, after=()):
-        ops.append({"eng": eng, "call": call, "rd": [x for x in reads if isr(x)], "wr": [x for x in writes if isr(x)],
+    def add(eng, call, reads, writes, cost, lat=0.0, sem=None, after=(), behind=()):
+        ops.append({"eng": eng, "bh": list(behind), "call": call, "rd": [x for x in reads if isr(x)], "wr": [x for x in writes if isr(x)],
                     "tag": tag[0], "cost": cost, "lat": lat, "sem": sem, "after": list(after)})
         return len(ops) - 1
 
@@ -94,8 +94,6 @@ def plan(r, T, topo, sc, opt):
         if not isr(x):
             return x
         t = T[x[1]]
-        if x[1] == "h0d":
-            return t[x[2]]
         p = x[5]
         ps = slice(None) if p is None else (slice(p[1], 128, 16) if p[0] == "rows" else slice(0, p[1]))
         a = t[ps, x[2]:x[3]] if x[4] == 1 else t[ps, x[2]:x[3]:x[4]]
@@ -105,7 +103,7 @@ def plan(r, T, topo, sc, opt):
         return [x[6] for x in xs if isr(x) and x[6]]
 
     def two(*xs):
-        return all(SCRATCH[x[1]][2] in (B16, U16) for x in xs)
+        return all(SCRATCH[x[1]][2] in (B16, H16, U16) for x in xs)
 
     def vcost(o, i, base):
         if o[6]:
@@ -135,39 +133,33 @@ def plan(r, T, topo, sc, opt):
         return add("dve", lambda g: g.vector.tensor_tensor_scan(ap(o), ap(d0), ap(d1), 0.0, ALU.mult, ALU.add), [d0, d1], [o],
                    vcost(o, d1, 0.5 if two(o, d0, d1) else 1))
 
-    def total(o, a):
-        return add("dve", lambda g: g.vector.tensor_reduce(ap(o), ap(a), AX.X, ALU.add), [a], [o], vcost(o, a, 1))
-
-    def act(o, a, func=AF.Identity, scale=None, bias=None):
+    def act(o, a, func=AF.Identity, scale=None, bias=None, total=None):
         if scale is None:
             call = lambda g: g.scalar.activation(ap(o), ap(a), func)
         else:
             call = lambda g: g.scalar.activation(ap(o), ap(a), func, bias=ap(bias) if isr(bias) else float(bias or 0.0),
-                                                 scale=ap(scale) if isr(scale) else float(scale))
-        return add("act", call, [a, scale, bias] + offs(o, a), [o], 0.015 + vcost(o, a, 1))
-
-    def lin(key, o, a, scale, bias):
-        if opt["lin"][key] == "a":
-            return act(o, a, scale=scale, bias=bias)
-        return ts(o, a, scale if isr(scale) else float(scale), ALU.mult, bias if isr(bias) else float(bias), ALU.add)
+                                                 scale=ap(scale) if isr(scale) else float(scale), accum_out=ap(total))
+        return add("act", call, [a, scale, bias] + offs(o, a), [o, total], 0.015 + vcost(o, a, 1))
 
     def const(o, v):
-        return lin(2, o, R("xr", 0, cnt(o)), 0.0, v)
+        return act(o, R("xr", 0, cnt(o)), scale=0.0, bias=v)
 
     def move(eng, o, a):
-        return cp(o, a) if eng == "dve" else act(o, a)
+        return cp(o, a) if eng == "d" else act(o, a)
 
     def mms(lst):
+        lst = [q if len(q) == 5 else q + (i == 0, i == len(lst) - 1) for i, q in enumerate(lst)]
+
         def call(g):
             ins = None
             for o, l, x, s0, s1 in lst:
                 ins = g.tensor.matmul(ap(o), ap(l), ap(x), s0, s1)
             return ins
-        c = sum(max(64, cnt(x)) * (4 if SCRATCH[x[1]][2] == F else 1) for o, l, x, s0, s1 in lst)
-        return add("pe", call, [q[1] for q in lst] + [q[2] for q in lst], [q[0] for q in lst], 0.1 + c * PEC)
+        c = sum(max(64, cnt(q[2])) * (4 if SCRATCH[q[2][1]][2] == F else 1) for q in lst)
+        return add("pe", call, [q[1] for q in lst] + [q[2] for q in lst], [q[0] for q in lst], c * PEC, 0.08)
 
-    def wrap(o, sel, s0, src, a, n):
-        return mms([(o, R(sel, s0 + 15 - i, s0 + 143 - i), R(src, a + i, a + 16 * n, 16), i == 0, i == 15) for i in range(16)])
+    def wrap(o, sel, s0, src, a, n, more=()):
+        return mms([(o, R(sel, s0 + 15 - i, s0 + 143 - i), R(src, a + i, a + 16 * n, 16)) for i in range(16)] + list(more))
 
     def iota(o, pat, base, cm):
         if SCRATCH[o[1]][2] != I32:
@@ -176,16 +168,18 @@ def plan(r, T, topo, sc, opt):
             call = lambda g: g.iota(ap(o), pat, base, cm)
         return add("pool", call, [], [o], 0.13 + 2 * cnt(o) * CY)
 
-    def dma(q, o, a, kb, behind=()):
+    def dma(q, o, a, kb, behind=(), adds=False):
         s = "d%d" % nd[0]
         nd[0] += 1
         if q == "sp":
             call = lambda g: g.sync.dma_start(ap(o), ap(a))
         elif q == "act":
             call = lambda g: g.scalar.dma_start(ap(o), ap(a))
+        elif adds:
+            call = lambda g: g.dma_start(ap(o), ap(a), accum_op=ALU.add)
         else:
             call = lambda g: g.dma_start(ap(o), ap(a))
-        return add(q, call, [a] + list(behind), [o], 0.1 if q != "pool" else 0.5, sc["dma"] + kb / 200.0, (s, 16))
+        return add(q, call, [a] + ([o] if adds else []), [o], 0.07 if q != "pool" else 0.5, sc["dma"] + kb / 400.0, (s, 16), (), behind)
 
     def dst(d):
         a = topo.addr(cores[d])
@@ -193,133 +187,147 @@ def plan(r, T, topo, sc, opt):
 
     sent = [0]
 
-    def send(trs, lat):
+    def send(trs, lat, behind=()):
         def call(g):
             g.remote_dma_fused([RemoteDMATransfer(dst_ids=[dst(d) for d, x in ds], dma_engine_mask=msk(es), remote_sem=T.sem[sm],
                                                   srcs=[ap(s)], dsts=[ap(x) for d, x in ds]) for s, ds, es, sm in trs],
                                local_sem=T.sem.sent)
             return None
         sent[0] += sum(len(q[2]) for q in trs)
-        return add("pool", call, [q[0] for q in trs], [], 0.8, lat * sc["net"], ("none", 0))
+        return add("pool", call, [q[0] for q in trs], [], 0.8, lat * sc["net"], ("none", 0), (), behind)
 
     def arrive(writes, sm, val, after):
         return add("net", None, [], writes, 0.0, 0.0, (sm, val), after)
 
     near, far, en, ef = peers(r, cores, topo)
     c1, c2 = pieces(r, cores, topo)
+    others = [q for q in range(N) if q != r]
     into = {}
     allin = 0
-    for s in range(N):
-        if s != r:
-            for i, c in enumerate(pieces(s, cores, topo)):
-                for d, es in c:
-                    if d == r:
-                        into[s] = (i, len(es))
-            q = peers(s, cores, topo)
-            allin += len(q[2]) if r in q[0] else len(q[3])
+    for s in others:
+        for i, c in enumerate(pieces(s, cores, topo)):
+            for d, es in c:
+                if d == r:
+                    into[s] = (i, len(es))
+        q = peers(s, cores, topo)
+        allin += len(q[2]) if r in q[0] else len(q[3])
 
-    def bcast(src, land, sm, lat=3.6):
-        return send([(src, [(d, land) for d in far], ef, sm), (src, [(d, land) for d in near], en, sm)], lat)
+    def bcast(src, land, sm, lat=3.2, behind=()):
+        return send([(src, [(d, land) for d in far], ef, sm), (src, [(d, land) for d in near], en, sm)], lat, behind)
 
     def row(name, a, b, i):
         return R(name, a, b, p=("rows", i))
 
+    def xr(n):
+        return R("xr", 0, n)
+
+    I1, IHALF, I64, I512, IBIG, INEG, ISC = [R("im", 128 * i, 128 * i + 128) for i in range(7)]
+    FSC, FNEG = R("i32", 0, 128), R("i32", 128, 256)
+    wc, ng, age = R("wc", 0, 224), R("ng", 0, 224), R("ag", 0, 224)
+    yy, prod = R("p_c1", 0, 224), R("p_c1", 224, 448)
+    hi, lo = R("cs", 0, 224), R("cs", 224, 448)
+
+    def score():
+        tt(hi, yy, wc, ALU.mult)
+        dma("sp", row("tb", 0, W, 1), hi, 57)
+        tt(prod, yy, wc, ALU.mult)
+        tt(lo, prod, hi, ALU.subtract)
+        dma("sp", row("tb", 0, W, 2), lo, 57)
+
+    def overdue():
+        act(age, yy)
+        mms([(R("p_n", 0, 224), I1, x) for x in (wc, hi, lo)])
+        act(R("sg", 224, 448), R("p_n", 0, 224), AF.Sign, scale=1.0, bias=2.0 ** -10 - 4.0)
+
+    def refill():
+        dma("sp", row("wn", 0, W, 1), R("fill", 224, 448), 114)
+        dma("sp", row("wn", 0, W, 0), R("fill", 0, 224), 114)
+
     dma("sp", R("lagc", 0, 224), T.lag[:], 114)
-    dma("act", R("wc", 0, 224), T.wt[:], 57)
+    dma("act", wc, T.wt[:], 57)
     dma("sp", R("bti", 0, 768), T.bt[:], 393)
     ms(R("tb", 0, W), 0.0)
     dma("sp", row("tb", 0, W, 0), T.wt[:], 57)
-    ts(R("am", 0, 224), R("lagc", 0, 224), -1.0, ALU.add)
-
-    def score(a, b):
-        tt(R("cs", 0, 224), a, b, ALU.mult)
-        tt(R("p_s", 288, 512), a, b, ALU.mult)
-        dma("sp", row("tb", 0, W, 1), R("cs", 0, 224), 57)
-        tt(R("cs", 224, 448), R("p_s", 288, 512), R("cs", 0, 224), ALU.subtract)
-        dma("sp", row("tb", 0, W, 2), R("cs", 224, 448), 57)
-
-    score(R("am", 0, 224), R("wc", 0, 224))
+    ts(yy, R("lagc", 0, 224), -1.0, ALU.add)
+    score()
+    cp(R("b16", 0, 192), R("bti", 0, 192))
     iota(R("pi", 0, 1), [[0, 1]], 0, 1)
-    iota(R("xr", 0, 224), [[1, 224]], 0, 0)
+    iota(xr(576), [[1, 576]], 0, 0)
     iota(R("x16", 0, 128), [[0, 8], [1, 16]], 0, 0)
-    ts(R("pi", 1, 2), R("pi", 0, 1), 15, ALU.bitwise_and)
-    ts(R("pi", 2, 3), R("pi", 0, 1), 1, ALU.bitwise_and)
-    cp(R("pc", 0, 3), R("pi", 0, 3))
-    pc = [R("pc", i, i + 1) for i in range(24)]
-    P_, P16, P2 = pc[:3]
-    tt(pc[3], P_, P16, ALU.subtract)
-    ts(pc[4], pc[3], 15.0, ALU.add)
-    ts(pc[5], P16, 224.0, ALU.mult)
-    ts(pc[6], P2, 224.0, ALU.mult, 64.0, ALU.add)
-    ts(R("e1", 0, 144), R("xr", 0, 144), pc[4], ALU.is_equal)
-    for i, (lo, hi) in enumerate(((0, 2), (3, 4), (5, 6), (7, 8))):
-        ts(pc[8 + i], P16, float(hi), ALU.is_le)
-        ts(pc[12 + i], P16, float(lo), ALU.is_ge, pc[8 + i], ALU.mult)
-        lin(2, R("gs", 144 * i, 144 * i + 144), R("e1", 0, 144), pc[12 + i], 0.0)
-    ts(pc[7], P16, 0.0, ALU.is_equal, 1.0 / SC, ALU.mult)
-    lin(2, R("gq", 0, 144), R("e1", 0, 144), pc[7], 0.0)
-    ms(R("gh", 0, 144), 0.0)
-    tt(R("gh", 0, 143), R("e1", 0, 143), R("e1", 1, 144), ALU.add)
-    ts(R("ge", 0, 128), R("xr", 0, 128), pc[3], ALU.is_ge)
-    ts(R("ge", 128, 256), R("xr", 0, 128), P_, ALU.is_ge)
-    ts(R("ge", 256, 384), R("xr", 0, 128), pc[4], ALU.is_gt)
-    tt(R("ut", 0, 128), R("ge", 0, 128), R("ge", 128, 256), ALU.subtract)
-    tt(R("lt", 0, 128), R("ge", 128, 256), R("ge", 256, 384), ALU.subtract)
-    ts(R("idn", 0, 128), R("xr", 0, 128), P_, ALU.is_equal)
-    ts(R("ee", 0, 128), R("x16", 0, 128), P16, ALU.is_equal)
-    lin(2, R("p_x", 0, 224), R("xr", 0, 224), 1.0, pc[5])
-    lin(2, R("p_x", 224, 448), R("xr", 0, 224), 1.0, pc[5])
-    lin(2, R("vq", 0, 224), R("xr", 0, 224), 1.0, pc[6])
-    act(R("cs", 1344, 1568), R("vq", 0, 224))
-    tt(R("cs", 1568, 1792), R("vq", 0, 224), R("cs", 1344, 1568), ALU.subtract)
-    dma("sp", row("tb", 0, W, 7), R("cs", 1344, 1568), 57)
-    dma("sp", row("tb", 0, W, 8), R("cs", 1568, 1792), 57)
-
-    def pointers(n):
-        act(R("cs", 448, 448 + n), R("p_x", 0, n))
-        tt(R("cs", 896, 896 + n), R("p_x", 0, n), R("cs", 448, 448 + n), ALU.subtract)
-        dma("sp", row("tb", 0, W, 3), R("cs", 448, 672), 57)
-        dma("sp", row("tb", 0, W, 4), R("cs", 896, 1120), 57)
-        if n > 224:
-            dma("sp", row("tb", 0, W, 5), R("cs", 672, 896), 57)
-            dma("sp", row("tb", 0, W, 6), R("cs", 1120, 1344), 57)
-
-    def refill():
-        dma("sp", row("wn", 0, 2 * W, 0), R("fill", 0, 448), 229)
-        dma("sp", row("wn", W, 2 * W, 1), R("fill", 448, 672), 114)
-
-    lin(2, R("dj", 0, 96), R("xr", 0, 96), 16.0, P16)
-    for h in range(8):
-        act(R("kk", 4 * h, 4 * h + 4), R("dj", 0, 4))
-    lin(2, R("dj", 0, 96), R("dj", 0, 96), 1.0, 1024.0)
-    iota(R("base", W + 3 * K, W + 4 * K), [[1, K]], 1, 0)
-    act(R("vv", 0, K), R("base", W + 3 * K, W + 4 * K), scale=SC)
-    ms(R("mm", 0, 784, 97), 0.0)
-    ms(R("mm", 776, 784), 0.0)
+    own = R("eb", W + M * r, W + M * r + M)
+    dma("act", own, T.e0[:, r * M:(r + 1) * M], 114)
+    s = bcast(own, own, "ha", 9.0, [row("tb", 0, W, 1), row("tb", 0, W, 2)])
+    arrive([R("eb", W + M * q, W + M * q + M) for q in others], "ha", allin, [s])
+    dma("sp", R("eb", 0, W), T.e0[:], 917, [row("tb", 0, W, 1), row("tb", 0, W, 2)])
+    for i, (sh, bits) in enumerate(((0, 15), (0, 1), (2, 3))):
+        ts(R("pi", i + 1, i + 2), R("pi", 0, 1), sh, ALU.logical_shift_right, bits, ALU.bitwise_and)
+    cp(R("pc", 0, 4), R("pi", 0, 4))
+    pc = [R("pc", i, i + 1) for i in range(16)]
+    P_, P16, P2, P4 = pc[:4]
+    tt(pc[4], P_, P16, ALU.subtract)
+    ts(pc[5], pc[4], 15.0, ALU.add)
+    ts(pc[6], P4, 144.0, ALU.mult, pc[5], ALU.add)
+    ts(R("gs", 0, 576), xr(576), pc[6], ALU.is_equal)
+    ts(I1, xr(128), P_, ALU.is_equal)
+    for x, v in ((IHALF, 0.5), (I64, 64.0), (I512, 512.0), (IBIG, BIG), (INEG, -BIG), (ISC, 1 / SC), (FSC, 1 / SC), (FNEG, -1 / SC)):
+        act(x, I1, scale=v)
+    cp(R("i16", 0, 128), I1)
+    overdue()
+    for a in range(0, K, 512):
+        act(R("vv", a, a + 512), xr(512), scale=SC, bias=(a + V0) * SC)
+    act(R("hh", 0, 64), xr(64), AF.Tanh, scale=0.0)
+    const(R("fill", 0, 224), -16384.0 * SC)
+    const(R("fill", 224, 448), 16384.0 * SC)
+    refill()
+    ms(R("sl", 0, 768), 0.0)
+    ms(R("mm", 0, 784), 0.0)
     ms(R("d97", 0, 784), 1.0)
     ms(R("d97", 0, 784, 97), 0.0)
-    const(R("d8", 0, 224), 8.0)
-    ms(R("d8", 0, 224, 8), 0.0)
-    const(R("fill", 0, 224), -8192.0 * SC)
-    const(R("fill", 224, 448), -8192.0 * SC)
-    const(R("fill", 448, 672), 8192.0 * SC)
-    const(R("zr", 0, 64), 0.0)
-    act(R("cw", 0, 1024), R("vv", 0, 1024), scale=0.0)
-    const(R("hh", 0, 64), 0.0)
+    ts(R("ge", 0, 128), xr(128), pc[4], ALU.is_ge)
+    ts(R("ge", 128, 256), xr(128), P_, ALU.is_ge)
+    ts(R("ge", 256, 384), xr(128), pc[5], ALU.is_gt)
+    tt(R("ut", 0, 128), R("ge", 0, 128), R("ge", 128, 256), ALU.subtract)
+    tt(R("lt", 0, 128), R("ge", 128, 256), R("ge", 256, 384), ALU.subtract)
+    act(pc[7], pc[5], scale=-1.0, bias=0.5)
+    act(R("ge", 0, 144), xr(144), AF.Abs, scale=1.0, bias=pc[7])
+    ts(R("gh", 0, 144), R("ge", 0, 144), 1.0, ALU.is_lt)
+    const(R("d4", 0, 224), 8.0)
+    const(R("d4", 0, 224, 4), 0.0)
+    const(R("t15", 0, 224), 15.0)
+    const(R("t24", 0, 96), -K / 64.0)
+    tag[0] = "late"
+    cp(R("b16", 192, 768), R("bti", 192, 768))
+    act(pc[8], P16, scale=224.0, bias=1.0)
+    act(pc[9], pc[8], scale=-1.0)
+    act(R("pt", 0, 224), xr(224), scale=1.0, bias=pc[8])
+    act(R("pt", 224, 448), xr(224), scale=-1.0, bias=pc[9])
+    ts(R("ee", 0, 128), R("x16", 0, 128), P16, ALU.is_equal)
+    act(pc[10], P16, scale=96.0)
+    tt(R("wk", 864, 960), xr(96), R("x16", 0, 96), ALU.subtract)
+    act(R("vt", 0, 96), R("wk", 864, 960), scale=1.0, bias=pc[10])
+    act(R("vt", 96, 192), R("x16", 0, 96), scale=1.0, bias=1.0)
+    const(R("vt", 192, 288), V0 - 1.0)
+    for a in (0, 512):
+        const(R("zr", a, a + 512), 0.0)
+    for a in (0, 768):
+        dma("sp", R("vb", a, a + 768), R("zr", 0, 768), 196)
+    for i in range(3):
+        dma("sp", row("vb", 0, K, i), R("vt", 96 * i, 96 * i + 96), 25)
+        dma("sp", R("cw", K + 1024 * i, K + 1024 * i + 1024), R("zr", 0, 1024), 262)
+    act(pc[11], P16, scale=1.0, bias=64.0 * KH + 1 - K)
+    act(R("dj", 0, 96), xr(96), scale=16.0, bias=pc[11])
+    act(pc[12], P16, scale=1.0, bias=1.0)
+    act(R("kk", 0, 32), R("x16", 0, 128, 4), scale=4.0, bias=pc[12])
+    act(pc[13], P2, scale=224.0, bias=64.0)
+    act(R("cs", 1344, 1568), xr(224), scale=1.0, bias=1.0)
+    act(R("cs", 1568, 1792), xr(224), scale=0.0, bias=pc[13])
+    ts(pc[14], P16, 12.0, ALU.is_equal)
     for t in range(2):
-        const(R("cg%d" % t, 0, 16), 0.0)
-    for t in range(3):
-        const(R("fl", 224 * t + 28 * r, 224 * t + 28 * r + 28), 0.0)
-    refill()
-    dma("sp", R("h0s", 0, M), T.e0[:, r * M:(r + 1) * M], 114)
-    s = bcast(R("h0s", 0, M), R("h0d", r, r + 1), "ha", 11.0)
-    arrive([R("h0d", q, q + 1) for q in range(N) if q != r], "ha", allin, [s])
-    dma("pool", R("big", 0, W), T.e0[:], 1835, [R("tb", 0, W)])
-    for k in range(N):
-        q = (r + k) % N
-        dma("pool", R("big", W + M * q, W + M * q + M), R("h0d", q, q + 1) if k else T.e0[:, r * M:(r + 1) * M], 229, [R("tb", 0, W)])
-    dma("pool", R("hh", 64, 512), T.e0[:, r * M:(r + 1) * M], 229, [R("big", W, 2 * W)])
-    dma("pool", R("base", 0, W), T.e0[:], 1835, [R("big", W, 2 * W)])
+        act(R("cg%d" % t, 0, 64), xr(64), scale=pc[14], bias=pc[14])
+    if "b" in opt["home"]:
+        const(R("hb", 0, 512), 0.0)
+    for t in range(RO - 1):
+        const(R("bg", O - KP * (t + 1), O - KP * (t + 1) + 64), 0.0)
     top16 = ("top", 16)
     dma("sp", R("tgb", 0, 768, p=top16), T.tg[:], 25)
     act(R("tgs", 0, 768, p=top16), R("tgb", 0, 768, p=top16), scale=-64.0)
@@ -327,93 +335,77 @@ def plan(r, T, topo, sc, opt):
     def wk(i):
         return R("wk", 96 * i, 96 * i + 96)
 
-    def qw(i):
-        return R("qw", 32 * i, 32 * i + 32)
-
     def prepare(t):
         tag[0] = "prep%d" % t
         a, m, b = 192 * t, 192 * t + 96, 192 * t + 192
-        cp(R("b16", a, b), R("bti", a, b))
-        ts(R("hq", 0, 192), R("bti", a, b), 1.0 / M, ALU.mult, 0.5 + 0.5 / M, ALU.add)
-        cp(R("hi", a, b), R("hq", 0, 192))
-        tt(R("dn", 96 * t, 96 * t + 96), R("bti", m, b), R("bti", a, m), ALU.subtract)
-        tt(R("dh", 96 * t, 96 * t + 96), R("hi", m, b), R("hi", a, m), ALU.subtract)
+        tt(R("dd", a, b, 2), R("bti", m, b), R("bti", a, m), ALU.subtract)
+        cp(R("dd", a + 1, b, 2), R("bti", a, m))
 
     def control(t):
         cg = "cg%d" % (t % 2)
         a0 = 192 * t
-        c0 = W + K * t
         tag[0] = "cg%d" % t
+        s1, s2 = R("p_n", 320, 416), R("p_s", 0, 96)
         for eng, a, b in opt["cg"]:
-            move(eng, R(cg, 16 + 16 * a, 16 + 16 * b), R("tb", 0, W, ind=R("b16", a0 + a, a0 + b)))
-        for a in (0, 64, 128):
-            wrap(R("p_s", a, a + 64), "gs", 0, cg, 16 + 16 * a, 64)
-        sa, sel, mx, th, h1, tn, nm, gr, of1, p1, pos = [wk(i) for i in range(11)]
-        w1, w2, w3, of2, ra, d1, d2, rt, g4, z, xl, du = [wk(i) for i in range(11, 23)]
-        cp(sa, R("p_s", 0, 96))
-        tt(sel, R("p_s", 96, 192), sa, ALU.is_gt)
-        tt(mx, R("p_s", 96, 192), sa, ALU.max)
-        tt(tn, sel, R("dn", 96 * t, 96 * t + 96), ALU.mult)
-        ts(du, mx, 4.0, ALU.is_ge, float(W), ALU.mult)
-        tt(nm, tn, R("bti", a0, a0 + 96), ALU.add)
-        tt(of1, du, nm, ALU.add)
-        cp(R("o16", 96 * t, 96 * t + 96), of1)
+            move(eng, R(cg, 64 + 16 * a, 64 + 16 * b), R("tb", 0, W, ind=R("b16", a0 + a, a0 + b)))
+        wrap(s1, "gs", 0, cg, 64, 96)
+        wrap(s2, "gs", 0, cg, 64 + K, 96)
+        sa, mx, key, u, w1, w3, of2, m1, m2 = [wk(i) for i in range(9)]
+        sel, nm = R("sl", a0 + 1, a0 + 192, 2), R("nm", 1, 192, 2)
+        nd2, kh = R("nd", 0, 96), R("kh", 0, 96)
+        act(sa, s1)
+        tt(sel, s2, sa, ALU.is_gt)
+        scan(R("nm", 0, 192), R("sl", a0, a0 + 192), R("dd", a0, a0 + 192))
+        cp(R("o16", 96 * t, 96 * t + 96), nm)
         tag[0] = "cnt%d" % t
-        tt(th, sel, R("dh", 96 * t, 96 * t + 96), ALU.mult)
-        ts(R("nd", 0, 96), mx, 4.0, ALU.is_lt, 128.0, ALU.mult)
-        tt(h1, th, R("hi", a0, a0 + 96), ALU.add)
-        tt(R("kh", 0, 96), h1, R("nd", 0, 96), ALU.add)
+        tt(mx, s2, sa, ALU.max)
+        ts(nd2, mx, 4.0, ALU.is_lt, 64.0 * M, ALU.mult)
+        tt(key, nm, nd2, ALU.add)
+        ts(kh, key, 1.0 / M, ALU.mult, KH - 0.5 + 0.5 / M, ALU.add)
         for h in range(8):
-            ts(R("mm", 97 * h + 1, 97 * h + 97), R("kh", 0, 96), float(h + 1), ALU.is_equal)
+            ts(R("mm", 97 * h + 1, 97 * h + 97), kh, float(KH + h), ALU.is_equal)
         scan(R("sc", 0, 784), R("d97", 0, 784), R("mm", 0, 784))
         for i, pb in enumerate(("p_c0", "p_c1")):
             x = 388 * i
-            mms([(R(pb, 0, 388), R("lt", 0, 128), R("sc", x + 1, x + 389), True, False),
-                 (R(pb, 0, 388), R("ut", 0, 128), R("sc", x, x + 388), False, True)])
-        cn = R("p_s", 192, 288)
+            mms([(R(pb, 0, 388), R("lt", 0, 128), R("sc", x + 1, x + 389)), (R(pb, 0, 388), R("ut", 0, 128), R("sc", x, x + 388))])
+        cn, p1, p2 = R("p_s", 96, 192), R("p_s", 192, 288), R("p_l", 0, 96)
+
+        def ranks(o, hs):
+            return [(o, I1, R("zz", 97 * h, 97 * h + 96)) for h in hs]
         for i, pb in enumerate(("p_c0", "p_c1")):
             x = 388 * i
             tt(R("zz", x, x + 388), R(pb, 0, 388), R("mm", x + 1, x + 389), ALU.mult)
-            if t < RO - 1:
-                if opt["ii"] == "a":
-                    act(R("ii", x, x + 388), R(pb, 0, 388), AF.Sign, scale=-1.0, bias=CAP + 0.5)
-                else:
-                    ts(R("ii", x, x + 388), R(pb, 0, 388), float(CAP), ALU.is_le)
-            lst = [(cn, R("idn", 0, 128), R("zz", x + 97 * h, x + 97 * h + 96), False, i == 1 and h == 3) for h in range(4)]
-            if i == 0:
-                lst = [(cn, R("idn", 0, 128), R("nd", 0, 96), True, False)] + lst
-            mms(lst)
-        ts(gr, cn, float(CAP), ALU.is_le, float(W), ALU.mult)
-        if t > 0:
-            lin(0, p1, h1, 64.0, -65.0)
-            lin(0, w2, sel, 512.0, W)
-            tt(pos, cn, p1, ALU.add)
-        if t < RO - 1:
-            mms([(R("p_s", 288, 384), R("gh", 14 - 2 * h, 142 - 2 * h), R("ii", 97 * h, 97 * h + 96), h == 0, h == 7) for h in range(8)])
-            total(R("tau", 0, 1), R("p_s", 288, 384))
-            if opt["ii"] == "a":
-                ts(R("tau", 1, 2), R("tau", 0, 1), K + 1.0, ALU.add, SC / 2, ALU.mult)
-            else:
-                ts(R("tau", 1, 2), R("tau", 0, 1), 0.5, ALU.add, SC, ALU.mult)
+            lst = ([(cn, I1, nd2)] if i == 0 else []) + ranks(cn, range(4 * i, 4 * i + 4))
+            mms([q + (i == 0 and k == 0, i == 1 and k == 3) for k, q in enumerate(lst)])
         if t == 0:
-            tt(xl, nm, gr, ALU.add)
-            cp(R("xl", 0, 96), xl)
-            return
-        tt(w1, pos, gr, ALU.subtract)
-        tt(w3, w1, w2, ALU.add)
-        tt(of2, w3, R("dj", 0, 96), ALU.min)
-        cp(R("c16", 96 * t, 96 * t + 96), of2)
-        tag[0] = "xl%d" % t
-        for a in (0, 96):
-            wrap(R("p_l", a, a + 96), "gs", 144, cg, 16 + 16 * a, 96)
-        lin(1, ra, R("p_l", 0, 96), 1.0, 0.0)
-        tt(d1, R("p_l", 96, 192), ra, ALU.subtract)
-        tt(d2, d1, sel, ALU.mult)
-        tt(rt, ra, d2, ALU.add)
-        lin(1, g4, gr, 4.0, c0 - 4 * W)
-        tt(z, pos, g4, ALU.add)
-        tt(xl, rt, z, ALU.max)
-        cp(R("xl", 96 * t, 96 * t + 96), xl)
+            ts(u, cn, CAP + 0.5, ALU.is_le, float(W), ALU.mult)
+            tt(w1, nm, u, ALU.add)
+            cp(R("xl", 0, 96), w1)
+        else:
+            mms([(p2, I64, kh), (p2, I512, sel)] + ranks(p2, range(8)))
+            ts(u, cn, CAP + 0.5, ALU.is_gt, 32768.0, ALU.mult)
+            tt(w3, p2, u, ALU.subtract)
+            tt(of2, w3, R("dj", 0, 96), ALU.max)
+            ts(R("c16", 96 * t, 96 * t + 96), of2, K - 1.0 - 64 * KH, ALU.add)
+        if t < RO - 1:
+            tag[0] = "tau%d" % t
+            for i, pb in enumerate(("p_c0", "p_c1")):
+                act(R("ii", 388 * i, 388 * i + 388), R(pb, 0, 388), AF.Sign, scale=-1.0, bias=CAP + 0.5)
+            mms([(R("p_n", 224, 320), R("gh", 14 - 2 * h, 142 - 2 * h), R("ii", 97 * h, 97 * h + 96)) for h in range(8)])
+            half = R("tau", 96, 97)
+            act(R("tau", 0, 96), R("p_n", 224, 320), scale=SC / 4, bias=(K / 4 + (V0 - 0.5) / 2) * SC / 96, total=half)
+            act(R("p_n", 0, 224), R("sg", 224, 448), scale=half, bias=half)
+        if t > 0:
+            tag[0] = "xl%d" % t
+            a1, a2 = R("p_l", 96, 192), R("p_l", 192, 288)
+            t24 = R("t24", 0, 96)
+            mms([(p1, I64, kh)] + [(p1, I64, t24)] * (RO - t) + ranks(p1, range(8)))
+            wrap(a1, "gs", 144, cg, 64, 96, [(a1, INEG, sel)])
+            wrap(a2, "gs", 144, cg, 64 + K, 96, [(a2, IBIG, sel), (a2, I512, t24)])
+            tt(w1, p1, u, ALU.subtract)
+            tt(m1, a1, w1, ALU.max)
+            tt(m2, a2, m1, ALU.max)
+            ts(R("xl", 96 * t, 96 * t + 96), m2, -1.0, ALU.add)
 
     def spread(engs, win, lst, t):
         n = 96 // len(engs)
@@ -427,85 +419,111 @@ def plan(r, T, topo, sc, opt):
     def names(t):
         last = t == RO - 1
         tag[0] = "ns%d" % t
-        f0 = 224 * t
-        nfl, ta = R("p_c0", 0, 224), R("p_c0", 224, 448)
-        spread(opt["ns"][t], R("wn", 0, 2 * W), "o16", t)
+        f0 = 448 * t
+        v0, v1 = R("cab", 0, 224), R("cab", 224, 448)
+        spread(opt["ns"][t], R("wn", 0, W), "o16", t)
         if not last:
-            dma("sp", R("cab", 448, 672), row("wn", W, 2 * W, 1), 114)
-        dma("sp", R("cab", 224, 448), row("wn", W, 2 * W, 0), 114)
-        dma("sp", R("cab", 0, 224), row("wn", 0, W, 0), 114)
+            dma("sp", v1, row("wn", 0, W, 1), 114)
+        dma("sp", v0, row("wn", 0, W, 0), 114)
         if not last:
             refill()
-            ts(nfl, R("cab", 448, 672), R("tau", 1, 2), ALU.is_gt)
-            scan(R("pk", 0, 224), R("d8", 0, 224), nfl)
-            cp(R("fs", 28 * t, 28 * t + 28), R("pk", 7, 224, 8))
-            s = bcast(R("fs", 28 * t, 28 * t + 28), R("fl", f0 + 28 * r, f0 + 28 * r + 28), "fa%d" % t)
-            arrive([R("fl", f0 + 28 * q, f0 + 28 * q + 28) for q in range(N) if q != r], "fa%d" % t, allin, [s])
+            tt(ng, v1, R("p_n", 0, 224), ALU.is_gt)
+            scan(R("pk", 0, 224), R("d4", 0, 224), ng)
+            fs = R("fs", 56 * t, 56 * t + 56)
+            cp(fs, R("pk", 3, 224, 4))
+            s = bcast(fs, R("fl", f0 + 56 * r, f0 + 56 * r + 56), "fa%d" % t)
+            arrive([R("fl", f0 + 56 * q, f0 + 56 * q + 56) for q in others], "fa%d" % t, allin, [s])
+            act(R("sg", 0, 224), v0, AF.Sign)
+            mms([(yy, I1, age), (yy, IHALF, R("sg", 0, 224)), (yy, IHALF, R("t15", 0, 224))])
         tag[0] = "ptr%d" % t
-        tt(R("cab", 0, 224), R("cab", 0, 224), R("cab", 224, 448), ALU.max)
         n = 224 if last else 448
+        za, zb, z = R("p_c0", 0, 224), R("p_c0", 224, 448), R("p_c0", 0, n)
+        ca, cb = R("ct", f0, f0 + 224), R("ct", f0 + 224, f0 + 448)
+        const(ca, (W + K * t + 1 - V0) / 64.0)
+        mms([(za, FSC, v0), (za, I64, ca)])
         if not last:
-            ts(ta, R("cab", 0, 224), 0.0, ALU.is_gt, float(N - 1), ALU.add)
-            tt(R("p_c1", 0, 224), R("am", 0, 224), ta, ALU.add)
-            tt(R("p_c1", 224, 448), R("wc", 0, 224), nfl, ALU.mult)
-        act(R("yy", 0, 224), R("cab", 0, 224), scale=1.0 / SC, bias=MAG + W - 1 + K * t)
-        act(R("yz", 0, 224), R("yy", 0, 224), scale=1.0, bias=-MAG)
-        tt(R("p_x", 0, 224), R("yz", 0, 224), R("p_x", 0, 224), ALU.max)
-        if not last:
-            ts(R("gf", 0, 224), R("cab", 448, 672), R("tau", 1, 2), ALU.is_le)
-            tt(R("yz", 224, 448), R("gf", 0, 224), R("p_x", 0, 224), ALU.mult)
-            tt(R("p_x", 224, 448), R("yz", 224, 448), R("p_x", 224, 448), ALU.max)
-        pointers(n)
+            const(cb, (KP * (t + 1) - 65 + V0) / 64.0)
+            mms([(zb, FNEG, v1), (zb, I64, cb), (zb, INEG, ng)])
+        tt(R("pt", 0, n), z, R("pt", 0, n), ALU.max)
+        act(R("cs", 448, 448 + n), R("pt", 0, n))
+        mms([(z, FNEG, R("pt", 0, n)), (z, ISC, R("cs", 448, 448 + n))])
+        for i in range(n // 224):
+            dma("sp", row("tb", 0, W, 4 + 4 * i), R("cs", 448 + 224 * i, 672 + 224 * i), 57)
+        act(R("cs", 896, 896 + n), z, scale=-SC)
+        for i in range(n // 224):
+            dma("sp", row("tb", 0, W, 5 + 4 * i), R("cs", 896 + 224 * i, 1120 + 224 * i), 57)
+        if t == 0:
+            dma("sp", row("tb", 0, W, 12), R("cs", 1344, 1568), 57)
+            dma("sp", row("tb", 0, W, 13), R("cs", 1568, 1792), 57)
         tag[0] = "age%d" % t
         if not last:
-            tt(R("s1", 0, 112), R("fl", f0, f0 + 112), R("fl", f0 + 112, f0 + 224), ALU.add)
-            tt(R("s2", 0, 56), R("s1", 0, 56), R("s1", 56, 112), ALU.add)
-            tt(R("s3", 0, 28), R("s2", 0, 28), R("s2", 28, 56), ALU.add)
-            for b in range(8):
-                ts(R("dc", b, 224, 8), R("s3", 0, 28), 3 * (7 - b), ALU.logical_shift_right, 7, ALU.bitwise_and)
-            tt(R("tt", 0, 224), R("p_c1", 0, 224), R("dc", 0, 224), ALU.subtract)
-            score(R("p_c1", 224, 448), R("tt", 0, 224))
-            tt(R("am", 0, 224), R("tt", 0, 224), nfl, ALU.mult)
+            mms([(R("p_c1", 448, 504), R("i16", 0, 128), R("fl", f0 + 56 * q, f0 + 56 * q + 56)) for q in others])
+            cp(R("s3", 0, 56), R("p_c1", 448, 504))
+            for b in range(4):
+                ts(R("dc", b, 224, 4), R("s3", 0, 56), 3 * (3 - b), ALU.logical_shift_right, 7, ALU.bitwise_and)
+            tt(yy, yy, R("dc", 0, 224), ALU.subtract)
+            tt(yy, yy, ng, ALU.mult)
+            score()
+            tag[0] = "od%d" % t
+            if t < RO - 2:
+                overdue()
+            if t == 0:
+                for x, a in ((R("bg", O, O + W), T.e0[:]), (R("hh", 64, 512), T.e0[:, r * M:(r + 1) * M])):
+                    dma("pool", x, a, cnt(x) // 2, [row("tb", 0, W, 1), row("tb", 0, W, 2)])
         else:
-            wrap(R("p_c1", 0, 224), "gs", 144, "tb", 0, 224)
-            cp(R("y16", 0, 224), R("p_c1", 0, 224))
+            wrap(R("p_n", 0, 224), "gs", 144, "tb", 0, 224)
+            ts(R("y16", 0, 224), R("p_n", 0, 224), -1.0, ALU.add)
 
     def lists(t):
         cg = "cg%d" % (t % 2)
         tag[0] = "ls%d" % t
-        spread(opt["cs"][t], R("cw", 0, 1024 + K), "c16", t)
-        wrap(R("p_l", 192, 256), "gq", 0, "cw", 0, 64)
-        if t < RO - 1:
-            dma("sp", row("cw", 0, 1024, 0), R("zr", 0, 64), 32)
-        ts(qw(0), R("p_l", 224, 256), 0.5, ALU.is_gt, float(K), ALU.mult)
-        tt(qw(1), R("p_l", 192, 224), qw(0), ALU.add)
-        tt(qw(2), R("p_l", 224, 256), qw(1), ALU.add)
-        ts(qw(3), qw(2), MAG + 15.0, ALU.add)
-        ts(R("q16", 32 * t, 32 * t + 32), qw(3), -MAG, ALU.add)
-        act(R("lg", 0, 512), R(cg, 0, 16 + 2 * K, ind=R("q16", 32 * t, 32 * t + 32)))
-        wrap(R("p_l", 256, 288), "gs", 144, "lg", 0, 32)
-        wrap(R("p_l", 288, 320), "gs", 288, "lg", 0, 32)
-        wrap(R("p_l", 320, 352), "gs", 432, "lg", 0, 32)
+        w0, n = 1024 * (t - 1), 96 // opt["cs"][t]
+        for a in range(0, 96, n):
+            cp(R("cw", w0, w0 + K + 1024, ind=R("c16", 96 * t + a, 96 * t + a + n)), R("vb", 16 * a, 16 * (a + n)))
+        wrap(R("p_l", 288, 352), "gs", 0, "cw", w0 + K, 64, [(R("p_l", 288, 320), I64, R("t24", 0, 32))])
+        tt(R("qw", 0, 32), R("p_l", 288, 320), R("kk", 0, 32), ALU.max)
+        tt(R("qw", 32, 64), R("p_l", 320, 352), R("qw", 0, 32), ALU.max)
+        ts(R("q16", 32 * t, 32 * t + 32), R("qw", 32, 64), -1.0, ALU.add)
+        act(R("lg", 0, 512), R(cg, 0, 64 + 2 * K, ind=R("q16", 32 * t, 32 * t + 32)))
+        m0 = 128 * t
+        wrap(R("p_l", 384, 416), "gs", 288, "lg", 0, 32)
+        ts(R("ml", m0 + 64, m0 + 96), R("p_l", 384, 416), -1.0, ALU.mult, KP * t - 1.0, ALU.add)
+        wrap(R("p_l", 448, 480), "gs", 144, "lg", 0, 32)
+        wrap(R("p_l", 416, 448), "gs", 432, "lg", 0, 32)
+        ts(R("ml", m0, m0 + 64), R("p_l", 416, 480), -1.0, ALU.add)
+        if opt["step"][t - 1] == "q":
+            c = float(W + K * (t - 1))
+            ts(R("ml", m0 + 96, m0 + 128), R("p_l", 448, 480), c, ALU.max, 63.0 - c, ALU.add)
         l0 = 256 * t
-        mine = R("ll", l0 + 32 * r, l0 + 32 * r + 32)
-        cp(R("rb16", 64 * t, 64 * t + 64), R("p_l", 256, 320))
-        tt(qw(4), R("p_l", 320, 352), R("kk", 0, 32), ALU.max)
-        cp(mine, qw(4))
-        s = bcast(mine, mine, "la%d" % t)
-        arrive([R("ll", l0 + 32 * q, l0 + 32 * q + 32) for q in range(N) if q != r], "la%d" % t, allin, [s])
+        s = bcast(R("ml", m0, m0 + 32), R("ll", l0 + 32 * r, l0 + 32 * r + 32), "la%d" % t)
+        arrive([R("ll", l0 + 32 * q, l0 + 32 * q + 32) for q in others], "la%d" % t, allin, [s])
+
+    def addup(t):
+        x0, c0 = O - KP * (t + 1) + 64, O + W + K * t
+        dma("pool", R("bg", c0, c0 + K), R("bg", x0, x0 + K), 1570, adds=True)
 
     def data(t):
-        c0 = W + K * t
+        x0, c0, m0 = O - KP * (t + 1) + 64, O + W + K * t, 128 * t
 
-        def home(s):
-            return R("hh", 0, 512, ind=R("ll", 256 * t + 32 * s + 4 * r, 256 * t + 32 * s + 4 * r + 4))
+        def home(s, part="hh"):
+            return R(part, 0, 512, ind=R("ml", m0 + 4 * r, m0 + 4 * r + 4) if s == r else
+                     R("ll", 256 * t + 32 * s + 4 * r, 256 * t + 32 * s + 4 * r + 4))
         tag[0] = "hm%d" % t
         if t > 0:
             p0 = 512 * (t - 1)
-            act(R("bs", 0, 512), R("base", 0, c0, ind=R("rb16", 64 * t + 32, 64 * t + 64)))
-            tt(R("psn", p0, p0 + 512), R("big", 0, c0, ind=R("rb16", 64 * t, 64 * t + 32)), R("bs", 0, 512), ALU.subtract)
+            act(R("bs", 0, 512), R("bg", O - KP * t, O + W, ind=R("ml", m0 + 64, m0 + 96)))
+            now = R("bg", O, c0, ind=R("ml", m0 + 32, m0 + 64))
+            if opt["step"][t - 1] == "q":
+                tt(R("bs", 512, 1024), R("bg", O - KP * t, O - KP * (t - 1), ind=R("ml", m0 + 96, m0 + 128)), R("bs", 0, 512), ALU.subtract)
+                tt(R("psn", p0, p0 + 512), now, R("bs", 512, 1024), ALU.add)
+            else:
+                tt(R("psn", p0, p0 + 512), now, R("bs", 0, 512), ALU.subtract)
             ss = [send([(R("psn", p0 + 64 * d, p0 + 64 * d + 64), [(d, R("pl", p0 + 64 * r, p0 + 64 * r + 64))], es, "pa%d" % r)
-                        for d, es in c], lat) for c, lat in ((c1, 3.6), (c2, 3.8))]
+                        for d, es in c], lat) for c, lat in ((c1, 3.4), (c2, 3.8))]
+            if opt["step"][t - 1] == "q":
+                i = len(ops)
+                addup(t - 1)
+                ops[i]["after"] = ss
             order = [r] + sorted(into, key=lambda s: (s not in near, into[s][0], (s - r) % N))
             for i, s in enumerate(order):
                 if s == r:
@@ -514,42 +532,55 @@ def plan(r, T, topo, sc, opt):
                     src = R("pl", p0 + 64 * s, p0 + 64 * s + 64)
                     arrive([src], "pa%d" % s, t * into[s][1], [ss[0 if i <= 5 else 1]])
                 tm = R("tm", 64 * (i % 2), 64 * (i % 2) + 64)
-                if opt["home"][t] == "a":
-                    act(tm, home(s))
-                    tt(home(s), tm, src, ALU.add)
+                part = "hb" if "b" in opt["home"] and i % 2 else "hh"
+                if "a" in opt["home"]:
+                    act(tm, home(s, part))
+                    tt(home(s, part), tm, src, ALU.add)
                 else:
-                    tt(tm, home(s), src, ALU.add)
-                    cp(home(s), tm)
-        a0 = 512 * (t - 1)
-        for i, d in enumerate([d for d, es in c1 + c2] + [r] if t else []):
-            o = R("big", c0 + 64 * r, c0 + 64 * r + 64) if d == r else R("asn", a0 + 64 * d, a0 + 64 * d + 64)
-            move("act" if opt["ans"][t][i] == "a" else "dve", o, home(d))
-        if t > 0:
-            ss = [send([(R("asn", a0 + 64 * d, a0 + 64 * d + 64), [(d, R("big", c0 + 64 * r, c0 + 64 * r + 64))], es, "aa%d" % t)
-                        for d, es in c], lat) for c, lat in ((c1, 3.6), (c2, 3.8))]
-            arrive([R("big", c0 + 64 * q, c0 + 64 * q + 64) for q in range(N) if q != r], "aa%d" % t, sum(v[1] for v in into.values()), ss)
-        if t == RO - 1:
+                    tt(tm, home(s, part), src, ALU.add)
+                    cp(home(s, part), tm)
+            for i, d in enumerate([d for d, es in c1 + c2] + [r]):
+                o = R("bg", c0 + 64 * r, c0 + 64 * r + 64) if d == r else R("asn", p0 + 64 * d, p0 + 64 * d + 64)
+                if "b" in opt["home"]:
+                    act(R("tn", 64 * i, 64 * i + 64), home(d))
+                    tt(o, home(d, "hb"), R("tn", 64 * i, 64 * i + 64), ALU.add)
+                else:
+                    move(opt["ans"][t][i], o, home(d))
+            ss = [send([(R("asn", p0 + 64 * d, p0 + 64 * d + 64), [(d, R("bg", c0 + 64 * r, c0 + 64 * r + 64))], es, "aa%d" % t)
+                        for d, es in c], lat) for c, lat in ((c1, 3.4), (c2, 3.8))]
+            arrive([R("bg", c0 + 64 * q, c0 + 64 * q + 64) for q in others], "aa%d" % t, sum(v[1] for v in into.values()), ss)
+        if t == RO - 1 and "b" in opt["home"]:
+            tt(R("ho", 0, M), R("hh", 64, 512), R("hb", 64, 512), ALU.add)
+            dma("sp", T.yh[:], R("ho", 0, M), 229)
+        elif t == RO - 1:
             dma("sp", T.yh[:], R("hh", 64, 512), 229)
         tag[0] = "st%d" % t
         pp = R("p_p", 0, 192)
         mms([(pp, R("ee", 0, 128, p=top16), R("tgs", 192 * t, 192 * t + 192, p=top16), True, False)])
 
         def xg(a, b):
-            return R("big", 0, c0 + 512 if t else 2 * W, ind=R("xl", 96 * t + a, 96 * t + b))
+            lst = R("xl", 96 * t + a, 96 * t + b)
+            return R("bg", O, c0 + 512, ind=lst) if t else R("eb", 0, 2 * W, ind=lst)
         for k in range(4):
-            xa = R("base", c0 + 192 * k, c0 + 192 * k + 192)
+            xa = R("bg", x0 + 192 * k, x0 + 192 * k + 192)
             act(xa, xg(12 * k, 12 * k + 12))
             tt(R("pr", 192 * k, 192 * k + 192), xg(48 + 12 * k, 60 + 12 * k), xa, ALU.mult)
             mms([(pp, R("ee", 0, 128), R("pr", 192 * k, 192 * k + 192), False, k == 3)])
-        act(R("base", c0 + 768, c0 + 1152), xg(48, 72))
-        act(R("base", c0 + 1152, c0 + 1536), xg(72, 96))
+        move(opt["x2"][0], R("bg", x0 + 768, x0 + 1152), xg(48, 72))
+        move(opt["x2"][1], R("bg", x0 + 1152, x0 + 1536), xg(72, 96))
         act(R("es", 0, 192), pp, AF.Tanh, scale=-1.0 / 64, bias=0.0)
         act(R("p_p", 0, 192), R("es", 0, 192), scale=1.0 / 64)
         act(R("p_p", 192, 384), R("es", 0, 192), scale=1.0 / 64)
-        for i, (own, par) in enumerate(((768, 0), (1152, 384), (0, 768), (384, 1152))):
-            tb = R("p_t%d" % (i % 2), 0, 384)
-            tt(tb, R("base", c0 + par, c0 + par + 384), R("p_p", 0, 384), ALU.mult)
-            tt(R("big", c0 + own, c0 + own + 384), R("base", c0 + own, c0 + own + 384), tb, ALU.add)
+        for i, (mine, par) in enumerate(((768, 0), (1152, 384), (0, 768), (384, 1152))):
+            out = R("bg", c0 + mine, c0 + mine + 384)
+            if opt["step"][t] == "d":
+                tb = R("p_t%d" % (i % 2), 0, 384)
+                tt(tb, R("bg", x0 + par, x0 + par + 384), R("p_p", 0, 384), ALU.mult)
+                tt(out, R("bg", x0 + mine, x0 + mine + 384), tb, ALU.add)
+            else:
+                tt(out, R("bg", x0 + par, x0 + par + 384), R("p_p", 0, 384), ALU.mult)
+        if opt["step"][t] == "m":
+            addup(t)
 
     for t in range(RO):
         prepare(t)
@@ -563,10 +594,11 @@ def plan(r, T, topo, sc, opt):
             lists(t)
             names(t)
         data(t)
+    tag[0] = "fin"
     for i in range(8):
         a = M * i
-        move("dve" if opt["fin"][i] == "d" else "act", R("base", a, a + M), R("big", 0, W + RO * K, ind=R("y16", 28 * i, 28 * i + 28)))
-        dma("sp" if i % 2 == 0 else "pool", T.yr[:, a:a + M], R("base", a, a + M), 229)
+        move(opt["fin"][i], R("bg", KP + a, KP + a + M), R("bg", O, O + W + RO * K, ind=R("y16", 28 * i, 28 * i + 28)))
+        dma("sp" if i % 2 == 0 else "pool", T.yr[:, a:a + M], R("bg", KP + a, KP + a + M), 229)
     return ops, sent[0]
 
 
@@ -588,51 +620,88 @@ def depends(ops):
             for j, y, v in seen.get(x[1], ()):
                 if (x[1] in PSUM and ops[j]["eng"] != o["eng"]) or ((w or v) and clash(x, y)):
                     d.add(j)
+        for x in o["bh"]:
+            d.update(j for j, y, v in seen.get(x[1], ()) if v and clash(x, y))
         for x, w in mine:
             seen.setdefault(x[1], []).append((i, x, w))
         deps.append(d)
     return deps
 
 
-def schedule(ops, deps, opt):
+def schedule(ops, deps, sc, opt, others=()):
     n = len(ops)
-    pre = [set(deps[i]) | set(ops[i]["after"]) for i in range(n)]
+    eng = [o["eng"] for o in ops]
+    cost = [o["cost"] for o in ops]
+    pre = [[] for i in range(n)]
     succ = [[] for i in range(n)]
     for i in range(n):
-        for j in pre[i]:
-            succ[j].append(i)
-    tail = [0.0] * n
-    for i in range(n - 1, -1, -1):
-        tail[i] = ops[i]["cost"] + ops[i]["lat"] + 0.08 + max([tail[j] for j in succ[i]] + [0.0])
-    tail = [tail[i] + opt["bias"].get(ops[i]["tag"], 0.0) for i in range(n)]
-    left = [len(p) for p in pre]
-    ready = [0.0] * n
-    free = {}
-    pool = [i for i in range(n) if left[i] == 0]
-    order = []
-    times = {}
-    while pool:
-        best = None
-        for e in sorted(set(ops[i]["eng"] for i in pool)):
-            c = [i for i in pool if ops[i]["eng"] == e]
-            t0 = max(free.get(e, 0.0), min(ready[i] for i in c))
-            i = max([i for i in c if ready[i] <= t0 + opt["look"]], key=lambda i: (tail[i] - max(0.0, ready[i] - t0), -i))
-            if best is None or t0 < best[0]:
-                best = (t0, max(free.get(e, 0.0), ready[i]), i)
-        t0, s, i = best
-        pool.remove(i)
-        e = ops[i]["eng"]
-        if e != "net":
-            free[e] = s + ops[i]["cost"]
-        end = s + ops[i]["cost"] + ops[i]["lat"]
-        times[i] = (s, end)
-        order.append(i)
-        for j in succ[i]:
-            ready[j] = max(ready[j], end + 0.08)
-            left[j] -= 1
-            if left[j] == 0:
-                pool.append(j)
-    return order, times
+        for j in set(deps[i]) | set(ops[i]["after"]):
+            lag = 0.0 if eng[i] == eng[j] and (eng[i] == "pe" or j not in deps[i]) else ops[j]["lat"] + sc["gap"]
+            pre[i].append((j, cost[j] + lag))
+            succ[j].append((i, cost[i] + lag))
+
+    def place(rank, links, first):
+        start = [0.0] * n
+        busy = {e: [] for e in eng}
+        for i in sorted(range(n), key=rank):
+            s = first[i]
+            for j, d in links[i]:
+                if start[j] + d > s:
+                    s = start[j] + d
+            if eng[i] != "net":
+                line = busy[eng[i]]
+                k = len(line)
+                while k and line[k - 1][1] > s:
+                    k -= 1
+                while k < len(line) and line[k][0] < s + cost[i] - 1e-9:
+                    s = line[k][1]
+                    k += 1
+                line.insert(k, (s, s + cost[i]))
+            start[i] = s
+        return start
+    zero = [0.0] * n
+    lat = [o["lat"] for o in ops]
+
+    def passes(weight):
+        back = [0.0] * n
+        for i in range(n - 1, -1, -1):
+            back[i] = max([back[j] + d for j, d in succ[i]] + [lat[i]]) + weight[ops[i]["tag"]] * cost[i]
+        start = place(lambda i: (-back[i] - cost[i], i), pre, zero)
+        back = place(lambda i: (-start[i] - cost[i], -i), succ, lat)
+        start = place(lambda i: (-back[i] - cost[i], i), pre, zero)
+        order = sorted(range(n), key=lambda i: (start[i], i))
+        return sum(replay(order, x) for x in others) + max(start[i] + cost[i] + lat[i] for i in range(n)), order, start
+
+    def replay(order, x):
+        end, free = [0.0] * n, {e: 0.0 for e in eng}
+        for i in order:
+            s = free[eng[i]]
+            for j, d in pre[i]:
+                v = end[j] + (x[j][1] if d > cost[j] else 0.0)
+                if v > s:
+                    s = v
+            end[i] = s + x[i][0]
+            if eng[i] != "net":
+                free[eng[i]] = end[i]
+        return max(end[i] + x[i][1] for i in range(n))
+    tags = sorted(set(o["tag"] for o in ops))
+    weight = {t: 0.0 for t in tags}
+    best = passes(weight)
+    seed = 1
+    for k in range(opt["tries"]):
+        trial = dict(weight)
+        for m in range(3):
+            seed = (seed * 1103515245 + 12345) % 2 ** 31
+            t = tags[(seed >> 8) % len(tags)]
+            trial[t] = max(0.0, trial[t] + ((seed >> 16) % 256 - 127.5) / 100)
+        got = passes(trial)
+        if got[0] <= best[0]:
+            weight, best = trial, got
+    start = best[2]
+    return best[1], {i: (start[i], start[i] + cost[i] + lat[i]) for i in range(n)}
+
+
+ORDER = {}
 
 
 def rank_program(g, core, T, topo):
@@ -641,8 +710,11 @@ def rank_program(g, core, T, topo):
         return
     ops, sent = plan(r, T, topo, PLAN, OPT)
     deps = depends(ops)
-    ref = plan(0, T, topo, PLAN, OPT)[0]
-    order, times = schedule(ref, depends(ref), OPT)
+    if not ORDER:
+        ref = plan(0, T, topo, PLAN, OPT)[0]
+        others = [[(o["cost"], o["lat"] + x["gap"]) for o in plan(0, T, topo, x, OPT)[0]] for x in [dict(PLAN, **y) for y in OTHER]]
+        ORDER["order"], ORDER["times"] = schedule(ref, depends(ref), PLAN, OPT, others)
+    order, times = ORDER["order"], ORDER["times"]
     queue = {"dve": g.vector, "act": g.scalar, "pe": g.tensor, "pool": g, "sp": g.sync}
     count = {}
     mark = {}

@@ -17,10 +17,10 @@ def sb(n, d):
 
 SCRATCH = {
     "bg": sb(O + W + RO * K, F), "eb": sb(2 * W, B16), "wn": sb(W, F), "cw": sb(K + 3072, B16), "tb": sb(W, B16), "vv": sb(K, F),
-    "vb": sb(K, B16), "vt": sb(288, B16), "hb": sb(512, F), "ho": sb(M, F), "tn": sb(512, F),
+    "vb": sb(K, B16), "vt": sb(288, B16), "hb": sb(512, F),
     "cg0": sb(64 + 2 * K, B16), "cg1": sb(64 + 2 * K, B16), "hh": sb(512, F), "bti": sb(768, I32), "b16": sb(768, U16),
-    "lagc": sb(224, I32), "wc": sb(224, B16), "cs": sb(8 * 224, B16), "ag": sb(224, B16), "sg": sb(448, B16), "ng": sb(224, B16),
-    "cab": sb(448, F), "pt": sb(448, F), "ct": sb(7 * 224, B16), "fill": sb(448, F), "zr": sb(1024, B16), "pk": sb(224, H16), "d4": sb(224, B16),
+    "lagc": sb(224, I32), "wc": sb(224, B16), "cs": sb(8 * 224, B16), "ag": sb(224, B16), "sg": sb(448, B16), "ng": sb(224, B16), "nw": sb(224, B16),
+    "cab": sb(448, F), "pt": sb(448, F), "ct": sb(7 * 224, B16), "fill": sb(512, F), "cf": sb(K + 1024, F), "gq": sb(144, F), "zr": sb(1024, B16), "pk": sb(224, H16), "d4": sb(224, B16),
     "dc": sb(224, I32), "s3": sb(56, I32), "fs": sb(3 * 56, H16), "fl": sb(3 * 448, H16), "pi": sb(8, I32), "pc": sb(16, F),
     "xr": sb(576, F), "x16": sb(128, F), "gs": sb(576, B16), "gh": sb(144, B16), "ge": sb(384, F), "lt": sb(128, B16),
     "ut": sb(128, B16), "im": sb(7 * 128, B16), "i32": sb(256, F), "i16": sb(128, H16), "ee": sb(128, F), "dj": sb(96, F), "kk": sb(32, F),
@@ -28,19 +28,21 @@ SCRATCH = {
     "ii": sb(784, B16), "tau": sb(104, F), "sl": sb(768, B16), "dd": sb(768, F), "nm": sb(192, F), "wk": sb(10 * 96, F), "nd": sb(96, B16),
     "kh": sb(96, B16), "o16": sb(384, U16), "c16": sb(384, U16), "xl": sb(384, U16), "qw": sb(64, F), "q16": sb(128, U16),
     "lg": sb(512, B16), "ml": sb(RO * 128, U16), "ll": sb(RO * 256, U16), "bs": sb(1024, F), "psn": sb(1536, F), "pl": sb(1536, F),
-    "tm": sb(128, F), "asn": sb(1536, F), "pr": sb(768, F), "tgb": sb(768, B16), "tgs": sb(768, F), "es": sb(192, F), "y16": sb(224, U16),
+    "tm": sb(128, F), "asn": sb(1536, F), "pr": sb(768, F), "tgb": sb(768, B16), "et": sb(128, B16), "es": sb(192, F), "y16": sb(224, U16),
 }
 PSUM = ("p_s", "p_c0", "p_c1", "p_n", "p_l", "p_p", "p_t0", "p_t1")
 for _n in PSUM:
     SCRATCH[_n] = ("psum", [128, 512], F)
 ND = 80
-SEMAPHORES = (["dve", "act", "pe", "pool", "sent", "ha"] + ["d%d" % i for i in range(ND)] + ["fa%d" % t for t in range(3)]
+SEMAPHORES = (["dve", "act", "pe", "pool", "sent", "ha", "hc"] + ["d%d" % i for i in range(ND)] + ["fa%d" % t for t in range(3)]
               + ["la%d" % t for t in range(1, RO)] + ["aa%d" % t for t in range(1, RO)] + ["pa%d" % s for s in range(N)])
 
-PLAN = {"cy": 0.0009, "ga": 1.5, "sa": 3.3, "pe": 0.00048, "dma": 1.9, "net": 1.0, "gap": 0.08}
-OPT = {"cg": (("a", 0, 48), ("d", 48, 96), ("a", 96, 144), ("d", 144, 192)), "ns": ("a", "a", "a", "aaa"), "cs": (0, 4, 4, 4),
-       "home": "ab", "x2": "aa", "step": "mqqd", "ans": ("", "dadadada", "dadadada", "dadadada"), "fin": "dadadada", "tries": 1000}
-OTHER = ({"cy": 0.00083, "ga": 1.2, "sa": 2.0, "net": 1.25}, {"cy": 0.0011, "ga": 1.8, "sa": 5.0, "pe": 0.0006, "gap": 0.1})
+PLAN = {"cy": 0.0009, "ga": 1.5, "sa": 3.3, "pe": 0.00048, "dma": 1.9, "net": 1.0, "link": 1.0, "gap": 0.08}
+OPT = {"half": "yyyn", "ns": ("aa", "aa", "aa", "xxxx"),
+       "cs": ((), (("d", 24),) * 4, (("d", 24), ("d", 24), ("a", 48)), (("a", 30), ("d", 34), ("d", 32))), "apart": "nnny",
+       "home": ("", "ab", "ab", "ab"), "hg": "x", "lg": "x", "x2": "xx", "step": "mqqp", "ans": ("", "xxxxxxxx", "xxxxxxxx", "xxxxxxxx"),
+       "fin": (24, 24, 36, 36, 32, 32, 20, 20), "out": ("sp", "sp"), "lean": 0.2, "h0": 10.0, "tries": 600, "swaps": 8000, "turns": 1, "heat": (0.4, 0.02), "seed": 5, "weight": {}}
+OTHER = ({"cy": 0.001, "ga": 1.2, "sa": 2.2, "net": 1.2, "link": 2.5, "dma": 2.2, "gap": 0.12}, {"cy": 0.0011, "ga": 1.8, "sa": 5.0, "pe": 0.0006, "gap": 0.1})
 
 
 def R(name, a, b, step=1, p=None, ind=None):
@@ -65,6 +67,13 @@ def peers(r, cores, topo):
     return near, far, en, ef
 
 
+def helper(r, cores, topo):
+    me = cores[r]
+    far = peers(r, cores, topo)[1]
+    able = [c for c in topo.cores_of(me) if c not in cores and topo.die(c) != topo.die(me) and all(topo.may_write(c, cores[d]) for d in far)]
+    return able[[c for c in cores if topo.chip(c) == topo.chip(me)].index(me)]
+
+
 def msk(es):
     return sum(1 << e for e in es)
 
@@ -73,8 +82,8 @@ def pieces(r, cores, topo):
     near, far, en, ef = peers(r, cores, topo)
     n1 = len(ef) // 4
     n2 = len(ef) // (len(far) - 4)
-    c1 = [(d, ef[i * n1:(i + 1) * n1]) for i, d in enumerate(far[:4])] + [(near[0], en)]
-    c2 = [(d, ef[i * n2:(i + 1) * n2]) for i, d in enumerate(far[4:])]
+    c1 = [(d, ef[i * n1:(i + 1) * n1]) for i, d in enumerate(far[:4])]
+    c2 = [(d, ef[i * n2:(i + 1) * n2]) for i, d in enumerate(far[4:])] + [(near[0], en)]
     return c1, c2
 
 
@@ -142,10 +151,24 @@ def plan(r, T, topo, sc, opt):
         return add("act", call, [a, scale, bias] + offs(o, a), [o, total], 0.015 + vcost(o, a, 1))
 
     def const(o, v):
-        return act(o, R("xr", 0, cnt(o)), scale=0.0, bias=v)
+        i = act(o, R("xr", 0, cnt(o)), scale=0.0, bias=v)
+        ops[i]["other"] = lambda g: g.vector.memset(ap(o), v)
+        return i
 
     def move(eng, o, a):
-        return cp(o, a) if eng == "d" else act(o, a)
+        if eng != "x":
+            return cp(o, a) if eng == "d" else act(o, a)
+        i = act(o, a)
+        ops[i]["other"] = lambda g: g.vector.tensor_copy(ap(o), ap(a))
+        return i
+
+    def lin(o, a, scale, bias, func=AF.Identity):
+        i = act(o, a, func, scale=scale, bias=bias)
+        if func == AF.Relu:
+            ops[i]["other"] = lambda g: g.vector.tensor_scalar(ap(o), ap(a), bias / scale, 0.0, ALU.add, ALU.max)
+        else:
+            ops[i]["other"] = lambda g: g.vector.tensor_scalar(ap(o), ap(a), scale, bias, ALU.mult, ALU.add)
+        return i
 
     def mms(lst):
         lst = [q if len(q) == 5 else q + (i == 0, i == len(lst) - 1) for i, q in enumerate(lst)]
@@ -182,7 +205,7 @@ def plan(r, T, topo, sc, opt):
         return add(q, call, [a] + ([o] if adds else []), [o], 0.07 if q != "pool" else 0.5, sc["dma"] + kb / 400.0, (s, 16), (), behind)
 
     def dst(d):
-        a = topo.addr(cores[d])
+        a = topo.addr(cores[d] if d >= 0 else helper(r, cores, topo))
         return DstId(rid=a[0], pnc=a[1])
 
     sent = [0]
@@ -194,7 +217,8 @@ def plan(r, T, topo, sc, opt):
                                local_sem=T.sem.sent)
             return None
         sent[0] += sum(len(q[2]) for q in trs)
-        return add("pool", call, [q[0] for q in trs], [], 0.8, lat * sc["net"], ("none", 0), (), behind)
+        i = add("pool", call, [q[0] for q in trs], [], 0.8, 1.0 * sc["net"], ("none", 0), (), behind)
+        return add("link", None, [], [], (lat - 2.2) * sc["link"], 1.12 * sc["net"], None, [i])
 
     def arrive(writes, sm, val, after):
         return add("net", None, [], writes, 0.0, 0.0, (sm, val), after)
@@ -227,15 +251,14 @@ def plan(r, T, topo, sc, opt):
     yy, prod = R("p_c1", 0, 224), R("p_c1", 224, 448)
     hi, lo = R("cs", 0, 224), R("cs", 224, 448)
 
-    def score():
-        tt(hi, yy, wc, ALU.mult)
+    def score(w):
+        tt(prod, yy, w, ALU.mult)
+        move("x", hi, prod)
         dma("sp", row("tb", 0, W, 1), hi, 57)
-        tt(prod, yy, wc, ALU.mult)
         tt(lo, prod, hi, ALU.subtract)
         dma("sp", row("tb", 0, W, 2), lo, 57)
 
     def overdue():
-        act(age, yy)
         mms([(R("p_n", 0, 224), I1, x) for x in (wc, hi, lo)])
         act(R("sg", 224, 448), R("p_n", 0, 224), AF.Sign, scale=1.0, bias=2.0 ** -10 - 4.0)
 
@@ -249,16 +272,20 @@ def plan(r, T, topo, sc, opt):
     ms(R("tb", 0, W), 0.0)
     dma("sp", row("tb", 0, W, 0), T.wt[:], 57)
     ts(yy, R("lagc", 0, 224), -1.0, ALU.add)
-    score()
+    score(wc)
+    move("x", age, yy)
     cp(R("b16", 0, 192), R("bti", 0, 192))
     iota(R("pi", 0, 1), [[0, 1]], 0, 1)
     iota(xr(576), [[1, 576]], 0, 0)
     iota(R("x16", 0, 128), [[0, 8], [1, 16]], 0, 0)
     own = R("eb", W + M * r, W + M * r + M)
     dma("act", own, T.e0[:, r * M:(r + 1) * M], 114)
-    s = bcast(own, own, "ha", 9.0, [row("tb", 0, W, 1), row("tb", 0, W, 2)])
-    arrive([R("eb", W + M * q, W + M * q + M) for q in others], "ha", allin, [s])
-    dma("sp", R("eb", 0, W), T.e0[:], 917, [row("tb", 0, W, 1), row("tb", 0, W, 2)])
+    rows = [row("tb", 0, W, 1), row("tb", 0, W, 2)]
+    half = len(en) // 2
+    s = send([(own, [(d, own) for d in far[:3]], ef, "ha"), (own, [(-1, own)], en[:half], "hc"), (own, [(near[0], own)], en[half:], "ha")], 6.0, rows)
+    ops[s]["lat"] = opt["h0"]
+    arrive([R("eb", W + M * q, W + M * q + M) for q in others], "ha", allin - half, [s])
+    dma("sp", R("eb", 0, W), T.e0[:], 917, rows)
     for i, (sh, bits) in enumerate(((0, 15), (0, 1), (2, 3))):
         ts(R("pi", i + 1, i + 2), R("pi", 0, 1), sh, ALU.logical_shift_right, bits, ALU.bitwise_and)
     cp(R("pc", 0, 4), R("pi", 0, 4))
@@ -279,10 +306,12 @@ def plan(r, T, topo, sc, opt):
     const(R("fill", 0, 224), -16384.0 * SC)
     const(R("fill", 224, 448), 16384.0 * SC)
     refill()
-    ms(R("sl", 0, 768), 0.0)
-    ms(R("mm", 0, 784), 0.0)
-    ms(R("d97", 0, 784), 1.0)
-    ms(R("d97", 0, 784, 97), 0.0)
+    for t in range(RO):
+        const(R("sl", 192 * t, 192 * t + 192, 2), 0.0)
+    const(R("mm", 0, 784, 97), 0.0)
+    for a in (0, 388):
+        const(R("d97", a, a + 388), 1.0)
+    const(R("d97", 0, 784, 97), 0.0)
     ts(R("ge", 0, 128), xr(128), pc[4], ALU.is_ge)
     ts(R("ge", 128, 256), xr(128), P_, ALU.is_ge)
     ts(R("ge", 256, 384), xr(128), pc[5], ALU.is_gt)
@@ -307,8 +336,12 @@ def plan(r, T, topo, sc, opt):
     act(R("vt", 0, 96), R("wk", 864, 960), scale=1.0, bias=pc[10])
     act(R("vt", 96, 192), R("x16", 0, 96), scale=1.0, bias=1.0)
     const(R("vt", 192, 288), V0 - 1.0)
+    ts(pc[15], P16, 15.0, ALU.is_equal, 1 / SC, ALU.mult)
+    ts(R("gq", 0, 144), xr(144), P_, ALU.is_equal, pc[15], ALU.mult)
+    const(R("fill", 448, 512), 0.0)
     for a in (0, 512):
         const(R("zr", a, a + 512), 0.0)
+        const(R("cf", K + a, K + a + 512), 0.0)
     for a in (0, 768):
         dma("sp", R("vb", a, a + 768), R("zr", 0, 768), 196)
     for i in range(3):
@@ -324,13 +357,13 @@ def plan(r, T, topo, sc, opt):
     ts(pc[14], P16, 12.0, ALU.is_equal)
     for t in range(2):
         act(R("cg%d" % t, 0, 64), xr(64), scale=pc[14], bias=pc[14])
-    if "b" in opt["home"]:
+    if "b" in "".join(opt["home"]):
         const(R("hb", 0, 512), 0.0)
     for t in range(RO - 1):
         const(R("bg", O - KP * (t + 1), O - KP * (t + 1) + 64), 0.0)
     top16 = ("top", 16)
     dma("sp", R("tgb", 0, 768, p=top16), T.tg[:], 25)
-    act(R("tgs", 0, 768, p=top16), R("tgb", 0, 768, p=top16), scale=-64.0)
+    act(R("et", 0, 128), R("ee", 0, 128), scale=-64.0)
 
     def wk(i):
         return R("wk", 96 * i, 96 * i + 96)
@@ -345,36 +378,43 @@ def plan(r, T, topo, sc, opt):
         cg = "cg%d" % (t % 2)
         a0 = 192 * t
         tag[0] = "cg%d" % t
-        s1, s2 = R("p_n", 320, 416), R("p_s", 0, 96)
-        for eng, a, b in opt["cg"]:
-            move(eng, R(cg, 64 + 16 * a, 64 + 16 * b), R("tb", 0, W, ind=R("b16", a0 + a, a0 + b)))
-        wrap(s1, "gs", 0, cg, 64, 96)
-        wrap(s2, "gs", 0, cg, 64 + K, 96)
         sa, mx, key, u, w1, w3, of2, m1, m2 = [wk(i) for i in range(9)]
         sel, nm = R("sl", a0 + 1, a0 + 192, 2), R("nm", 1, 192, 2)
         nd2, kh = R("nd", 0, 96), R("kh", 0, 96)
-        act(sa, s1)
-        tt(sel, s2, sa, ALU.is_gt)
-        scan(R("nm", 0, 192), R("sl", a0, a0 + 192), R("dd", a0, a0 + 192))
-        cp(R("o16", 96 * t, 96 * t + 96), nm)
-        tag[0] = "cnt%d" % t
-        tt(mx, s2, sa, ALU.max)
+        halves = opt["half"][t] == "y"
+        for a in ((0, 96, 48, 144) if halves else (0, 48, 96, 144)):
+            move("x", R(cg, 64 + 16 * a, 832 + 16 * a), R("tb", 0, W, ind=R("b16", a0 + a, a0 + a + 48)))
+        for a, b in ((0, 48), (48, 96)) if halves else ((0, 96),):
+            tag[0] = "cg%d" % t
+            s1, s2 = R("p_n", 320 + a, 320 + b), R("p_l" if a else "p_s", 2 * a, a + b)
+            for x, c in ((s2, K), (s1, 0)) if a else ((s1, 0), (s2, K)):
+                wrap(x, "gs", 0, cg, 64 + c + 16 * a, b - a)
+            move("x", R("wk", a, b), s1)
+            tt(R("sl", a0 + 2 * a + 1, a0 + 2 * b, 2), s2, R("wk", a, b), ALU.is_gt)
+            scan(R("nm", 2 * a, 2 * b), R("sl", a0 + 2 * a, a0 + 2 * b), R("dd", a0 + 2 * a, a0 + 2 * b))
+            cp(R("o16", 96 * t + a, 96 * t + b), R("nm", 2 * a + 1, 2 * b, 2))
+            tag[0] = "cnt%d" % t
+            tt(R("wk", 96 + a, 96 + b), s2, R("wk", a, b), ALU.max)
         ts(nd2, mx, 4.0, ALU.is_lt, 64.0 * M, ALU.mult)
         tt(key, nm, nd2, ALU.add)
-        ts(kh, key, 1.0 / M, ALU.mult, KH - 0.5 + 0.5 / M, ALU.add)
+        lin(kh, key, 1.0 / M, KH - 0.5 + 0.5 / M)
         for h in range(8):
             ts(R("mm", 97 * h + 1, 97 * h + 97), kh, float(KH + h), ALU.is_equal)
-        scan(R("sc", 0, 784), R("d97", 0, 784), R("mm", 0, 784))
+        scan(R("sc", 0, 777), R("d97", 0, 777), R("mm", 0, 777))
         for i, pb in enumerate(("p_c0", "p_c1")):
             x = 388 * i
-            mms([(R(pb, 0, 388), R("lt", 0, 128), R("sc", x + 1, x + 389)), (R(pb, 0, 388), R("ut", 0, 128), R("sc", x, x + 388))])
+            mms([(R(pb, 0, 388), I512, R("mm", x + 1, x + 389))] * (t == RO - 1)
+                + [(R(pb, 0, 388), R("lt", 0, 128), R("sc", x + 1, x + 389)), (R(pb, 0, 388), R("ut", 0, 128), R("sc", x, x + 388))])
         cn, p1, p2 = R("p_s", 96, 192), R("p_s", 192, 288), R("p_l", 0, 96)
 
         def ranks(o, hs):
             return [(o, I1, R("zz", 97 * h, 97 * h + 96)) for h in hs]
         for i, pb in enumerate(("p_c0", "p_c1")):
             x = 388 * i
-            tt(R("zz", x, x + 388), R(pb, 0, 388), R("mm", x + 1, x + 389), ALU.mult)
+            if t == RO - 1:
+                lin(R("zz", x, x + 388), R(pb, 0, 388), 1.0, -512.0, AF.Relu)
+            else:
+                tt(R("zz", x, x + 388), R(pb, 0, 388), R("mm", x + 1, x + 389), ALU.mult)
             lst = ([(cn, I1, nd2)] if i == 0 else []) + ranks(cn, range(4 * i, 4 * i + 4))
             mms([q + (i == 0 and k == 0, i == 1 and k == 3) for k, q in enumerate(lst)])
         if t == 0:
@@ -383,7 +423,8 @@ def plan(r, T, topo, sc, opt):
             cp(R("xl", 0, 96), w1)
         else:
             mms([(p2, I64, kh), (p2, I512, sel)] + ranks(p2, range(8)))
-            ts(u, cn, CAP + 0.5, ALU.is_gt, 32768.0, ALU.mult)
+            i = act(u, cn, AF.Relu, scale=65536.0, bias=-65536.0 * (CAP + 0.5))
+            ops[i]["other"] = lambda g: g.vector.tensor_scalar(ap(u), ap(cn), CAP + 0.5, 32768.0, ALU.is_gt, ALU.mult)
             tt(w3, p2, u, ALU.subtract)
             tt(of2, w3, R("dj", 0, 96), ALU.max)
             ts(R("c16", 96 * t, 96 * t + 96), of2, K - 1.0 - 64 * KH, ALU.add)
@@ -397,7 +438,7 @@ def plan(r, T, topo, sc, opt):
             act(R("p_n", 0, 224), R("sg", 224, 448), scale=half, bias=half)
         if t > 0:
             tag[0] = "xl%d" % t
-            a1, a2 = R("p_l", 96, 192), R("p_l", 192, 288)
+            a1, a2 = R("p_t0", 0, 96), R("p_t0", 96, 192)
             t24 = R("t24", 0, 96)
             mms([(p1, I64, kh)] + [(p1, I64, t24)] * (RO - t) + ranks(p1, range(8)))
             wrap(a1, "gs", 144, cg, 64, 96, [(a1, INEG, sel)])
@@ -411,10 +452,10 @@ def plan(r, T, topo, sc, opt):
         n = 96 // len(engs)
         for i, eng in enumerate(engs):
             o = R(win[1], win[2], win[3], ind=R(lst, 96 * t + n * i, 96 * t + n * i + n))
-            if eng == "a":
-                act(o, R("vv", 16 * n * i, 16 * n * (i + 1)), AF.Tanh)
-            else:
-                cp(o, R("vv", 16 * n * i, 16 * n * (i + 1)))
+            a = R("vv", 16 * n * i, 16 * n * (i + 1))
+            k = act(o, a, AF.Tanh)
+            if eng == "x":
+                ops[k]["other"] = lambda g, o=o, a=a: g.vector.tensor_copy(ap(o), ap(a))
 
     def names(t):
         last = t == RO - 1
@@ -433,6 +474,11 @@ def plan(r, T, topo, sc, opt):
             cp(fs, R("pk", 3, 224, 4))
             s = bcast(fs, R("fl", f0 + 56 * r, f0 + 56 * r + 56), "fa%d" % t)
             arrive([R("fl", f0 + 56 * q, f0 + 56 * q + 56) for q in others], "fa%d" % t, allin, [s])
+            if t and opt["step"][t - 1] == "m":
+                addup(t - 1)
+                ops[-1]["after"] = [s - 1]
+            mms([(R("p_n", 0, 224), I1, wc), (R("p_n", 0, 224), IBIG, ng)])
+            lin(R("nw", 0, 224), R("p_n", 0, 224), 1.0, -BIG, AF.Relu)
             act(R("sg", 0, 224), v0, AF.Sign)
             mms([(yy, I1, age), (yy, IHALF, R("sg", 0, 224)), (yy, IHALF, R("t15", 0, 224))])
         tag[0] = "ptr%d" % t
@@ -462,14 +508,14 @@ def plan(r, T, topo, sc, opt):
             for b in range(4):
                 ts(R("dc", b, 224, 4), R("s3", 0, 56), 3 * (3 - b), ALU.logical_shift_right, 7, ALU.bitwise_and)
             tt(yy, yy, R("dc", 0, 224), ALU.subtract)
-            tt(yy, yy, ng, ALU.mult)
-            score()
+            score(R("nw", 0, 224))
             tag[0] = "od%d" % t
             if t < RO - 2:
+                tt(age, yy, ng, ALU.mult)
                 overdue()
             if t == 0:
                 for x, a in ((R("bg", O, O + W), T.e0[:]), (R("hh", 64, 512), T.e0[:, r * M:(r + 1) * M])):
-                    dma("pool", x, a, cnt(x) // 2, [row("tb", 0, W, 1), row("tb", 0, W, 2)])
+                    dma("pool", x, a, cnt(x) // 2, rows)
         else:
             wrap(R("p_n", 0, 224), "gs", 144, "tb", 0, 224)
             ts(R("y16", 0, 224), R("p_n", 0, 224), -1.0, ALU.add)
@@ -477,30 +523,51 @@ def plan(r, T, topo, sc, opt):
     def lists(t):
         cg = "cg%d" % (t % 2)
         tag[0] = "ls%d" % t
-        w0, n = 1024 * (t - 1), 96 // opt["cs"][t]
-        for a in range(0, 96, n):
-            cp(R("cw", w0, w0 + K + 1024, ind=R("c16", 96 * t + a, 96 * t + a + n)), R("vb", 16 * a, 16 * (a + n)))
-        wrap(R("p_l", 288, 352), "gs", 0, "cw", w0 + K, 64, [(R("p_l", 288, 320), I64, R("t24", 0, 32))])
+        w0, a, fs = 1024 * (t - 1), 0, R("p_l", 288, 352)
+        for eng, n in opt["cs"][t]:
+            lst = R("c16", 96 * t + a, 96 * t + a + n)
+            if eng == "d":
+                cp(R("cw", w0, w0 + K + 1024, ind=lst), R("vb", 16 * a, 16 * (a + n)))
+            else:
+                act(R("cf", 0, K + 1024, ind=lst), R("vv", 16 * a, 16 * (a + n)), AF.Tanh)
+            a += n
+        runs = [[(fs, R(sel, 15 - i, 143 - i), R(win, b + i, b + 1024, 16)) for i in range(16)]
+                for eng, sel, win, b in (("d", "gs", "cw", w0 + K), ("a", "gq", "cf", K)) if eng in [q[0] for q in opt["cs"][t]]]
+        if opt["cs"][t][0][0] == "a":
+            runs = runs[::-1]
+        runs[0].insert(1, (R("p_l", 288, 320), I64, R("t24", 0, 32)))
+        lst = [q for x in runs for q in x]
+        lst = [q + (k == 0, k == len(lst) - 1) for k, q in enumerate(lst)]
+        for k in range(0, len(lst) - 1, 8):
+            mms(lst[k:k + 8] if k + 9 < len(lst) else lst[k:])
+        if "a" in [q[0] for q in opt["cs"][t]] and t < RO - 1:
+            dma("sp", row("cf", K, K + 1024, 15), R("fill", 448, 512), 32)
         tt(R("qw", 0, 32), R("p_l", 288, 320), R("kk", 0, 32), ALU.max)
         tt(R("qw", 32, 64), R("p_l", 320, 352), R("qw", 0, 32), ALU.max)
         ts(R("q16", 32 * t, 32 * t + 32), R("qw", 32, 64), -1.0, ALU.add)
-        act(R("lg", 0, 512), R(cg, 0, 64 + 2 * K, ind=R("q16", 32 * t, 32 * t + 32)))
+        for a, b in ((0, 16), (16, 32)) if opt["apart"][t] == "y" else ((0, 32),):
+            move(opt["lg"], R("lg", 16 * a, 16 * b), R(cg, 0, 64 + 2 * K, ind=R("q16", 32 * t + a, 32 * t + b)))
         m0 = 128 * t
         wrap(R("p_l", 384, 416), "gs", 288, "lg", 0, 32)
         ts(R("ml", m0 + 64, m0 + 96), R("p_l", 384, 416), -1.0, ALU.mult, KP * t - 1.0, ALU.add)
-        wrap(R("p_l", 448, 480), "gs", 144, "lg", 0, 32)
-        wrap(R("p_l", 416, 448), "gs", 432, "lg", 0, 32)
-        ts(R("ml", m0, m0 + 64), R("p_l", 416, 480), -1.0, ALU.add)
+        wrap(R("p_t1", 32, 64), "gs", 144, "lg", 0, 32)
         if opt["step"][t - 1] == "q":
             c = float(W + K * (t - 1))
-            ts(R("ml", m0 + 96, m0 + 128), R("p_l", 448, 480), c, ALU.max, 63.0 - c, ALU.add)
+            ts(R("ml", m0 + 96, m0 + 128), R("p_t1", 32, 64), c, ALU.max, 63.0 - c, ALU.add)
+        if opt["apart"][t] == "y":
+            ts(R("ml", m0 + 32, m0 + 64), R("p_t1", 32, 64), -1.0, ALU.add)
+            wrap(R("p_l", 416, 448), "gs", 432, "lg", 0, 32)
+            ts(R("ml", m0, m0 + 32), R("p_l", 416, 448), -1.0, ALU.add)
+        else:
+            wrap(R("p_t1", 0, 32), "gs", 432, "lg", 0, 32)
+            ts(R("ml", m0, m0 + 64), R("p_t1", 0, 64), -1.0, ALU.add)
         l0 = 256 * t
         s = bcast(R("ml", m0, m0 + 32), R("ll", l0 + 32 * r, l0 + 32 * r + 32), "la%d" % t)
         arrive([R("ll", l0 + 32 * q, l0 + 32 * q + 32) for q in others], "la%d" % t, allin, [s])
 
-    def addup(t):
+    def addup(t, behind=()):
         x0, c0 = O - KP * (t + 1) + 64, O + W + K * t
-        dma("pool", R("bg", c0, c0 + K), R("bg", x0, x0 + K), 1570, adds=True)
+        dma("pool", R("bg", c0, c0 + K), R("bg", x0, x0 + K), 1570, behind, True)
 
     def data(t):
         x0, c0, m0 = O - KP * (t + 1) + 64, O + W + K * t, 128 * t
@@ -511,76 +578,87 @@ def plan(r, T, topo, sc, opt):
         tag[0] = "hm%d" % t
         if t > 0:
             p0 = 512 * (t - 1)
-            act(R("bs", 0, 512), R("bg", O - KP * t, O + W, ind=R("ml", m0 + 64, m0 + 96)))
-            now = R("bg", O, c0, ind=R("ml", m0 + 32, m0 + 64))
-            if opt["step"][t - 1] == "q":
-                tt(R("bs", 512, 1024), R("bg", O - KP * t, O - KP * (t - 1), ind=R("ml", m0 + 96, m0 + 128)), R("bs", 0, 512), ALU.subtract)
-                tt(R("psn", p0, p0 + 512), now, R("bs", 512, 1024), ALU.add)
-            else:
-                tt(R("psn", p0, p0 + 512), now, R("bs", 0, 512), ALU.subtract)
+            late = opt["step"][t - 1] == "q"
+            chips = sorted(range(0, N, 2), key=lambda d: (d - far[0]) % N)
+            for d, n in [(d, 2) for d in chips] if opt["apart"][t] == "y" else [(0, N)]:
+                a, b = 64 * d, 64 * (d + n)
+                move(opt["lg"], R("bs", a, b), R("bg", O - KP * t, O + W, ind=R("ml", m0 + 64 + 4 * d, m0 + 64 + 4 * (d + n))))
+                if late:
+                    tt(R("bs", 512 + a, 512 + b), R("bg", O - KP * t, O - KP * (t - 1), ind=R("ml", m0 + 96 + 4 * d, m0 + 96 + 4 * (d + n))),
+                       R("bs", a, b), ALU.subtract)
+            for d in chips:
+                a = 64 * d + 512 * late
+                tt(R("psn", p0 + 64 * d, p0 + 64 * d + 128), R("bg", O, c0, ind=R("ml", m0 + 32 + 4 * d, m0 + 40 + 4 * d)),
+                   R("bs", a, a + 128), ALU.add if late else ALU.subtract)
             ss = [send([(R("psn", p0 + 64 * d, p0 + 64 * d + 64), [(d, R("pl", p0 + 64 * r, p0 + 64 * r + 64))], es, "pa%d" % r)
-                        for d, es in c], lat) for c, lat in ((c1, 3.4), (c2, 3.8))]
-            if opt["step"][t - 1] == "q":
+                        for d, es in c], lat) for c, lat in ((c1, 3.4), (c2, 3.0))]
+            if late:
                 i = len(ops)
                 addup(t - 1)
-                ops[i]["after"] = ss
-            order = [r] + sorted(into, key=lambda s: (s not in near, into[s][0], (s - r) % N))
+                ops[i]["after"] = [ss[1] - 1]
+            order = [r] + sorted(into, key=lambda s: (into[s][0], s not in near, (s - r) % N))
             for i, s in enumerate(order):
                 if s == r:
                     src = R("psn", p0 + 64 * r, p0 + 64 * r + 64)
                 else:
                     src = R("pl", p0 + 64 * s, p0 + 64 * s + 64)
-                    arrive([src], "pa%d" % s, t * into[s][1], [ss[0 if i <= 5 else 1]])
+                    arrive([src], "pa%d" % s, t * into[s][1], [ss[into[s][0]]])
                 tm = R("tm", 64 * (i % 2), 64 * (i % 2) + 64)
-                part = "hb" if "b" in opt["home"] and i % 2 else "hh"
-                if "a" in opt["home"]:
-                    act(tm, home(s, part))
+                part = "hb" if "b" in opt["home"][t] and i % 2 else "hh"
+                if "a" in opt["home"][t]:
+                    move(opt["hg"], tm, home(s, part))
                     tt(home(s, part), tm, src, ALU.add)
                 else:
                     tt(tm, home(s, part), src, ALU.add)
                     cp(home(s, part), tm)
             for i, d in enumerate([d for d, es in c1 + c2] + [r]):
                 o = R("bg", c0 + 64 * r, c0 + 64 * r + 64) if d == r else R("asn", p0 + 64 * d, p0 + 64 * d + 64)
-                if "b" in opt["home"]:
-                    act(R("tn", 64 * i, 64 * i + 64), home(d))
-                    tt(o, home(d, "hb"), R("tn", 64 * i, 64 * i + 64), ALU.add)
+                if "b" in "".join(opt["home"][:t + 1]):
+                    move(opt["hg"], R("bs", 512 + 64 * i, 576 + 64 * i), home(d))
+                    tt(o, home(d, "hb"), R("bs", 512 + 64 * i, 576 + 64 * i), ALU.add)
                 else:
                     move(opt["ans"][t][i], o, home(d))
             ss = [send([(R("asn", p0 + 64 * d, p0 + 64 * d + 64), [(d, R("bg", c0 + 64 * r, c0 + 64 * r + 64))], es, "aa%d" % t)
-                        for d, es in c], lat) for c, lat in ((c1, 3.4), (c2, 3.8))]
+                        for d, es in c], lat) for c, lat in ((c1, 3.4), (c2, 3.2))]
             arrive([R("bg", c0 + 64 * q, c0 + 64 * q + 64) for q in others], "aa%d" % t, sum(v[1] for v in into.values()), ss)
-        if t == RO - 1 and "b" in opt["home"]:
-            tt(R("ho", 0, M), R("hh", 64, 512), R("hb", 64, 512), ALU.add)
-            dma("sp", T.yh[:], R("ho", 0, M), 229)
+        if t == RO - 1 and "b" in "".join(opt["home"]):
+            tt(R("bs", 0, M), R("hh", 64, 512), R("hb", 64, 512), ALU.add)
+            dma("sp", T.yh[:], R("bs", 0, M), 229)
         elif t == RO - 1:
             dma("sp", T.yh[:], R("hh", 64, 512), 229)
         tag[0] = "st%d" % t
         pp = R("p_p", 0, 192)
-        mms([(pp, R("ee", 0, 128, p=top16), R("tgs", 192 * t, 192 * t + 192, p=top16), True, False)])
+        mms([(pp, R("et", 0, 128, p=top16), R("tgb", 192 * t, 192 * t + 192, p=top16), True, False)])
 
         def xg(a, b):
             lst = R("xl", 96 * t + a, 96 * t + b)
             return R("bg", O, c0 + 512, ind=lst) if t else R("eb", 0, 2 * W, ind=lst)
-        for k in range(4):
-            xa = R("bg", x0 + 192 * k, x0 + 192 * k + 192)
-            act(xa, xg(12 * k, 12 * k + 12))
-            tt(R("pr", 192 * k, 192 * k + 192), xg(48 + 12 * k, 60 + 12 * k), xa, ALU.mult)
-            mms([(pp, R("ee", 0, 128), R("pr", 192 * k, 192 * k + 192), False, k == 3)])
+        for a, b in ((0, 6), (6, 12), (12, 24), (24, 36), (36, 48)):
+            xa, pr = R("bg", x0 + 16 * a, x0 + 16 * b), R("pr", 16 * a, 16 * b)
+            move(opt["lg"], xa, xg(a, b))
+            tt(pr, xg(48 + a, 48 + b), xa, ALU.mult)
+            mms([(R("p_p", 16 * a % 192, 16 * a % 192 + cnt(pr)), R("ee", 0, 128), pr, False, b == 48)])
         move(opt["x2"][0], R("bg", x0 + 768, x0 + 1152), xg(48, 72))
         move(opt["x2"][1], R("bg", x0 + 1152, x0 + 1536), xg(72, 96))
+        both = opt["step"][t] == "p"
+        for i in range(2 * both):
+            mms([(R("p_t%d" % i, 0, 384), FSC, R("bg", x0 + 384 * i, x0 + 384 * i + 384), True, False)])
         act(R("es", 0, 192), pp, AF.Tanh, scale=-1.0 / 64, bias=0.0)
         act(R("p_p", 0, 192), R("es", 0, 192), scale=1.0 / 64)
         act(R("p_p", 192, 384), R("es", 0, 192), scale=1.0 / 64)
-        for i, (mine, par) in enumerate(((768, 0), (1152, 384), (0, 768), (384, 1152))):
+        for i, (mine, par) in enumerate(((0, 768), (384, 1152), (768, 0), (1152, 384))):
             out = R("bg", c0 + mine, c0 + mine + 384)
-            if opt["step"][t] == "d":
-                tb = R("p_t%d" % (i % 2), 0, 384)
+            if both and i < 2:
+                tb = R("pr", mine, mine + 384)
+                tt(tb, R("bg", x0 + par, x0 + par + 384), R("p_p", 0, 384), ALU.mult)
+                mms([(R("p_t%d" % i, 0, 384), FSC, tb, False, True)])
+                act(out, R("p_t%d" % i, 0, 384), scale=SC)
+            elif opt["step"][t] in "dp":
+                tb = R(("p_c%d" if both else "p_t%d") % (i % 2), 0, 384)
                 tt(tb, R("bg", x0 + par, x0 + par + 384), R("p_p", 0, 384), ALU.mult)
                 tt(out, R("bg", x0 + mine, x0 + mine + 384), tb, ALU.add)
             else:
                 tt(out, R("bg", x0 + par, x0 + par + 384), R("p_p", 0, 384), ALU.mult)
-        if opt["step"][t] == "m":
-            addup(t)
 
     for t in range(RO):
         prepare(t)
@@ -595,10 +673,11 @@ def plan(r, T, topo, sc, opt):
             names(t)
         data(t)
     tag[0] = "fin"
-    for i in range(8):
-        a = M * i
-        move(opt["fin"][i], R("bg", KP + a, KP + a + M), R("bg", O, O + W + RO * K, ind=R("y16", 28 * i, 28 * i + 28)))
-        dma("sp" if i % 2 == 0 else "pool", T.yr[:, a:a + M], R("bg", KP + a, KP + a + M), 229)
+    a = 0
+    for i, n in enumerate(opt["fin"]):
+        move("ad"[i % 2], R("bg", KP + 16 * a, KP + 16 * (a + n)), R("bg", O, O + W + RO * K, ind=R("y16", a, a + n)))
+        dma(opt["out"][i % 2], T.yr[:, 16 * a:16 * (a + n)], R("bg", KP + 16 * a, KP + 16 * (a + n)), 8 * n)
+        a += n
     return ops, sent[0]
 
 
@@ -618,7 +697,7 @@ def depends(ops):
         mine = [(x, False) for x in o["rd"]] + [(x, True) for x in o["wr"]]
         for x, w in mine:
             for j, y, v in seen.get(x[1], ()):
-                if (x[1] in PSUM and ops[j]["eng"] != o["eng"]) or ((w or v) and clash(x, y)):
+                if (x[1] in PSUM and (ops[j]["eng"] != o["eng"] or "other" in o or "other" in ops[j]) and j != i) or ((w or v) and clash(x, y)):
                     d.add(j)
         for x in o["bh"]:
             d.update(j for j, y, v in seen.get(x[1], ()) if v and clash(x, y))
@@ -640,7 +719,18 @@ def schedule(ops, deps, sc, opt, others=()):
             pre[i].append((j, cost[j] + lag))
             succ[j].append((i, cost[i] + lag))
 
-    def place(rank, links, first):
+    either = ["other" in o for o in ops]
+
+    def gap(line, s, c):
+        k = len(line)
+        while k and line[k - 1][1] > s:
+            k -= 1
+        while k < len(line) and line[k][0] < s + c - 1e-9:
+            s = line[k][1]
+            k += 1
+        return s, k
+
+    def place(rank, links, first, choose=False):
         start = [0.0] * n
         busy = {e: [] for e in eng}
         for i in sorted(range(n), key=rank):
@@ -648,15 +738,11 @@ def schedule(ops, deps, sc, opt, others=()):
             for j, d in links[i]:
                 if start[j] + d > s:
                     s = start[j] + d
+            if choose and either[i]:
+                eng[i] = "dve" if gap(busy["dve"], s, cost[i])[0] + opt["lean"] < gap(busy["act"], s, cost[i])[0] else "act"
             if eng[i] != "net":
-                line = busy[eng[i]]
-                k = len(line)
-                while k and line[k - 1][1] > s:
-                    k -= 1
-                while k < len(line) and line[k][0] < s + cost[i] - 1e-9:
-                    s = line[k][1]
-                    k += 1
-                line.insert(k, (s, s + cost[i]))
+                s, k = gap(busy[eng[i]], s, cost[i])
+                busy[eng[i]].insert(k, (s, s + cost[i]))
             start[i] = s
         return start
     zero = [0.0] * n
@@ -666,11 +752,11 @@ def schedule(ops, deps, sc, opt, others=()):
         back = [0.0] * n
         for i in range(n - 1, -1, -1):
             back[i] = max([back[j] + d for j, d in succ[i]] + [lat[i]]) + weight[ops[i]["tag"]] * cost[i]
-        start = place(lambda i: (-back[i] - cost[i], i), pre, zero)
+        start = place(lambda i: (-back[i] - cost[i], i), pre, zero, True)
         back = place(lambda i: (-start[i] - cost[i], -i), succ, lat)
-        start = place(lambda i: (-back[i] - cost[i], i), pre, zero)
+        start = place(lambda i: (-back[i] - cost[i], i), pre, zero, True)
         order = sorted(range(n), key=lambda i: (start[i], i))
-        return sum(replay(order, x) for x in others) + max(start[i] + cost[i] + lat[i] for i in range(n)), order, start
+        return sum(replay(order, x) for x in others) + max(start[i] + cost[i] + lat[i] for i in range(n)), order, start, list(eng)
 
     def replay(order, x):
         end, free = [0.0] * n, {e: 0.0 for e in eng}
@@ -685,9 +771,9 @@ def schedule(ops, deps, sc, opt, others=()):
                 free[eng[i]] = end[i]
         return max(end[i] + x[i][1] for i in range(n))
     tags = sorted(set(o["tag"] for o in ops))
-    weight = {t: 0.0 for t in tags}
+    weight = {t: opt["weight"].get(t, opt["weight"].get(t[:-1], 0.0)) for t in tags}
     best = passes(weight)
-    seed = 1
+    seed = opt["seed"]
     for k in range(opt["tries"]):
         trial = dict(weight)
         for m in range(3):
@@ -697,8 +783,90 @@ def schedule(ops, deps, sc, opt, others=()):
         got = passes(trial)
         if got[0] <= best[0]:
             weight, best = trial, got
-    start = best[2]
-    return best[1], {i: (start[i], start[i] + cost[i] + lat[i]) for i in range(n)}
+    ORDER["weight"] = (best[0], weight)
+    figures = [[(cost[i], lat[i] + sc["gap"]) for i in range(n)]] + list(others)
+    order, best = best[1], (1e9, best[1], best[3])
+    eng[:] = best[2]
+    for k in range(opt["turns"]):
+        got = polish(order, eng, pre, cost, either, figures, opt["swaps"], opt["heat"])
+        best = min(best, got)
+        eng[:] = best[2]
+        end = walk(best[1], eng, [[(j, d > cost[j]) for j, d in p] for p in pre], figures[k % len(figures)])[1]
+        back = place(lambda i: (-end[i], -i), succ, lat)
+        start = place(lambda i: (-back[i] - cost[i], i), pre, zero)
+        order = sorted(range(n), key=lambda i: (start[i], i))
+    order, eng = best[1:]
+    end = walk(order, eng, [[(j, d > cost[j]) for j, d in p] for p in pre], figures[0])[1]
+    return order, {i: (end[i] - cost[i], end[i] + lat[i]) for i in range(n)}, eng
+
+
+def walk(order, eng, pre, x, a=0, old=None):
+    end, by = (list(old[1]), list(old[2])) if a else ([0.0] * len(order), [-1] * len(order))
+    last = {eng[i]: i for i in order[:a] if eng[i] != "net"}
+    for i in order[a:]:
+        k = last.get(eng[i], -1)
+        s = end[k] if k >= 0 else 0.0
+        for j, far in pre[i]:
+            v = end[j] + x[j][1] if far else end[j]
+            if v >= s:
+                s, k = v, -2 - j
+        end[i], by[i] = s + x[i][0], k
+        if eng[i] != "net":
+            last[eng[i]] = i
+    i = max(order[-40:], key=lambda i: end[i] + x[i][1])
+    return end[i] + x[i][1], end, by, i
+
+
+def polish(order, eng, pre, cost, either, figures, swaps, heat):
+    n = len(order)
+    above = [0] * n
+    for i in range(n):
+        for j, d in pre[i]:
+            above[i] |= above[j] | 1 << j
+    pre = [[(j, d > cost[j]) for j, d in p if not any(above[k] >> j & 1 and (d <= cost[j] or cost[k] > 3) for k, c in p)] for p in pre]
+    eng = list(eng)
+    sends = [i for i in range(n) if eng[i] == "pool"]
+
+    def worth(ws):
+        return sum(w[0] + heat[1] * sum(w[1][i] for i in sends) for w in ws)
+    now = [walk(order, eng, pre, x) for x in figures]
+    best = (worth(now), order, list(eng))
+    here = best[0]
+    seed = 7
+    for turn in range(swaps):
+        seed = (seed * 1103515245 + 12345) % 2 ** 31
+        by, i = now[turn % len(now)][2:]
+        if turn & 4:
+            i = sends[(seed >> 4) % len(sends)]
+        links = []
+        while by[i] != -1:
+            if by[i] >= 0 and not above[i] >> by[i] & 1:
+                links.append((by[i], i))
+            i = by[i] if by[i] >= 0 else -2 - by[i]
+        if not links:
+            continue
+        j, i = links[(seed >> 8) % len(links)]
+        flip = [k for k in (i, j) if either[k]]
+        new = order
+        if flip and seed >> 20 & 3 == 0:
+            flip = flip[(seed >> 22) % len(flip)]
+            eng[flip] = "act" if eng[flip] == "dve" else "dve"
+            a = order.index(flip)
+        else:
+            flip = -1
+            a, b = order.index(j), order.index(i) + 1
+            up = above[i] | 1 << i
+            new = order[:a] + [k for k in order[a:b] if up >> k & 1] + [k for k in order[a:b] if not up >> k & 1] + order[b:]
+        got = [walk(new, eng, pre, x, a, w) for x, w in zip(figures, now)]
+        total = worth(got)
+        if total <= here + heat[0] * (seed >> 12 & 15) / 15 * (1 - turn / swaps):
+            end = got[0][1]
+            order, now, here = sorted(new, key=lambda k: end[k] - cost[k]), got, total
+            if total < best[0]:
+                best = (total, order, list(eng))
+        elif flip >= 0:
+            eng[flip] = "act" if eng[flip] == "dve" else "dve"
+    return best
 
 
 ORDER = {}
@@ -707,14 +875,29 @@ ORDER = {}
 def rank_program(g, core, T, topo):
     r = T.rank_of(core)
     if r is None:
+        cores = list(T.cores)
+        for q in range(N):
+            if core == helper(q, cores, topo):
+                near, far, en, ef = peers(q, cores, topo)
+                far = far[3:]
+                es = topo.engines(core, cores[far[0]])
+                x = T.eb[:, W + M * q:W + M * q + M]
+                g.wait_ge(T.sem.hc, len(en) // 2)
+                g.remote_dma_fused([RemoteDMATransfer(dst_ids=[DstId(rid=topo.addr(cores[d])[0], pnc=topo.addr(cores[d])[1]) for d in far],
+                                                      dma_engine_mask=msk(es), remote_sem=T.sem.ha, srcs=[x], dsts=[x] * len(far))],
+                                   local_sem=T.sem.sent)
+                g.wait_ge(T.sem.sent, len(es))
         return
     ops, sent = plan(r, T, topo, PLAN, OPT)
     deps = depends(ops)
-    if not ORDER:
+    if "order" not in ORDER:
         ref = plan(0, T, topo, PLAN, OPT)[0]
         others = [[(o["cost"], o["lat"] + x["gap"]) for o in plan(0, T, topo, x, OPT)[0]] for x in [dict(PLAN, **y) for y in OTHER]]
-        ORDER["order"], ORDER["times"] = schedule(ref, depends(ref), PLAN, OPT, others)
+        ORDER["order"], ORDER["times"], ORDER["queues"] = schedule(ref, depends(ref), PLAN, OPT, others)
     order, times = ORDER["order"], ORDER["times"]
+    for o, e in zip(ops, ORDER["queues"]):
+        if e != o["eng"]:
+            o["eng"], o["call"] = e, o["other"]
     queue = {"dve": g.vector, "act": g.scalar, "pe": g.tensor, "pool": g, "sp": g.sync}
     count = {}
     mark = {}
@@ -724,6 +907,8 @@ def rank_program(g, core, T, topo):
     for i in order:
         o = ops[i]
         e = o["eng"]
+        if e == "link":
+            continue
         if e == "net":
             mark[i] = o["sem"]
             clock[i] = {o["sem"][0]: o["sem"][1]}

from concourse.bass import DstId, RemoteDMATransfer
from concourse.mybir import AluOpType as ALU, ActivationFunctionType as AF

N, W, K, M, RO, CAP = 8, 3584, 1536, 448, 4, 64
SC = 2.0 ** -18
V0 = K + 65
KP = K + 64
O = RO * KP
KH = 152
BIG = 12288.0
F, B16, H16, I32, U16 = "float32", "bfloat16", "float16", "int32", "uint16"


def sb(n, d):
    return ("sbuf", [128, n], d)


SCRATCH = {
    "bg": sb(O + W + RO * K, F), "eb": sb(2 * W, B16), "wn": sb(W, F), "cw": sb(K + 3072, B16), "tb": sb(W, B16), "vv": sb(K, F),
    "vb": sb(K, B16), "vt": sb(288, B16), "hb": sb(512, F),
    "cg0": sb(64 + 2 * K, B16), "cg1": sb(64 + 2 * K, B16), "hh": sb(512, F), "bti": sb(768, I32), "b16": sb(768, U16),
    "lagc": sb(224, I32), "wc": sb(224, B16), "cs": sb(8 * 224, B16), "ag": sb(224, B16), "sg": sb(448, B16), "ng": sb(224, B16), "nw": sb(224, B16),
    "cab": sb(448, F), "pt": sb(448, F), "ct": sb(7 * 224, B16), "fill": sb(512, F), "cf": sb(K + 1024, F), "gq": sb(144, F), "zr": sb(1024, B16), "pk": sb(224, H16), "d4": sb(224, B16),
    "dc": sb(224, I32), "s3": sb(56, I32), "fs": sb(3 * 56, H16), "fl": sb(3 * 448, H16), "pi": sb(8, I32), "pc": sb(16, F),
    "xr": sb(576, F), "x16": sb(128, F), "gs": sb(576, B16), "gh": sb(144, B16), "ge": sb(384, F), "lt": sb(128, B16),
    "ut": sb(128, B16), "im": sb(7 * 128, B16), "i32": sb(256, F), "i16": sb(128, H16), "ee": sb(128, F), "dj": sb(96, F), "kk": sb(32, F),
    "t15": sb(224, B16), "t24": sb(96, B16), "mm": sb(784, B16), "sc": sb(784, B16), "d97": sb(784, B16), "zz": sb(784, B16),
    "ii": sb(784, B16), "tau": sb(104, F), "sl": sb(768, B16), "dd": sb(768, F), "nm": sb(192, F), "wk": sb(10 * 96, F), "nd": sb(96, B16),
    "kh": sb(96, B16), "o16": sb(384, U16), "c16": sb(384, U16), "xl": sb(384, U16), "qw": sb(64, F), "q16": sb(128, U16),
    "lg": sb(512, B16), "ml": sb(RO * 128, U16), "ll": sb(RO * 256, U16), "bs": sb(1024, F), "psn": sb(1536, F), "pl": sb(1536, F),
    "tm": sb(128, F), "asn": sb(1536, F), "pr": sb(768, F), "tgb": sb(768, B16), "et": sb(128, B16), "es": sb(192, F), "y16": sb(224, U16),
}
PSUM = ("p_s", "p_c0", "p_c1", "p_n", "p_l", "p_p", "p_t0", "p_t1")
for _n in PSUM:
    SCRATCH[_n] = ("psum", [128, 512], F)
ND = 80
SEMAPHORES = (["dve", "act", "pe", "pool", "sent", "ha", "hc"] + ["d%d" % i for i in range(ND)] + ["fa%d" % t for t in range(3)]
              + ["la%d" % t for t in range(1, RO)] + ["aa%d" % t for t in range(1, RO)] + ["pa%d" % s for s in range(N)])

PLAN = {"cy": 0.0009, "ga": 1.5, "sa": 3.3, "pe": 0.00048, "dma": 1.9, "net": 1.0, "link": 1.0, "gap": 0.08}
OPT = {"half": "yyyn", "ns": ("aa", "aa", "aa", "xxxx"),
       "cs": ((), (("d", 24),) * 4, (("d", 24), ("d", 24), ("a", 48)), (("a", 30), ("d", 34), ("d", 32))), "apart": "nnny",
       "home": ("", "ab", "ab", "ab"), "hg": "x", "lg": "x", "x2": "xx", "step": "mqqp", "ans": ("", "xxxxxxxx", "xxxxxxxx", "xxxxxxxx"),
       "fin": (24, 24, 36, 36, 32, 32, 20, 20), "out": ("sp", "sp"), "lean": 0.2, "h0": 10.0, "tries": 600, "swaps": 8000, "turns": 1, "heat": (0.4, 0.02), "seed": 5, "weight": {}}
OTHER = ({"cy": 0.001, "ga": 1.2, "sa": 2.2, "net": 1.2, "link": 2.5, "dma": 2.2, "gap": 0.12}, {"cy": 0.0011, "ga": 1.8, "sa": 5.0, "pe": 0.0006, "gap": 0.1})


def R(name, a, b, step=1, p=None, ind=None):
    return ("R", name, a, b, step, p, ind)


def isr(x):
    return isinstance(x, tuple) and x[0] == "R"


def cnt(r):
    return 16 * (r[6][3] - r[6][2]) if r[6] else len(range(r[2], r[3], r[4]))


def peers(r, cores, topo):
    me = cores[r]
    order = [(r + k) % N for k in range(1, N)]
    near = [d for d in order if topo.chip(cores[d]) == topo.chip(me)]
    far = [d for d in order if d not in near]
    ef = topo.engines(me, cores[far[0]])
    en = [e for e in topo.engines(me, cores[near[0]]) if e not in ef]
    return near, far, en, ef


def helper(r, cores, topo):
    me = cores[r]
    far = peers(r, cores, topo)[1]
    able = [c for c in topo.cores_of(me) if c not in cores and topo.die(c) != topo.die(me) and all(topo.may_write(c, cores[d]) for d in far)]
    return able[[c for c in cores if topo.chip(c) == topo.chip(me)].index(me)]


def msk(es):
    return sum(1 << e for e in es)


def pieces(r, cores, topo):
    near, far, en, ef = peers(r, cores, topo)
    n1 = len(ef) // 4
    n2 = len(ef) // (len(far) - 4)
    c1 = [(d, ef[i * n1:(i + 1) * n1]) for i, d in enumerate(far[:4])]
    c2 = [(d, ef[i * n2:(i + 1) * n2]) for i, d in enumerate(far[4:])] + [(near[0], en)]
    return c1, c2


def plan(r, T, topo, sc, opt):
    CY, PEC = sc["cy"], sc["pe"]
    cores = list(T.cores)
    ops = []
    nd = [0]
    tag = ["init"]

    def add(eng, call, reads, writes, cost, lat=0.0, sem=None, after=(), behind=()):
        ops.append({"eng": eng, "bh": list(behind), "call": call, "rd": [x for x in reads if isr(x)], "wr": [x for x in writes if isr(x)],
                    "tag": tag[0], "cost": cost, "lat": lat, "sem": sem, "after": list(after)})
        return len(ops) - 1

    def ap(x):
        if not isr(x):
            return x
        t = T[x[1]]
        p = x[5]
        ps = slice(None) if p is None else (slice(p[1], 128, 16) if p[0] == "rows" else slice(0, p[1]))
        a = t[ps, x[2]:x[3]] if x[4] == 1 else t[ps, x[2]:x[3]:x[4]]
        return a.indirect(ap(x[6])) if x[6] else a

    def offs(*xs):
        return [x[6] for x in xs if isr(x) and x[6]]

    def two(*xs):
        return all(SCRATCH[x[1]][2] in (B16, H16, U16) for x in xs)

    def vcost(o, i, base):
        if o[6]:
            return 0.05 + cnt(o) * sc["sa"] * CY
        if i[6]:
            return 0.05 + cnt(i) * sc["ga"] * CY
        return 0.05 + max(64, cnt(i) * base) * CY

    def tt(o, a, b, op):
        f = 1 if (a[1] in PSUM or b[1] in PSUM) else 2
        return add("dve", lambda g: g.vector.tensor_tensor(ap(o), ap(a), ap(b), op), [a, b] + offs(o, a), [o], vcost(o, a, f))

    def ts(o, a, s1, op0, s2=None, op1=None):
        if op1 is None:
            call = lambda g: g.vector.tensor_scalar(ap(o), ap(a), ap(s1), None, op0)
        else:
            call = lambda g: g.vector.tensor_scalar(ap(o), ap(a), ap(s1), ap(s2), op0, op1)
        return add("dve", call, [a, s1, s2], [o], vcost(o, a, 0.5 if two(o, a) else 1))

    def cp(o, a):
        return add("dve", lambda g: g.vector.tensor_copy(ap(o), ap(a)), [a] + offs(o, a), [o], vcost(o, a, 0.5 if two(o, a) else 1))

    def ms(o, v):
        return add("dve", lambda g: g.vector.memset(ap(o), v), [], [o], vcost(o, o, 0.5 if two(o) else 1))

    def scan(o, d0, d1):
        return add("dve", lambda g: g.vector.tensor_tensor_scan(ap(o), ap(d0), ap(d1), 0.0, ALU.mult, ALU.add), [d0, d1], [o],
                   vcost(o, d1, 0.5 if two(o, d0, d1) else 1))

    def act(o, a, func=AF.Identity, scale=None, bias=None, total=None):
        if scale is None:
            call = lambda g: g.scalar.activation(ap(o), ap(a), func)
        else:
            call = lambda g: g.scalar.activation(ap(o), ap(a), func, bias=ap(bias) if isr(bias) else float(bias or 0.0),
                                                 scale=ap(scale) if isr(scale) else float(scale), accum_out=ap(total))
        return add("act", call, [a, scale, bias] + offs(o, a), [o, total], 0.015 + vcost(o, a, 1))

    def const(o, v):
        i = act(o, R("xr", 0, cnt(o)), scale=0.0, bias=v)
        ops[i]["other"] = lambda g: g.vector.memset(ap(o), v)
        return i

    def move(eng, o, a):
        if eng != "x":
            return cp(o, a) if eng == "d" else act(o, a)
        i = act(o, a)
        ops[i]["other"] = lambda g: g.vector.tensor_copy(ap(o), ap(a))
        return i

    def lin(o, a, scale, bias, func=AF.Identity):
        i = act(o, a, func, scale=scale, bias=bias)
        if func == AF.Relu:
            ops[i]["other"] = lambda g: g.vector.tensor_scalar(ap(o), ap(a), bias / scale, 0.0, ALU.add, ALU.max)
        else:
            ops[i]["other"] = lambda g: g.vector.tensor_scalar(ap(o), ap(a), scale, bias, ALU.mult, ALU.add)
        return i

    def mms(lst):
        lst = [q if len(q) == 5 else q + (i == 0, i == len(lst) - 1) for i, q in enumerate(lst)]

        def call(g):
            ins = None
            for o, l, x, s0, s1 in lst:
                ins = g.tensor.matmul(ap(o), ap(l), ap(x), s0, s1)
            return ins
        c = sum(max(64, cnt(q[2])) * (4 if SCRATCH[q[2][1]][2] == F else 1) for q in lst)
        return add("pe", call, [q[1] for q in lst] + [q[2] for q in lst], [q[0] for q in lst], c * PEC, 0.08)

    def wrap(o, sel, s0, src, a, n, more=()):
        return mms([(o, R(sel, s0 + 15 - i, s0 + 143 - i), R(src, a + i, a + 16 * n, 16)) for i in range(16)] + list(more))

    def iota(o, pat, base, cm):
        if SCRATCH[o[1]][2] != I32:
            call = lambda g: g.iota(ap(o), pat, base, cm, allow_small_or_imprecise_dtypes=True)
        else:
            call = lambda g: g.iota(ap(o), pat, base, cm)
        return add("pool", call, [], [o], 0.13 + 2 * cnt(o) * CY)

    def dma(q, o, a, kb, behind=(), adds=False):
        s = "d%d" % nd[0]
        nd[0] += 1
        if q == "sp":
            call = lambda g: g.sync.dma_start(ap(o), ap(a))
        elif q == "act":
            call = lambda g: g.scalar.dma_start(ap(o), ap(a))
        elif adds:
            call = lambda g: g.dma_start(ap(o), ap(a), accum_op=ALU.add)
        else:
            call = lambda g: g.dma_start(ap(o), ap(a))
        return add(q, call, [a] + ([o] if adds else []), [o], 0.07 if q != "pool" else 0.5, sc["dma"] + kb / 400.0, (s, 16), (), behind)

    def dst(d):
        a = topo.addr(cores[d] if d >= 0 else helper(r, cores, topo))
        return DstId(rid=a[0], pnc=a[1])

    sent = [0]

    def send(trs, lat, behind=()):
        def call(g):
            g.remote_dma_fused([RemoteDMATransfer(dst_ids=[dst(d) for d, x in ds], dma_engine_mask=msk(es), remote_sem=T.sem[sm],
                                                  srcs=[ap(s)], dsts=[ap(x) for d, x in ds]) for s, ds, es, sm in trs],
                               local_sem=T.sem.sent)
            return None
        sent[0] += sum(len(q[2]) for q in trs)
        i = add("pool", call, [q[0] for q in trs], [], 0.8, 1.0 * sc["net"], ("none", 0), (), behind)
        return add("link", None, [], [], (lat - 2.2) * sc["link"], 1.12 * sc["net"], None, [i])

    def arrive(writes, sm, val, after):
        return add("net", None, [], writes, 0.0, 0.0, (sm, val), after)

    near, far, en, ef = peers(r, cores, topo)
    c1, c2 = pieces(r, cores, topo)
    others = [q for q in range(N) if q != r]
    into = {}
    allin = 0
    for s in others:
        for i, c in enumerate(pieces(s, cores, topo)):
            for d, es in c:
                if d == r:
                    into[s] = (i, len(es))
        q = peers(s, cores, topo)
        allin += len(q[2]) if r in q[0] else len(q[3])

    def bcast(src, land, sm, lat=3.2, behind=()):
        return send([(src, [(d, land) for d in far], ef, sm), (src, [(d, land) for d in near], en, sm)], lat, behind)

    def row(name, a, b, i):
        return R(name, a, b, p=("rows", i))

    def xr(n):
        return R("xr", 0, n)

    I1, IHALF, I64, I512, IBIG, INEG, ISC = [R("im", 128 * i, 128 * i + 128) for i in range(7)]
    FSC, FNEG = R("i32", 0, 128), R("i32", 128, 256)
    wc, ng, age = R("wc", 0, 224), R("ng", 0, 224), R("ag", 0, 224)
    yy, prod = R("p_c1", 0, 224), R("p_c1", 224, 448)
    hi, lo = R("cs", 0, 224), R("cs", 224, 448)

    def score(w):
        tt(prod, yy, w, ALU.mult)
        move("x", hi, prod)
        dma("sp", row("tb", 0, W, 1), hi, 57)
        tt(lo, prod, hi, ALU.subtract)
        dma("sp", row("tb", 0, W, 2), lo, 57)

    def overdue():
        mms([(R("p_n", 0, 224), I1, x) for x in (wc, hi, lo)])
        act(R("sg", 224, 448), R("p_n", 0, 224), AF.Sign, scale=1.0, bias=2.0 ** -10 - 4.0)

    def refill():
        dma("sp", row("wn", 0, W, 1), R("fill", 224, 448), 114)
        dma("sp", row("wn", 0, W, 0), R("fill", 0, 224), 114)

    dma("sp", R("lagc", 0, 224), T.lag[:], 114)
    dma("act", wc, T.wt[:], 57)
    dma("sp", R("bti", 0, 768), T.bt[:], 393)
    ms(R("tb", 0, W), 0.0)
    dma("sp", row("tb", 0, W, 0), T.wt[:], 57)
    ts(yy, R("lagc", 0, 224), -1.0, ALU.add)
    score(wc)
    move("x", age, yy)
    cp(R("b16", 0, 192), R("bti", 0, 192))
    iota(R("pi", 0, 1), [[0, 1]], 0, 1)
    iota(xr(576), [[1, 576]], 0, 0)
    iota(R("x16", 0, 128), [[0, 8], [1, 16]], 0, 0)
    own = R("eb", W + M * r, W + M * r + M)
    dma("act", own, T.e0[:, r * M:(r + 1) * M], 114)
    rows = [row("tb", 0, W, 1), row("tb", 0, W, 2)]
    half = len(en) // 2
    s = send([(own, [(d, own) for d in far[:3]], ef, "ha"), (own, [(-1, own)], en[:half], "hc"), (own, [(near[0], own)], en[half:], "ha")], 6.0, rows)
    ops[s]["lat"] = opt["h0"]
    arrive([R("eb", W + M * q, W + M * q + M) for q in others], "ha", allin - half, [s])
    dma("sp", R("eb", 0, W), T.e0[:], 917, rows)
    for i, (sh, bits) in enumerate(((0, 15), (0, 1), (2, 3))):
        ts(R("pi", i + 1, i + 2), R("pi", 0, 1), sh, ALU.logical_shift_right, bits, ALU.bitwise_and)
    cp(R("pc", 0, 4), R("pi", 0, 4))
    pc = [R("pc", i, i + 1) for i in range(16)]
    P_, P16, P2, P4 = pc[:4]
    tt(pc[4], P_, P16, ALU.subtract)
    ts(pc[5], pc[4], 15.0, ALU.add)
    ts(pc[6], P4, 144.0, ALU.mult, pc[5], ALU.add)
    ts(R("gs", 0, 576), xr(576), pc[6], ALU.is_equal)
    ts(I1, xr(128), P_, ALU.is_equal)
    for x, v in ((IHALF, 0.5), (I64, 64.0), (I512, 512.0), (IBIG, BIG), (INEG, -BIG), (ISC, 1 / SC), (FSC, 1 / SC), (FNEG, -1 / SC)):
        act(x, I1, scale=v)
    cp(R("i16", 0, 128), I1)
    overdue()
    for a in range(0, K, 512):
        act(R("vv", a, a + 512), xr(512), scale=SC, bias=(a + V0) * SC)
    act(R("hh", 0, 64), xr(64), AF.Tanh, scale=0.0)
    const(R("fill", 0, 224), -16384.0 * SC)
    const(R("fill", 224, 448), 16384.0 * SC)
    refill()
    for t in range(RO):
        const(R("sl", 192 * t, 192 * t + 192, 2), 0.0)
    const(R("mm", 0, 784, 97), 0.0)
    for a in (0, 388):
        const(R("d97", a, a + 388), 1.0)
    const(R("d97", 0, 784, 97), 0.0)
    ts(R("ge", 0, 128), xr(128), pc[4], ALU.is_ge)
    ts(R("ge", 128, 256), xr(128), P_, ALU.is_ge)
    ts(R("ge", 256, 384), xr(128), pc[5], ALU.is_gt)
    tt(R("ut", 0, 128), R("ge", 0, 128), R("ge", 128, 256), ALU.subtract)
    tt(R("lt", 0, 128), R("ge", 128, 256), R("ge", 256, 384), ALU.subtract)
    act(pc[7], pc[5], scale=-1.0, bias=0.5)
    act(R("ge", 0, 144), xr(144), AF.Abs, scale=1.0, bias=pc[7])
    ts(R("gh", 0, 144), R("ge", 0, 144), 1.0, ALU.is_lt)
    const(R("d4", 0, 224), 8.0)
    const(R("d4", 0, 224, 4), 0.0)
    const(R("t15", 0, 224), 15.0)
    const(R("t24", 0, 96), -K / 64.0)
    tag[0] = "late"
    cp(R("b16", 192, 768), R("bti", 192, 768))
    act(pc[8], P16, scale=224.0, bias=1.0)
    act(pc[9], pc[8], scale=-1.0)
    act(R("pt", 0, 224), xr(224), scale=1.0, bias=pc[8])
    act(R("pt", 224, 448), xr(224), scale=-1.0, bias=pc[9])
    ts(R("ee", 0, 128), R("x16", 0, 128), P16, ALU.is_equal)
    act(pc[10], P16, scale=96.0)
    tt(R("wk", 864, 960), xr(96), R("x16", 0, 96), ALU.subtract)
    act(R("vt", 0, 96), R("wk", 864, 960), scale=1.0, bias=pc[10])
    act(R("vt", 96, 192), R("x16", 0, 96), scale=1.0, bias=1.0)
    const(R("vt", 192, 288), V0 - 1.0)
    ts(pc[15], P16, 15.0, ALU.is_equal, 1 / SC, ALU.mult)
    ts(R("gq", 0, 144), xr(144), P_, ALU.is_equal, pc[15], ALU.mult)
    const(R("fill", 448, 512), 0.0)
    for a in (0, 512):
        const(R("zr", a, a + 512), 0.0)
        const(R("cf", K + a, K + a + 512), 0.0)
    for a in (0, 768):
        dma("sp", R("vb", a, a + 768), R("zr", 0, 768), 196)
    for i in range(3):
        dma("sp", row("vb", 0, K, i), R("vt", 96 * i, 96 * i + 96), 25)
        dma("sp", R("cw", K + 1024 * i, K + 1024 * i + 1024), R("zr", 0, 1024), 262)
    act(pc[11], P16, scale=1.0, bias=64.0 * KH + 1 - K)
    act(R("dj", 0, 96), xr(96), scale=16.0, bias=pc[11])
    act(pc[12], P16, scale=1.0, bias=1.0)
    act(R("kk", 0, 32), R("x16", 0, 128, 4), scale=4.0, bias=pc[12])
    act(pc[13], P2, scale=224.0, bias=64.0)
    act(R("cs", 1344, 1568), xr(224), scale=1.0, bias=1.0)
    act(R("cs", 1568, 1792), xr(224), scale=0.0, bias=pc[13])
    ts(pc[14], P16, 12.0, ALU.is_equal)
    for t in range(2):
        act(R("cg%d" % t, 0, 64), xr(64), scale=pc[14], bias=pc[14])
    if "b" in "".join(opt["home"]):
        const(R("hb", 0, 512), 0.0)
    for t in range(RO - 1):
        const(R("bg", O - KP * (t + 1), O - KP * (t + 1) + 64), 0.0)
    top16 = ("top", 16)
    dma("sp", R("tgb", 0, 768, p=top16), T.tg[:], 25)
    act(R("et", 0, 128), R("ee", 0, 128), scale=-64.0)

    def wk(i):
        return R("wk", 96 * i, 96 * i + 96)

    def prepare(t):
        tag[0] = "prep%d" % t
        a, m, b = 192 * t, 192 * t + 96, 192 * t + 192
        tt(R("dd", a, b, 2), R("bti", m, b), R("bti", a, m), ALU.subtract)
        cp(R("dd", a + 1, b, 2), R("bti", a, m))

    def control(t):
        cg = "cg%d" % (t % 2)
        a0 = 192 * t
        tag[0] = "cg%d" % t
        sa, mx, key, u, w1, w3, of2, m1, m2 = [wk(i) for i in range(9)]
        sel, nm = R("sl", a0 + 1, a0 + 192, 2), R("nm", 1, 192, 2)
        nd2, kh = R("nd", 0, 96), R("kh", 0, 96)
        halves = opt["half"][t] == "y"
        for a in ((0, 96, 48, 144) if halves else (0, 48, 96, 144)):
            move("x", R(cg, 64 + 16 * a, 832 + 16 * a), R("tb", 0, W, ind=R("b16", a0 + a, a0 + a + 48)))
        for a, b in ((0, 48), (48, 96)) if halves else ((0, 96),):
            tag[0] = "cg%d" % t
            s1, s2 = R("p_n", 320 + a, 320 + b), R("p_l" if a else "p_s", 2 * a, a + b)
            for x, c in ((s2, K), (s1, 0)) if a else ((s1, 0), (s2, K)):
                wrap(x, "gs", 0, cg, 64 + c + 16 * a, b - a)
            move("x", R("wk", a, b), s1)
            tt(R("sl", a0 + 2 * a + 1, a0 + 2 * b, 2), s2, R("wk", a, b), ALU.is_gt)
            scan(R("nm", 2 * a, 2 * b), R("sl", a0 + 2 * a, a0 + 2 * b), R("dd", a0 + 2 * a, a0 + 2 * b))
            cp(R("o16", 96 * t + a, 96 * t + b), R("nm", 2 * a + 1, 2 * b, 2))
            tag[0] = "cnt%d" % t
            tt(R("wk", 96 + a, 96 + b), s2, R("wk", a, b), ALU.max)
        ts(nd2, mx, 4.0, ALU.is_lt, 64.0 * M, ALU.mult)
        tt(key, nm, nd2, ALU.add)
        lin(kh, key, 1.0 / M, KH - 0.5 + 0.5 / M)
        for h in range(8):
            ts(R("mm", 97 * h + 1, 97 * h + 97), kh, float(KH + h), ALU.is_equal)
        scan(R("sc", 0, 777), R("d97", 0, 777), R("mm", 0, 777))
        for i, pb in enumerate(("p_c0", "p_c1")):
            x = 388 * i
            mms([(R(pb, 0, 388), I512, R("mm", x + 1, x + 389))] * (t == RO - 1)
                + [(R(pb, 0, 388), R("lt", 0, 128), R("sc", x + 1, x + 389)), (R(pb, 0, 388), R("ut", 0, 128), R("sc", x, x + 388))])
        cn, p1, p2 = R("p_s", 96, 192), R("p_s", 192, 288), R("p_l", 0, 96)

        def ranks(o, hs):
            return [(o, I1, R("zz", 97 * h, 97 * h + 96)) for h in hs]
        for i, pb in enumerate(("p_c0", "p_c1")):
            x = 388 * i
            if t == RO - 1:
                lin(R("zz", x, x + 388), R(pb, 0, 388), 1.0, -512.0, AF.Relu)
            else:
                tt(R("zz", x, x + 388), R(pb, 0, 388), R("mm", x + 1, x + 389), ALU.mult)
            lst = ([(cn, I1, nd2)] if i == 0 else []) + ranks(cn, range(4 * i, 4 * i + 4))
            mms([q + (i == 0 and k == 0, i == 1 and k == 3) for k, q in enumerate(lst)])
        if t == 0:
            ts(u, cn, CAP + 0.5, ALU.is_le, float(W), ALU.mult)
            tt(w1, nm, u, ALU.add)
            cp(R("xl", 0, 96), w1)
        else:
            mms([(p2, I64, kh), (p2, I512, sel)] + ranks(p2, range(8)))
            i = act(u, cn, AF.Relu, scale=65536.0, bias=-65536.0 * (CAP + 0.5))
            ops[i]["other"] = lambda g: g.vector.tensor_scalar(ap(u), ap(cn), CAP + 0.5, 32768.0, ALU.is_gt, ALU.mult)
            tt(w3, p2, u, ALU.subtract)
            tt(of2, w3, R("dj", 0, 96), ALU.max)
            ts(R("c16", 96 * t, 96 * t + 96), of2, K - 1.0 - 64 * KH, ALU.add)
        if t < RO - 1:
            tag[0] = "tau%d" % t
            for i, pb in enumerate(("p_c0", "p_c1")):
                act(R("ii", 388 * i, 388 * i + 388), R(pb, 0, 388), AF.Sign, scale=-1.0, bias=CAP + 0.5)
            mms([(R("p_n", 224, 320), R("gh", 14 - 2 * h, 142 - 2 * h), R("ii", 97 * h, 97 * h + 96)) for h in range(8)])
            half = R("tau", 96, 97)
            act(R("tau", 0, 96), R("p_n", 224, 320), scale=SC / 4, bias=(K / 4 + (V0 - 0.5) / 2) * SC / 96, total=half)
            act(R("p_n", 0, 224), R("sg", 224, 448), scale=half, bias=half)
        if t > 0:
            tag[0] = "xl%d" % t
            a1, a2 = R("p_t0", 0, 96), R("p_t0", 96, 192)
            t24 = R("t24", 0, 96)
            mms([(p1, I64, kh)] + [(p1, I64, t24)] * (RO - t) + ranks(p1, range(8)))
            wrap(a1, "gs", 144, cg, 64, 96, [(a1, INEG, sel)])
            wrap(a2, "gs", 144, cg, 64 + K, 96, [(a2, IBIG, sel), (a2, I512, t24)])
            tt(w1, p1, u, ALU.subtract)
            tt(m1, a1, w1, ALU.max)
            tt(m2, a2, m1, ALU.max)
            ts(R("xl", 96 * t, 96 * t + 96), m2, -1.0, ALU.add)

    def spread(engs, win, lst, t):
        n = 96 // len(engs)
        for i, eng in enumerate(engs):
            o = R(win[1], win[2], win[3], ind=R(lst, 96 * t + n * i, 96 * t + n * i + n))
            a = R("vv", 16 * n * i, 16 * n * (i + 1))
            k = act(o, a, AF.Tanh)
            if eng == "x":
                ops[k]["other"] = lambda g, o=o, a=a: g.vector.tensor_copy(ap(o), ap(a))

    def names(t):
        last = t == RO - 1
        tag[0] = "ns%d" % t
        f0 = 448 * t
        v0, v1 = R("cab", 0, 224), R("cab", 224, 448)
        spread(opt["ns"][t], R("wn", 0, W), "o16", t)
        if not last:
            dma("sp", v1, row("wn", 0, W, 1), 114)
        dma("sp", v0, row("wn", 0, W, 0), 114)
        if not last:
            refill()
            tt(ng, v1, R("p_n", 0, 224), ALU.is_gt)
            scan(R("pk", 0, 224), R("d4", 0, 224), ng)
            fs = R("fs", 56 * t, 56 * t + 56)
            cp(fs, R("pk", 3, 224, 4))
            s = bcast(fs, R("fl", f0 + 56 * r, f0 + 56 * r + 56), "fa%d" % t)
            arrive([R("fl", f0 + 56 * q, f0 + 56 * q + 56) for q in others], "fa%d" % t, allin, [s])
            if t and opt["step"][t - 1] == "m":
                addup(t - 1)
                ops[-1]["after"] = [s - 1]
            mms([(R("p_n", 0, 224), I1, wc), (R("p_n", 0, 224), IBIG, ng)])
            lin(R("nw", 0, 224), R("p_n", 0, 224), 1.0, -BIG, AF.Relu)
            act(R("sg", 0, 224), v0, AF.Sign)
            mms([(yy, I1, age), (yy, IHALF, R("sg", 0, 224)), (yy, IHALF, R("t15", 0, 224))])
        tag[0] = "ptr%d" % t
        n = 224 if last else 448
        za, zb, z = R("p_c0", 0, 224), R("p_c0", 224, 448), R("p_c0", 0, n)
        ca, cb = R("ct", f0, f0 + 224), R("ct", f0 + 224, f0 + 448)
        const(ca, (W + K * t + 1 - V0) / 64.0)
        mms([(za, FSC, v0), (za, I64, ca)])
        if not last:
            const(cb, (KP * (t + 1) - 65 + V0) / 64.0)
            mms([(zb, FNEG, v1), (zb, I64, cb), (zb, INEG, ng)])
        tt(R("pt", 0, n), z, R("pt", 0, n), ALU.max)
        act(R("cs", 448, 448 + n), R("pt", 0, n))
        mms([(z, FNEG, R("pt", 0, n)), (z, ISC, R("cs", 448, 448 + n))])
        for i in range(n // 224):
            dma("sp", row("tb", 0, W, 4 + 4 * i), R("cs", 448 + 224 * i, 672 + 224 * i), 57)
        act(R("cs", 896, 896 + n), z, scale=-SC)
        for i in range(n // 224):
            dma("sp", row("tb", 0, W, 5 + 4 * i), R("cs", 896 + 224 * i, 1120 + 224 * i), 57)
        if t == 0:
            dma("sp", row("tb", 0, W, 12), R("cs", 1344, 1568), 57)
            dma("sp", row("tb", 0, W, 13), R("cs", 1568, 1792), 57)
        tag[0] = "age%d" % t
        if not last:
            mms([(R("p_c1", 448, 504), R("i16", 0, 128), R("fl", f0 + 56 * q, f0 + 56 * q + 56)) for q in others])
            cp(R("s3", 0, 56), R("p_c1", 448, 504))
            for b in range(4):
                ts(R("dc", b, 224, 4), R("s3", 0, 56), 3 * (3 - b), ALU.logical_shift_right, 7, ALU.bitwise_and)
            tt(yy, yy, R("dc", 0, 224), ALU.subtract)
            score(R("nw", 0, 224))
            tag[0] = "od%d" % t
            if t < RO - 2:
                tt(age, yy, ng, ALU.mult)
                overdue()
            if t == 0:
                for x, a in ((R("bg", O, O + W), T.e0[:]), (R("hh", 64, 512), T.e0[:, r * M:(r + 1) * M])):
                    dma("pool", x, a, cnt(x) // 2, rows)
        else:
            wrap(R("p_n", 0, 224), "gs", 144, "tb", 0, 224)
            ts(R("y16", 0, 224), R("p_n", 0, 224), -1.0, ALU.add)

    def lists(t):
        cg = "cg%d" % (t % 2)
        tag[0] = "ls%d" % t
        w0, a, fs = 1024 * (t - 1), 0, R("p_l", 288, 352)
        for eng, n in opt["cs"][t]:
            lst = R("c16", 96 * t + a, 96 * t + a + n)
            if eng == "d":
                cp(R("cw", w0, w0 + K + 1024, ind=lst), R("vb", 16 * a, 16 * (a + n)))
            else:
                act(R("cf", 0, K + 1024, ind=lst), R("vv", 16 * a, 16 * (a + n)), AF.Tanh)
            a += n
        runs = [[(fs, R(sel, 15 - i, 143 - i), R(win, b + i, b + 1024, 16)) for i in range(16)]
                for eng, sel, win, b in (("d", "gs", "cw", w0 + K), ("a", "gq", "cf", K)) if eng in [q[0] for q in opt["cs"][t]]]
        if opt["cs"][t][0][0] == "a":
            runs = runs[::-1]
        runs[0].insert(1, (R("p_l", 288, 320), I64, R("t24", 0, 32)))
        lst = [q for x in runs for q in x]
        lst = [q + (k == 0, k == len(lst) - 1) for k, q in enumerate(lst)]
        for k in range(0, len(lst) - 1, 8):
            mms(lst[k:k + 8] if k + 9 < len(lst) else lst[k:])
        if "a" in [q[0] for q in opt["cs"][t]] and t < RO - 1:
            dma("sp", row("cf", K, K + 1024, 15), R("fill", 448, 512), 32)
        tt(R("qw", 0, 32), R("p_l", 288, 320), R("kk", 0, 32), ALU.max)
        tt(R("qw", 32, 64), R("p_l", 320, 352), R("qw", 0, 32), ALU.max)
        ts(R("q16", 32 * t, 32 * t + 32), R("qw", 32, 64), -1.0, ALU.add)
        for a, b in ((0, 16), (16, 32)) if opt["apart"][t] == "y" else ((0, 32),):
            move(opt["lg"], R("lg", 16 * a, 16 * b), R(cg, 0, 64 + 2 * K, ind=R("q16", 32 * t + a, 32 * t + b)))
        m0 = 128 * t
        wrap(R("p_l", 384, 416), "gs", 288, "lg", 0, 32)
        ts(R("ml", m0 + 64, m0 + 96), R("p_l", 384, 416), -1.0, ALU.mult, KP * t - 1.0, ALU.add)
        wrap(R("p_t1", 32, 64), "gs", 144, "lg", 0, 32)
        if opt["step"][t - 1] == "q":
            c = float(W + K * (t - 1))
            ts(R("ml", m0 + 96, m0 + 128), R("p_t1", 32, 64), c, ALU.max, 63.0 - c, ALU.add)
        if opt["apart"][t] == "y":
            ts(R("ml", m0 + 32, m0 + 64), R("p_t1", 32, 64), -1.0, ALU.add)
            wrap(R("p_l", 416, 448), "gs", 432, "lg", 0, 32)
            ts(R("ml", m0, m0 + 32), R("p_l", 416, 448), -1.0, ALU.add)
        else:
            wrap(R("p_t1", 0, 32), "gs", 432, "lg", 0, 32)
            ts(R("ml", m0, m0 + 64), R("p_t1", 0, 64), -1.0, ALU.add)
        l0 = 256 * t
        s = bcast(R("ml", m0, m0 + 32), R("ll", l0 + 32 * r, l0 + 32 * r + 32), "la%d" % t)
        arrive([R("ll", l0 + 32 * q, l0 + 32 * q + 32) for q in others], "la%d" % t, allin, [s])

    def addup(t, behind=()):
        x0, c0 = O - KP * (t + 1) + 64, O + W + K * t
        dma("pool", R("bg", c0, c0 + K), R("bg", x0, x0 + K), 1570, behind, True)

    def data(t):
        x0, c0, m0 = O - KP * (t + 1) + 64, O + W + K * t, 128 * t

        def home(s, part="hh"):
            return R(part, 0, 512, ind=R("ml", m0 + 4 * r, m0 + 4 * r + 4) if s == r else
                     R("ll", 256 * t + 32 * s + 4 * r, 256 * t + 32 * s + 4 * r + 4))
        tag[0] = "hm%d" % t
        if t > 0:
            p0 = 512 * (t - 1)
            late = opt["step"][t - 1] == "q"
            chips = sorted(range(0, N, 2), key=lambda d: (d - far[0]) % N)
            for d, n in [(d, 2) for d in chips] if opt["apart"][t] == "y" else [(0, N)]:
                a, b = 64 * d, 64 * (d + n)
                move(opt["lg"], R("bs", a, b), R("bg", O - KP * t, O + W, ind=R("ml", m0 + 64 + 4 * d, m0 + 64 + 4 * (d + n))))
                if late:
                    tt(R("bs", 512 + a, 512 + b), R("bg", O - KP * t, O - KP * (t - 1), ind=R("ml", m0 + 96 + 4 * d, m0 + 96 + 4 * (d + n))),
                       R("bs", a, b), ALU.subtract)
            for d in chips:
                a = 64 * d + 512 * late
                tt(R("psn", p0 + 64 * d, p0 + 64 * d + 128), R("bg", O, c0, ind=R("ml", m0 + 32 + 4 * d, m0 + 40 + 4 * d)),
                   R("bs", a, a + 128), ALU.add if late else ALU.subtract)
            ss = [send([(R("psn", p0 + 64 * d, p0 + 64 * d + 64), [(d, R("pl", p0 + 64 * r, p0 + 64 * r + 64))], es, "pa%d" % r)
                        for d, es in c], lat) for c, lat in ((c1, 3.4), (c2, 3.0))]
            if late:
                i = len(ops)
                addup(t - 1)
                ops[i]["after"] = [ss[1] - 1]
            order = [r] + sorted(into, key=lambda s: (into[s][0], s not in near, (s - r) % N))
            for i, s in enumerate(order):
                if s == r:
                    src = R("psn", p0 + 64 * r, p0 + 64 * r + 64)
                else:
                    src = R("pl", p0 + 64 * s, p0 + 64 * s + 64)
                    arrive([src], "pa%d" % s, t * into[s][1], [ss[into[s][0]]])
                tm = R("tm", 64 * (i % 2), 64 * (i % 2) + 64)
                part = "hb" if "b" in opt["home"][t] and i % 2 else "hh"
                if "a" in opt["home"][t]:
                    move(opt["hg"], tm, home(s, part))
                    tt(home(s, part), tm, src, ALU.add)
                else:
                    tt(tm, home(s, part), src, ALU.add)
                    cp(home(s, part), tm)
            for i, d in enumerate([d for d, es in c1 + c2] + [r]):
                o = R("bg", c0 + 64 * r, c0 + 64 * r + 64) if d == r else R("asn", p0 + 64 * d, p0 + 64 * d + 64)
                if "b" in "".join(opt["home"][:t + 1]):
                    move(opt["hg"], R("bs", 512 + 64 * i, 576 + 64 * i), home(d))
                    tt(o, home(d, "hb"), R("bs", 512 + 64 * i, 576 + 64 * i), ALU.add)
                else:
                    move(opt["ans"][t][i], o, home(d))
            ss = [send([(R("asn", p0 + 64 * d, p0 + 64 * d + 64), [(d, R("bg", c0 + 64 * r, c0 + 64 * r + 64))], es, "aa%d" % t)
                        for d, es in c], lat) for c, lat in ((c1, 3.4), (c2, 3.2))]
            arrive([R("bg", c0 + 64 * q, c0 + 64 * q + 64) for q in others], "aa%d" % t, sum(v[1] for v in into.values()), ss)
        if t == RO - 1 and "b" in "".join(opt["home"]):
            tt(R("bs", 0, M), R("hh", 64, 512), R("hb", 64, 512), ALU.add)
            dma("sp", T.yh[:], R("bs", 0, M), 229)
        elif t == RO - 1:
            dma("sp", T.yh[:], R("hh", 64, 512), 229)
        tag[0] = "st%d" % t
        pp = R("p_p", 0, 192)
        mms([(pp, R("et", 0, 128, p=top16), R("tgb", 192 * t, 192 * t + 192, p=top16), True, False)])

        def xg(a, b):
            lst = R("xl", 96 * t + a, 96 * t + b)
            return R("bg", O, c0 + 512, ind=lst) if t else R("eb", 0, 2 * W, ind=lst)
        for a, b in ((0, 6), (6, 12), (12, 24), (24, 36), (36, 48)):
            xa, pr = R("bg", x0 + 16 * a, x0 + 16 * b), R("pr", 16 * a, 16 * b)
            move(opt["lg"], xa, xg(a, b))
            tt(pr, xg(48 + a, 48 + b), xa, ALU.mult)
            mms([(R("p_p", 16 * a % 192, 16 * a % 192 + cnt(pr)), R("ee", 0, 128), pr, False, b == 48)])
        move(opt["x2"][0], R("bg", x0 + 768, x0 + 1152), xg(48, 72))
        move(opt["x2"][1], R("bg", x0 + 1152, x0 + 1536), xg(72, 96))
        both = opt["step"][t] == "p"
        for i in range(2 * both):
            mms([(R("p_t%d" % i, 0, 384), FSC, R("bg", x0 + 384 * i, x0 + 384 * i + 384), True, False)])
        act(R("es", 0, 192), pp, AF.Tanh, scale=-1.0 / 64, bias=0.0)
        act(R("p_p", 0, 192), R("es", 0, 192), scale=1.0 / 64)
        act(R("p_p", 192, 384), R("es", 0, 192), scale=1.0 / 64)
        for i, (mine, par) in enumerate(((0, 768), (384, 1152), (768, 0), (1152, 384))):
            out = R("bg", c0 + mine, c0 + mine + 384)
            if both and i < 2:
                tb = R("pr", mine, mine + 384)
                tt(tb, R("bg", x0 + par, x0 + par + 384), R("p_p", 0, 384), ALU.mult)
                mms([(R("p_t%d" % i, 0, 384), FSC, tb, False, True)])
                act(out, R("p_t%d" % i, 0, 384), scale=SC)
            elif opt["step"][t] in "dp":
                tb = R(("p_c%d" if both else "p_t%d") % (i % 2), 0, 384)
                tt(tb, R("bg", x0 + par, x0 + par + 384), R("p_p", 0, 384), ALU.mult)
                tt(out, R("bg", x0 + mine, x0 + mine + 384), tb, ALU.add)
            else:
                tt(out, R("bg", x0 + par, x0 + par + 384), R("p_p", 0, 384), ALU.mult)

    for t in range(RO):
        prepare(t)
    for t in range(RO):
        control(t)
        if t < RO - 1:
            names(t)
            if t > 0:
                lists(t)
        else:
            lists(t)
            names(t)
        data(t)
    tag[0] = "fin"
    a = 0
    for i, n in enumerate(opt["fin"]):
        move("ad"[i % 2], R("bg", KP + 16 * a, KP + 16 * (a + n)), R("bg", O, O + W + RO * K, ind=R("y16", a, a + n)))
        dma(opt["out"][i % 2], T.yr[:, 16 * a:16 * (a + n)], R("bg", KP + 16 * a, KP + 16 * (a + n)), 8 * n)
        a += n
    return ops, sent[0]


def clash(x, y):
    if x[1] != y[1] or x[3] <= y[2] or y[3] <= x[2]:
        return False
    if x[4] > 1 and x[4] == y[4] and (x[2] - y[2]) % x[4]:
        return False
    return not (x[5] and y[5] and x[5][0] == "rows" and y[5][0] == "rows" and x[5][1] != y[5][1])


def depends(ops):
    seen = {}
    deps = []
    for i, o in enumerate(ops):
        d = set()
        mine = [(x, False) for x in o["rd"]] + [(x, True) for x in o["wr"]]
        for x, w in mine:
            for j, y, v in seen.get(x[1], ()):
                if (x[1] in PSUM and (ops[j]["eng"] != o["eng"] or "other" in o or "other" in ops[j]) and j != i) or ((w or v) and clash(x, y)):
                    d.add(j)
        for x in o["bh"]:
            d.update(j for j, y, v in seen.get(x[1], ()) if v and clash(x, y))
        for x, w in mine:
            seen.setdefault(x[1], []).append((i, x, w))
        deps.append(d)
    return deps


def schedule(ops, deps, sc, opt, others=()):
    n = len(ops)
    eng = [o["eng"] for o in ops]
    cost = [o["cost"] for o in ops]
    pre = [[] for i in range(n)]
    succ = [[] for i in range(n)]
    for i in range(n):
        for j in set(deps[i]) | set(ops[i]["after"]):
            lag = 0.0 if eng[i] == eng[j] and (eng[i] == "pe" or j not in deps[i]) else ops[j]["lat"] + sc["gap"]
            pre[i].append((j, cost[j] + lag))
            succ[j].append((i, cost[i] + lag))

    either = ["other" in o for o in ops]

    def gap(line, s, c):
        k = len(line)
        while k and line[k - 1][1] > s:
            k -= 1
        while k < len(line) and line[k][0] < s + c - 1e-9:
            s = line[k][1]
            k += 1
        return s, k

    def place(rank, links, first, choose=False):
        start = [0.0] * n
        busy = {e: [] for e in eng}
        for i in sorted(range(n), key=rank):
            s = first[i]
            for j, d in links[i]:
                if start[j] + d > s:
                    s = start[j] + d
            if choose and either[i]:
                eng[i] = "dve" if gap(busy["dve"], s, cost[i])[0] + opt["lean"] < gap(busy["act"], s, cost[i])[0] else "act"
            if eng[i] != "net":
                s, k = gap(busy[eng[i]], s, cost[i])
                busy[eng[i]].insert(k, (s, s + cost[i]))
            start[i] = s
        return start
    zero = [0.0] * n
    lat = [o["lat"] for o in ops]

    def passes(weight):
        back = [0.0] * n
        for i in range(n - 1, -1, -1):
            back[i] = max([back[j] + d for j, d in succ[i]] + [lat[i]]) + weight[ops[i]["tag"]] * cost[i]
        start = place(lambda i: (-back[i] - cost[i], i), pre, zero, True)
        back = place(lambda i: (-start[i] - cost[i], -i), succ, lat)
        start = place(lambda i: (-back[i] - cost[i], i), pre, zero, True)
        order = sorted(range(n), key=lambda i: (start[i], i))
        return sum(replay(order, x) for x in others) + max(start[i] + cost[i] + lat[i] for i in range(n)), order, start, list(eng)

    def replay(order, x):
        end, free = [0.0] * n, {e: 0.0 for e in eng}
        for i in order:
            s = free[eng[i]]
            for j, d in pre[i]:
                v = end[j] + (x[j][1] if d > cost[j] else 0.0)
                if v > s:
                    s = v
            end[i] = s + x[i][0]
            if eng[i] != "net":
                free[eng[i]] = end[i]
        return max(end[i] + x[i][1] for i in range(n))
    tags = sorted(set(o["tag"] for o in ops))
    weight = {t: opt["weight"].get(t, opt["weight"].get(t[:-1], 0.0)) for t in tags}
    best = passes(weight)
    seed = opt["seed"]
    for k in range(opt["tries"]):
        trial = dict(weight)
        for m in range(3):
            seed = (seed * 1103515245 + 12345) % 2 ** 31
            t = tags[(seed >> 8) % len(tags)]
            trial[t] = max(0.0, trial[t] + ((seed >> 16) % 256 - 127.5) / 100)
        got = passes(trial)
        if got[0] <= best[0]:
            weight, best = trial, got
    ORDER["weight"] = (best[0], weight)
    figures = [[(cost[i], lat[i] + sc["gap"]) for i in range(n)]] + list(others)
    order, best = best[1], (1e9, best[1], best[3])
    eng[:] = best[2]
    for k in range(opt["turns"]):
        got = polish(order, eng, pre, cost, either, figures, opt["swaps"], opt["heat"])
        best = min(best, got)
        eng[:] = best[2]
        end = walk(best[1], eng, [[(j, d > cost[j]) for j, d in p] for p in pre], figures[k % len(figures)])[1]
        back = place(lambda i: (-end[i], -i), succ, lat)
        start = place(lambda i: (-back[i] - cost[i], i), pre, zero)
        order = sorted(range(n), key=lambda i: (start[i], i))
    order, eng = best[1:]
    end = walk(order, eng, [[(j, d > cost[j]) for j, d in p] for p in pre], figures[0])[1]
    return order, {i: (end[i] - cost[i], end[i] + lat[i]) for i in range(n)}, eng


def walk(order, eng, pre, x, a=0, old=None):
    end, by = (list(old[1]), list(old[2])) if a else ([0.0] * len(order), [-1] * len(order))
    last = {eng[i]: i for i in order[:a] if eng[i] != "net"}
    for i in order[a:]:
        k = last.get(eng[i], -1)
        s = end[k] if k >= 0 else 0.0
        for j, far in pre[i]:
            v = end[j] + x[j][1] if far else end[j]
            if v >= s:
                s, k = v, -2 - j
        end[i], by[i] = s + x[i][0], k
        if eng[i] != "net":
            last[eng[i]] = i
    i = max(order[-40:], key=lambda i: end[i] + x[i][1])
    return end[i] + x[i][1], end, by, i


def polish(order, eng, pre, cost, either, figures, swaps, heat):
    n = len(order)
    above = [0] * n
    for i in range(n):
        for j, d in pre[i]:
            above[i] |= above[j] | 1 << j
    pre = [[(j, d > cost[j]) for j, d in p if not any(above[k] >> j & 1 and (d <= cost[j] or cost[k] > 3) for k, c in p)] for p in pre]
    eng = list(eng)
    sends = [i for i in range(n) if eng[i] == "pool"]

    def worth(ws):
        return sum(w[0] + heat[1] * sum(w[1][i] for i in sends) for w in ws)
    now = [walk(order, eng, pre, x) for x in figures]
    best = (worth(now), order, list(eng))
    here = best[0]
    seed = 7
    for turn in range(swaps):
        seed = (seed * 1103515245 + 12345) % 2 ** 31
        by, i = now[turn % len(now)][2:]
        if turn & 4:
            i = sends[(seed >> 4) % len(sends)]
        links = []
        while by[i] != -1:
            if by[i] >= 0 and not above[i] >> by[i] & 1:
                links.append((by[i], i))
            i = by[i] if by[i] >= 0 else -2 - by[i]
        if not links:
            continue
        j, i = links[(seed >> 8) % len(links)]
        flip = [k for k in (i, j) if either[k]]
        new = order
        if flip and seed >> 20 & 3 == 0:
            flip = flip[(seed >> 22) % len(flip)]
            eng[flip] = "act" if eng[flip] == "dve" else "dve"
            a = order.index(flip)
        else:
            flip = -1
            a, b = order.index(j), order.index(i) + 1
            up = above[i] | 1 << i
            new = order[:a] + [k for k in order[a:b] if up >> k & 1] + [k for k in order[a:b] if not up >> k & 1] + order[b:]
        got = [walk(new, eng, pre, x, a, w) for x, w in zip(figures, now)]
        total = worth(got)
        if total <= here + heat[0] * (seed >> 12 & 15) / 15 * (1 - turn / swaps):
            end = got[0][1]
            order, now, here = sorted(new, key=lambda k: end[k] - cost[k]), got, total
            if total < best[0]:
                best = (total, order, list(eng))
        elif flip >= 0:
            eng[flip] = "act" if eng[flip] == "dve" else "dve"
    return best


ORDER = {}


def rank_program(g, core, T, topo):
    r = T.rank_of(core)
    if r is None:
        cores = list(T.cores)
        for q in range(N):
            if core == helper(q, cores, topo):
                near, far, en, ef = peers(q, cores, topo)
                far = far[3:]
                es = topo.engines(core, cores[far[0]])
                x = T.eb[:, W + M * q:W + M * q + M]
                g.wait_ge(T.sem.hc, len(en) // 2)
                g.remote_dma_fused([RemoteDMATransfer(dst_ids=[DstId(rid=topo.addr(cores[d])[0], pnc=topo.addr(cores[d])[1]) for d in far],
                                                      dma_engine_mask=msk(es), remote_sem=T.sem.ha, srcs=[x], dsts=[x] * len(far))],
                                   local_sem=T.sem.sent)
                g.wait_ge(T.sem.sent, len(es))
        return
    ops, sent = plan(r, T, topo, PLAN, OPT)
    deps = depends(ops)
    if "order" not in ORDER:
        ref = plan(0, T, topo, PLAN, OPT)[0]
        others = [[(o["cost"], o["lat"] + x["gap"]) for o in plan(0, T, topo, x, OPT)[0]] for x in [dict(PLAN, **y) for y in OTHER]]
        ORDER["order"], ORDER["times"], ORDER["queues"] = schedule(ref, depends(ref), PLAN, OPT, others)
    order, times = ORDER["order"], ORDER["times"]
    for o, e in zip(ops, ORDER["queues"]):
        if e != o["eng"]:
            o["eng"], o["call"] = e, o["other"]
    queue = {"dve": g.vector, "act": g.scalar, "pe": g.tensor, "pool": g, "sp": g.sync}
    count = {}
    mark = {}
    clock = {}
    known = {e: {} for e in queue}
    top = {}
    for i in order:
        o = ops[i]
        e = o["eng"]
        if e == "link":
            continue
        if e == "net":
            mark[i] = o["sem"]
            clock[i] = {o["sem"][0]: o["sem"][1]}
            top[o["sem"][0]] = max(top.get(o["sem"][0], 0), o["sem"][1])
            continue
        kn = known[e]
        need = {}
        for j in deps[i]:
            if e == "pe" and ops[j]["eng"] == "pe":
                continue
            s, v = mark[j]
            if kn.get(s, 0) < v and need.get(s, (0, 0))[0] < v:
                need[s] = (v, j)
        for s, (v, j) in sorted(need.items(), key=lambda x: -times[x[1][1]][1]):
            if kn.get(s, 0) < v:
                queue[e].wait_ge(T.sem[s], v)
                for s2, v2 in clock[j].items():
                    kn[s2] = max(kn.get(s2, 0), v2)
        ins = o["call"](g)
        if ins is None:
            continue
        if o["sem"] is None:
            count[e] = count.get(e, 0) + 1
            mark[i] = (e, count[e])
            ins.then_inc(T.sem[e], 1)
        else:
            mark[i] = o["sem"]
            ins.then_inc(T.sem[o["sem"][0]], 16)
        c = dict(kn)
        c[mark[i][0]] = mark[i][1]
        clock[i] = c
        top[mark[i][0]] = max(top.get(mark[i][0], 0), mark[i][1])
    top["sent"] = sent
    for s in sorted(top):
        g.wait_ge(T.sem[s], top[s])
